import numpy as np, ml_dtypes
CORES = [113,118,241,246]
N = 4
BF = ml_dtypes.bfloat16
def gentries(a):
    return np.ascontiguousarray(a.reshape(8, 16, -1).transpose(0, 2, 1)).reshape(8, -1)
def gtable(e):
    e = np.asarray(e); return np.ascontiguousarray(e.reshape(8, -1, 16).transpose(0, 2, 1)).reshape(128, -1).astype(np.int32)
T, P, R, CAP = 512, 2048, 4, 320
def put(o):
    return np.stack([gtable(o[r].reshape(8, -1).astype(np.int32)) for r in range(N)])
def get(came):
    return np.stack([gentries(came[r]).reshape(8, R, N - 1, T) for r in range(N)])
def start(rng):
    o = np.stack([rng.permutation(8) for r in range(N)])
    s = np.array([16, 16, 16, 12, 12, 8, 4, 2])[o]; c = np.array([1, 1, 2, 2, 0, 2, 1, 0])[o]
    had = np.array([P // 2, 3 * P // 4, P])[c] + rng.integers(0, np.array([P // 8, P // 4, P + 1])[c])
    n = (rng.integers(0, CAP + 1, (N, 8, R, N - 1)) * s[:, :, None, None]) >> 4
    for r in range(N):
        n[r, rng.integers(0, 8), rng.integers(0, R), rng.integers(0, N - 1)] = 0
        n[r, np.argmax(s[r]), rng.integers(0, R), rng.integers(0, N - 1)] = CAP
    return had[:, :, None].astype(np.int32), n
def consts(rng):
    h = np.zeros((N, 8, 6 * R + 3), np.int32)
    for e in range(R):
        h[:, :, 6 * e:6 * e + 3] = 2 * rng.integers(0, 2048, (N, 8, 3)) + 1
        h[:, :, 6 * e + 3:6 * e + 6] = rng.integers(0, 4096, (N, 8, 3))
    h[:, :, 6 * R:] = 2 * rng.integers(0, 128, (N, 8, 3)) + 1
    return h
def arrivals(rng, n):
    o = np.argsort(np.argsort(rng.random((N, 8, R, N - 1, T)), -1), -1)
    return put(o < n[..., None])
def setup_inputs(rng):
    had, n = start(rng)
    return {"ring": rng.integers(0, 256, (N, 128, P)).astype(np.float32).astype(BF), "had": had, "hc": consts(rng), "came": arrivals(rng, n)}
def setup_inputs_full(rng):
    d = setup_inputs(rng); d["came"] = arrivals(rng, np.full((N, 8, R, N - 1), CAP))
    v = np.array([P // 2, P - 1, P, 2 * P, P + 1, 2 * P - 1, P // 2 + 1, 3 * P // 2])
    d["had"] = np.stack([rng.permutation(v) for r in range(N)])[:, :, None].astype(np.int32); return d
def setup_inputs_lost(rng):
    d = setup_inputs(rng); o = get(d["came"]) > 0; z = rng.integers(0, N)
    for r in range(N):
        w = rng.permutation(8)
        o[r, w[0]] = False
        o[r, w[1]] = False; o[r, w[1], :, :, 0] = True
        o[r, w[2]] = False; o[r, w[2], :, :, T - 1] = True
        o[r, w[3], rng.integers(0, R)] = False
        o[r, w[4], :, :N - 2] = False
    o[z] = False
    d["came"] = put(o); return d
def setup_inputs_ends(rng):
    d = setup_inputs(rng); o = get(d["came"]); hc = d["hc"]
    n0 = np.sum(o[:, :, 0], axis=(2, 3)); v = np.array([P, P - 1, P + 1, 2 * P, 2 * P - 1, P, 2 * P, P + 1])
    d["had"] = (np.stack([rng.permutation(v) for r in range(N)]) - n0)[:, :, None].astype(np.int32)
    a = np.arange(4096); top = int(np.flatnonzero(((2 * ((a * a) & 2047) + a) & 4095) == 4095)[0])
    for q in range(N):
        for e in range(R):
            for g in range(8):
                dd = int(rng.integers(1, N)); r = (q - dd) % N; w = np.flatnonzero(o[r, g, e, dd - 1])
                x = r * T + (int(rng.choice(w)) if w.size else 0)
                for k, u in ((0, 0), (1, top)): hc[q, g, 6 * e + 3 + k] = (u - int(hc[q, g, 6 * e + k]) * x) & 4095
                if g & 1:
                    hc[q, g, 6 * e + 2] = hc[q, g, 6 * e]; hc[q, g, 6 * e + 5] = hc[q, g, 6 * e + 3]
    return d
def setup_inputs_bursts(rng):
    d = setup_inputs(rng); had, n = start(rng); d["had"] = had
    a = rng.integers(0, T - n + 1); b = np.where(rng.random(n.shape) < 0.5, 0, T - n)
    a[:, ::2] = b[:, ::2]; t = np.arange(T)
    d["came"] = put((t >= a[..., None]) & (t < (a + n)[..., None])); return d
def setup_inputs_spread(rng):
    d = setup_inputs(rng)
    d["ring"] = (rng.integers(0, 256, (N, 128, P)) >> rng.integers(0, 9, (N, 1, P))).astype(np.float32).astype(BF)
    d["had"] = rng.integers(P // 2, 2 * P + 1, (N, 8, 1)).astype(np.int32)
    hc = d["hc"]; m = rng.random(hc.shape) < 0.25; lo = np.zeros(6 * R + 3, np.int64); hi = np.full(6 * R + 3, 4095)
    for e in range(R): lo[6 * e:6 * e + 3] = 1
    lo[6 * R:] = 1; hi[6 * R:] = 255
    d["hc"] = np.where(m, np.where(rng.random(hc.shape) < 0.5, lo, hi), hc).astype(np.int32)
    n = np.floor(rng.random((N, 8, R, N - 1)) ** 3 * (CAP + 1)).astype(np.int64)
    d["came"] = arrivals(rng, np.minimum(n, CAP)); return d
def check_inputs(d):
    bad = []; v = d["ring"].astype(np.float32); hc = d["hc"]
    if not ((v >= 0) & (v <= 255) & (v == np.floor(v))).all(): bad.append("ring")
    if not ((d["had"] >= P // 2) & (d["had"] <= 2 * P)).all(): bad.append("had")
    for e in range(R):
        a = hc[:, :, 6 * e:6 * e + 3]; b = hc[:, :, 6 * e + 3:6 * e + 6]
        if not ((a >= 1) & (a <= 4095) & (a & 1 == 1)).all() or not ((b >= 0) & (b <= 4095)).all(): bad.append("hash")
    f = hc[:, :, 6 * R:]
    if not ((f >= 1) & (f <= 255) & (f & 1 == 1)).all(): bad.append("factors")
    if not ((d["came"] == 0) | (d["came"] == 1)).all(): bad.append("flags")
    elif np.max(np.sum(get(d["came"]), axis=-1)) > CAP: bad.append("cap")
    return bad
def reference(ring, had, hc, came):
    y = ring.astype(np.float32).astype(np.int64).reshape(N, 8, 16, P); m = had[:, :, 0].astype(np.int64); h = hc.astype(np.int64)
    fl = get(came) == 1; x = np.arange(N * T)
    for e in range(R):
        pk = np.zeros((N, 8, 16, N * T), np.int64)
        for q in range(N):
            for g in range(8):
                c = min(int(m[q, g]), P)
                for k in range(3):
                    u = (h[q, g, 6 * e + k] * x + h[q, g, 6 * e + 3 + k]) & 4095
                    s = (u * u) & 2047
                    p = (((2 * s + u) & 4095) * c) >> 12
                    pk[q, g] += h[q, g, 6 * R + k] * y[q, g][:, p]
        pk = pk & 255
        for r in range(N):
            for g in range(8):
                for d in range(1, N):
                    keep = pk[(r + d) % N, g][:, r * T:r * T + T][:, fl[r, g, e, d - 1]]; n = keep.shape[1]
                    y[r, g][:, (m[r, g] + np.arange(n)) & (P - 1)] = keep
                    m[r, g] += n
    return {"y": y.reshape(N, 128, P).astype(np.float32), "now": m.reshape(N, 8, 1).astype(np.float32)}

@@ -1,0 +1,432 @@
+from concourse.bass import DstId, RemoteDMATransfer
+from concourse.mybir import AluOpType as A, ActivationFunctionType as AF
+
+NR, P, CAP, TT = 4, 2048, 320, 512
+CW = CAP // 16
+EPS = 2.0 ** -13
+BIG = 1024.0
+
+
+def _sb(n, t):
+    return ("sbuf", [128] + (n if isinstance(n, list) else [n]), t)
+
+
+SCRATCH = {
+    "WIN": _sb(P + 12 * CAP, "bfloat16"), "OUT": _sb(12 * CAP, "bfloat16"), "GG": _sb(9 * CAP, "bfloat16"),
+    "KI": _sb(3 * CAP, "int32"), "YY": _sb(P, "float32"),
+    "CMA": _sb([3, 32], "int32"), "CMB": _sb([9, 32], "int32"), "FA": _sb([3, 33], "bfloat16"), "FB": _sb([9, 33], "bfloat16"),
+    "HCI": _sb(28, "int32"), "HCF": _sb(28, "float32"), "HC": _sb(28, "float32"),
+    "PCI": _sb(4, "int32"), "PCF": _sb(8, "float32"),
+    "MG": _sb(128, "bfloat16"), "MI": _sb(144, "float32"), "BON": _sb(128, "bfloat16"), "UT": _sb(128, "bfloat16"),
+    "UU": _sb(128, "bfloat16"), "WM": _sb(144, "float16"), "E8": _sb(128, "float32"), "IDB": _sb(128, "bfloat16"),
+    "IDH": _sb(128, "float16"), "DG": _sb(3 * 128, "bfloat16"),
+    "CBM": _sb(297, "float32"), "CBR": _sb(297, "bfloat16"), "K2": _sb(24, "float32"), "KA": _sb(96, "float32"),
+    "KB": _sb(288, "float32"), "PLC": _sb(128, "float32"),
+    "JK": _sb(24 * 32, "bfloat16"), "ACC": _sb(24, "float32"), "AC2": _sb(24, "float32"),
+    "OFA": _sb(6, "uint16"), "OFB": _sb(18, "uint16"),
+    "XA": _sb(96, "float32"), "XB": _sb(288, "float32"), "LA": _sb([3, CW], "float32"), "LB": _sb([3, 96], "float32"),
+    "CNT": _sb(12, "float32"), "EP": _sb(14, "float32"), "NEP": _sb(14, "float32"), "DL": _sb(13, "float32"),
+    "MM": _sb(4, "float32"), "NC": _sb(12, "float32"), "MUI": _sb(8, "int32"), "MU": _sb(4, "float32"), "HI": _sb(2, "int32"),
+    "TH": _sb(4 * 16, "float32"),
+    "Z1": _sb(180, "int32"), "Z2": _sb(180, "int32"), "Z3": _sb(180, "int32"), "Z4": _sb(180, "int32"),
+    "Z5": _sb(180, "int32"), "Z6": _sb(180, "int32"), "NA": _sb(180, "float16"), "TM": _sb(13 * 180, "float16"),
+    "OFF": _sb(5 * 180, "uint16"),
+    "PCS": ("psum", [128, 512], "float32"), "PU": ("psum", [128, 512], "float32"), "PD": ("psum", [128, 512], "float32"),
+    "PX0": ("psum", [128, 512], "float32"), "PX1": ("psum", [128, 512], "float32"), "PX2": ("psum", [128, 512], "float32"),
+    "PM": ("psum", [128, 512], "float32"), "PH": ("psum", [128, 512], "float32"),
+}
+for _n, _w in (("A", 99), ("B", 297)):
+    SCRATCH["CI" + _n] = _sb(_w, "float32")
+    SCRATCH["RM" + _n] = _sb(_w, "int32")
+    SCRATCH["RB" + _n] = _sb(_w, "int32")
+    SCRATCH["RH" + _n] = _sb(_w, "float16")
+    SCRATCH["OH" + _n] = _sb(16 * (_w + 1), "float16")
+    SCRATCH["CJ" + _n] = _sb(_w, "int32")
+    SCRATCH["CK" + _n] = _sb(_w, "int32")
+    SCRATCH["HB" + _n] = _sb(_w, "float32")
+    SCRATCH["VL" + _n] = _sb(_w, "float32")
+    SCRATCH["MX" + _n] = _sb(_w, "float32")
+
+SEMAPHORES = ["sV", "sS", "sP", "sG", "ldA", "ldB", "ldH", "ldR", "st", "loc", "arA", "arB", "ar0", "ar1", "ar2", "ar3"]
+PSUM = ("PCS", "PU", "PD", "PX0", "PX1", "PX2", "PM", "PH")
+
+
+def _bits(engs):
+    m = 0
+    for e in engs:
+        m |= 1 << e
+    return m
+
+
+def _peers(T, topo, q):
+    me = T.cores[q]
+    n = len(T.cores)
+    others = [(q + d) % n for d in range(1, n)]
+    far = [r for r in others if T.cores[r] not in topo.cores_of(me)]
+    far.sort(key=lambda r: topo.die(T.cores[r]) == topo.die(me))
+    near = [r for r in others if T.cores[r] in topo.cores_of(me)]
+    res = []
+    used = set()
+    k = 1
+    for i, r in enumerate(far):
+        en = topo.engines(me, T.cores[r])
+        used |= set(en)
+        k = len(en) // len(far)
+        res.append((r, en, en[i * k:(i + 1) * k], en[i * k:(i + 1) * k]))
+    for r in near:
+        en = [x for x in topo.engines(me, T.cores[r]) if x not in used]
+        res.append((r, en, en[:k], en))
+    return res
+
+
+def rank_program(g, core, T, topo):
+    rank = T.rank_of(core)
+    if rank is None:
+        return
+    n = len(T.cores)
+    Q = {"V": g.vector, "S": g.scalar, "P": g.tensor, "G": g, "Y": g.sync}
+    cnt = {"V": 0, "S": 0, "P": 0, "G": 0}
+    waited = {q: {} for q in Q}
+    wr, rd, pend = {}, {}, []
+
+    def wait(q, tok):
+        if waited[q].get(tok[0], 0) < tok[1]:
+            Q[q].wait_ge(T.sem[tok[0]], tok[1])
+            waited[q][tok[0]] = tok[1]
+
+    def deps(q, r, w):
+        need = {}
+        for k in r:
+            toks = [wr[k]] if k in wr else []
+            if k in PSUM:
+                toks += [t for t in rd.get(k, []) if t[0] != "s" + q]
+            for t in toks:
+                need[t[0]] = max(need.get(t[0], 0), t[1])
+        for k in w:
+            for t in ([wr[k]] if k in wr else []) + rd.get(k, []):
+                if not (q == "P" and t[0] == "sP"):
+                    need[t[0]] = max(need.get(t[0], 0), t[1])
+        for s in need:
+            wait(q, (s, need[s]))
+
+    def done(tok, r, w):
+        for k in r:
+            rd.setdefault(k, []).append(tok)
+        for k in w:
+            wr[k] = tok
+            rd[k] = []
+
+    def op(q, f, r, w, last=True):
+        deps(q, r, w)
+        ins = f()
+        if not last:
+            pend.extend(r)
+            return
+        cnt[q] += 1
+        ins.then_inc(T.sem["s" + q], 1)
+        if q == "P":
+            r = list(r) + pend
+            del pend[:]
+        done(("s" + q, cnt[q]), r, w)
+
+    v, s, pe = g.vector, g.scalar, g.tensor
+
+    def ts(out, i, a, b, o0, o1, r, w):
+        if o1 is None:
+            op("V", lambda: v.tensor_scalar(out, i, a, None, o0), r, w)
+        else:
+            op("V", lambda: v.tensor_scalar(out, i, a, b, o0, o1), r, w)
+
+    def tt(out, a, b, o, r, w):
+        op("V", lambda: v.tensor_tensor(out, a, b, o), r, w)
+
+    def cp(out, i, r, w):
+        op("V", lambda: v.tensor_copy(out, i), r, w)
+
+    def act(out, i, r, w, func=AF.Identity, **kw):
+        op("S", lambda: s.activation(out, i, func, **kw), r, w)
+
+    def mm(out, l, rh, st, sp, r, w):
+        op("P", lambda: pe.matmul(out, l, rh, st, sp), r, w, last=sp)
+
+    def iota(out, pat, base, cm, w, flt=True):
+        if flt:
+            op("G", lambda: g.iota(out, pat, base, cm, allow_small_or_imprecise_dtypes=True), [], w)
+        else:
+            op("G", lambda: g.iota(out, pat, base, cm), [], w)
+
+    peers = _peers(T, topo, rank)
+    got = [0, 0, 0]
+    slot = {}
+    for q in range(n):
+        if q != rank:
+            for j, pr in enumerate(_peers(T, topo, q)):
+                if pr[0] == rank:
+                    got = [a + len(b) for a, b in zip(got, pr[1:])]
+                    slot[q] = j
+    wr["LA"], wr["LB"] = ("arA", got[1]), ("arB", got[2])
+    for e in range(NR):
+        wr["W%d" % e] = ("ar%d" % e, got[0])
+    sent = [0]
+
+    g.sync.dma_start(T.CMA[:], T.came[:, 0:96]).then_inc(T.sem.ldA, 16)
+    s.dma_start(T.HCI[0:8, 0:27], T.hc[:]).then_inc(T.sem.ldH, 16)
+    s.dma_start(T.HCI[0:8, 27:28], T.had[:]).then_inc(T.sem.ldH, 16)
+    g.sync.dma_start(T.CMB[:], T.came[:, 96:384]).then_inc(T.sem.ldB, 16)
+    g.sync.dma_start(T.WIN[:, 0:P], T.ring[:]).then_inc(T.sem.ldR, 16)
+    wr["CMA"], wr["CMB"], wr["HCI"], wr["RING"] = ("ldA", 16), ("ldB", 16), ("ldH", 32), ("ldR", 16)
+
+    iota(T.PCI[:, 0:1], [[0, 1]], 0, 1, ["p"], flt=False)
+    iota(T.MG[:], [[16, 8], [0, 16]], 0, 0, ["MG"])
+    iota(T.CBM[:, 0:99], [[0, 3], [512, 33]], 0, 0, ["CBMA"])
+    op("V", lambda: v.memset(T.FA[:, :, 32:33], 0.0), [], ["FA"])
+    op("V", lambda: v.memset(T.FB[:, :, 32:33], 0.0), [], ["FB"])
+    op("V", lambda: v.memset(T.PD[:, 0:129:128], -BIG), [], ["PD"])
+    pf, gf, bf = T.PCF[:, 0:1], T.PCF[:, 1:2], T.PCF[:, 2:3]
+    ts(T.PCI[:, 1:2], T.PCI[:, 0:1], 112, None, A.bitwise_and, None, ["p"], ["gi"])
+    ts(T.PCI[:, 2:3], T.PCI[:, 0:1], 15, None, A.bitwise_and, None, ["p"], ["bi"])
+    cp(T.PCF[:, 0:3], T.PCI[:, 0:3], ["p", "gi", "bi"], ["pf"])
+    ts(T.BON[:], T.MG[:], gf, None, A.is_equal, None, ["MG", "pf"], ["BON"])
+    op("G", lambda: g.affine_select(T.UT[:], T.BON[:], [[-1, 128]], A.is_gt, 0.0, 0, 1), ["BON"], ["UT"])
+    op("G", lambda: g.affine_select(T.UU[:], T.UT[:], [[-1, 128]], A.not_equal, -512.0, 0, 1), ["UT"], ["UU"])
+    iota(T.MI[:], [[1, 144]], 0, 0, ["MI"])
+    iota(T.CBR[:, 0:99], [[32, 3], [1, 33]], -64, 0, ["CBRA"])
+    iota(T.K2[:, 0:6], [[66, 3], [0, 2]], 32, 0, ["K2A"])
+    iota(T.KA[:], [[-TT, 3], [0, 32]], TT * rank, 0, ["KA"])
+    op("V", lambda: v.memset(T.EP[:, 1:2], 0.0), [], ["EP1"])
+    op("V", lambda: v.memset(T.DL[:, 0:1], float(P)), [], ["DL0"])
+    ts(T.PCF[:, 3:4], gf, 15.0, None, A.add, None, ["pf"], ["g15"])
+    ts(T.PCF[:, 4:5], bf, BIG, None, A.add, None, ["pf"], ["bB"])
+    ts(T.PCF[:, 5:6], bf, 16.0, 15.5, A.mult, A.add, ["pf"], ["th0"])
+    ts(T.PCF[:, 6:7], bf, 16.0, 271.5, A.mult, A.add, ["pf"], ["th1"])
+    ts(T.E8[0:8, :], T.MG[0:8, :], 1.0 / 16, T.PCF[0:8, 0:1], A.mult, A.is_equal, ["MG", "pf"], ["E8"])
+
+    def lists(b, ns, c0):
+        w = 33 * ns
+        F, CM = T["F" + b], T["CM" + b]
+        CI, RM, RB, RH, OH, CJ, CK, HB, VL, MX = [T[x + b] for x in ("CI", "RM", "RB", "RH", "OH", "CJ", "CK", "HB", "VL", "MX")]
+        a0 = 0 if b == "A" else 6
+        OF, X, K = T["OF" + b], T["X" + b], T["K" + b]
+
+        def flags():
+            cp(F[:, :, 0:32], CM[:], ["CM" + b], ["F" + b])
+            mm(T.PCS[:, c0:c0 + w], T.BON[:], F[:], True, True, ["BON", "F" + b], ["PCS"])
+            mm(T.PU[:, c0:c0 + w], T.UU[:], F[:], True, True, ["UU", "F" + b], ["PU"])
+
+        def ranks():
+            op("V", lambda: v.tensor_tensor_scan(CI[:], T.CBM[:, 0:w], T.PCS[:, c0:c0 + w], 0.0, A.min, A.add),
+               ["CBMA", "CBM" + b, "PCS"], ["CI" + b])
+            tt(RM[:], CI[:], T.PU[:, c0:c0 + w], A.subtract, ["CI" + b, "PU"], ["RM" + b])
+            ts(RB[:], RM[:], 527, None, A.bitwise_and, None, ["RM" + b], ["RB" + b])
+            cp(RH[:], RB[:], ["RB" + b], ["RH" + b])
+            mm(T.PD[:, c0 + 1:c0 + 1 + w], T.BON[:], T.CBR[:, 0:w], True, False, ["BON", "CBRA", "CBR" + b], ["PD"])
+
+        def ends():
+            for i in range(2 * ns):
+                h = i % 2
+                sl = i // 2 if b == "A" else 3 * ((i // 2) % 3) + i // 6
+                act(T.JK[:, 32 * (a0 + i):32 * (a0 + i + 1)], CI[:, 33 * sl:33 * sl + 32], ["CI" + b, "th%d" % h],
+                    ["ACC%d" % (a0 + i)], func=AF.Sign, scale=-1.0, bias=T.PCF[:, 5 + h:6 + h],
+                    accum_out=T.ACC[:, a0 + i:a0 + i + 1])
+
+        def hot(lo, hi):
+            for k in range(lo, hi):
+                o = OH[:, k * (w + 1):k * (w + 1) + w]
+                ts(o, RH[:], float(512 + ((k + 1) & 15)), None, A.is_equal, None, ["RH" + b], ["OH%s%d" % (b, k)])
+                mm(T.PD[:, c0 + 1:c0 + 1 + w], T.WM[:, 15 - k:143 - k], o, False, k == 15, ["WM", "OH%s%d" % (b, k)], ["PD"])
+
+        def finish():
+            cp(CJ[:], CI[:], ["CI" + b], ["CJ" + b])
+            tt(T.AC2[:, a0:a0 + 2 * ns], T.ACC[:, a0:a0 + 2 * ns], T.K2[:, a0:a0 + 2 * ns], A.add,
+               ["ACC%d" % (a0 + i) for i in range(2 * ns)] + ["K2" + b], ["AC2" + b])
+            ts(CK[:], CJ[:], 15, None, A.bitwise_and, None, ["CJ" + b], ["CK" + b])
+            ts(OF[:], T.AC2[:, a0:a0 + 2 * ns], 0.5, None, A.mult, None, ["AC2" + b], ["OF" + b])
+            ts(HB[:], CK[:], bf, BIG, A.is_gt, A.mult, ["CK" + b, "pf"], ["HB" + b])
+            tt(VL[:], T.PD[:, c0 + 1:c0 + 1 + w], HB[:], A.subtract, ["PD", "HB" + b], ["VL" + b])
+            op("V", lambda: v.tensor_tensor_scan(MX[:], T.PD[:, c0:c0 + w], VL[:], -BIG, A.max, A.max),
+               ["PD", "VL" + b], ["MX" + b])
+            tt(X[:], MX[:].indirect(OF[:]), K[:], A.add, ["MX" + b, "OF" + b, "K" + b], ["X" + b])
+
+        def send():
+            deps("G", ["X" + b], [])
+            trs = []
+            for pr in peers:
+                q = pr[0]
+                el = pr[2] if b == "A" else pr[3]
+                d = (q - rank) % n
+                rid, pid = topo.addr(T.cores[q], core)
+                if b == "A":
+                    src, dst = X[:, 32 * (d - 1):32 * (d - 1) + CW], T.LA[:, slot[q], :]
+                else:
+                    src, dst = X[:, 96 * (d - 1):96 * (d - 1) + 64 + CW], T.LB[:, slot[q], 0:64 + CW]
+                trs.append(RemoteDMATransfer(dst_ids=[DstId(rid=rid, pnc=pid)], dma_engine_mask=_bits(el),
+                                             remote_sem=T.sem["ar" + b], src=src, dst=dst))
+                sent[0] += len(el)
+            g.remote_dma_fused(trs, local_sem=T.sem.loc)
+
+        return flags, ranks, ends, hot, finish, send
+
+    def hash_(e):
+        x = T.LA[:] if e == 0 else T.LB[:, :, 32 * (e - 1):32 * (e - 1) + CW]
+        for k in range(3):
+            ts(T.Z1[:, 60 * k:60 * k + 60], x, T.HC[:, 6 * e + k:6 * e + k + 1], T.HC[:, 6 * e + 3 + k:6 * e + 4 + k],
+               A.mult, A.add, ["LA" if e == 0 else "LB", "HC"], ["Z1%d" % k])
+        ts(T.Z2[:], T.Z1[:], 4095, None, A.bitwise_and, None, ["Z10", "Z11", "Z12"], ["Z2"])
+        ts(T.PH[:, 64:244], T.Z2[:], 2.0, -4095.0, A.mult, A.add, ["Z2"], ["PH"])
+        tt(T.Z3[:], T.Z2[:], T.PH[:, 64:244], A.mult, ["Z2", "PH"], ["Z3"])
+        ts(T.Z4[:], T.Z3[:], 4095, None, A.bitwise_and, None, ["Z3"], ["Z4"])
+
+    def place(e):
+        off = T.OFF[:, 180 * e:180 * e + 180]
+        if e == 0:
+            ts(off, T.Z4[:], T.NC[:, 4:5], EPS - 0.5, A.mult, A.add, ["Z4", "C0"], ["OFF0"])
+            return
+        w = 180 if e < NR else 128
+        if e < NR:
+            ts(T.Z5[:], T.Z4[:], T.NC[:, e - 1:e], T.MU[:, e - 1:e], A.mult, A.add, ["Z4", "NC", "MU"], ["Z5"])
+        else:
+            ts(T.Z5[:, 0:w], T.PLC[:], -1.0, T.MU[:, e - 1:e], A.mult, A.add, ["PLC", "MU"], ["Z5"])
+        ts(T.Z6[:, 0:w], T.Z5[:, 0:w], P - 1, None, A.bitwise_and, None, ["Z5"], ["Z6"])
+        ts(T.NA[:, 0:w], T.Z6[:, 0:w], -1.0, None, A.mult, None, ["Z6"], ["NA"])
+        mm(T.PM[:, 0:w], T.IDH[:], T.NA[:, 0:w], True, False, ["IDH", "NA"], ["PM"])
+        for i in range(3 * e + 1):
+            o = T.TM[:, 180 * i:180 * i + w]
+            c = 16 * (e - 1) + i
+            ts(o, T.NA[:, 0:w], T.TH[:, c:c + 1], T.DL[:, i:i + 1], A.is_le, A.mult,
+               ["NA", "TH%d" % e, "DL0", "DL1", "DL2"], ["TM%d" % i])
+            mm(T.PM[:, 0:w], T.IDH[:], o, False, i == 3 * e, ["IDH", "TM%d" % i], ["PM"])
+        ts(off[:, 0:w], T.PM[:, 0:w], T.CNT[:, 3 * e - 1:3 * e], float(P - 1 + CAP * (3 * e - 1)), A.add, A.add,
+           ["PM", "CNTA", "CNTB"], ["OFF%d" % e])
+
+    def gather(q, e, j, k, lo=0, hi=CW):
+        c = 180 * e + 60 * k + CW * j
+        win = T.WIN[:, 0:P + 3 * CAP * e].indirect(T.OFF[:, c + lo:c + hi])
+        o = T.GG[:, CAP * (3 * j + k) + 16 * lo:CAP * (3 * j + k) + 16 * hi]
+        r = ["RING", "OFF%d" % e] + ["W%d" % i for i in range(e)]
+        w = ["G%d%d%s" % (j, k, h) for h in ("a" if lo == 0 else "") + ("b" if hi == CW else "")]
+        if q == "V":
+            cp(o, win, r, w)
+        else:
+            act(o, win, r, w, func=AF.Copy)
+
+    def weigh(j, order):
+        for i, k in enumerate(order):
+            mm(T["PX%d" % j][:, 0:CAP], T.DG[:, 128 * k:128 * k + 128], T.GG[:, CAP * (3 * j + k):CAP * (3 * j + k + 1)],
+               i == 0, i == 2, ["DG%d" % k, "G%d%da" % (j, k), "G%d%db" % (j, k)], ["PX%d" % j])
+
+    def reduce_send(e, j):
+        px, ki = T["PX%d" % j][:, 0:CAP], T.KI[:, CAP * j:CAP * (j + 1)]
+        o = T.OUT[:, CAP * (3 * e + j):CAP * (3 * e + j + 1)]
+        ts(ki, px, -127.5 / 256, None, A.add, None, ["PX%d" % j], ["KI%d" % j])
+        tt(o, px, ki, A.subtract, ["PX%d" % j, "KI%d" % j], ["O%d%d" % (e, j)])
+        r, en = peers[j][0:2]
+        rid, pid = topo.addr(T.cores[r], core)
+        c = P + CAP * (3 * e + (rank - r) % n - 1)
+        deps("G", ["O%d%d" % (e, j)], [])
+        g.remote_dma(T.WIN[:, c:c + CAP], o, T.sem["ar%d" % e], T.sem.loc, pid, rid, _bits(en))
+        sent[0] += len(en)
+
+    fA, rA, eA, hA, zA, sA = lists("A", 3, 0)
+    fB, rB, eB, hB, zB, sB = lists("B", 9, 128)
+    had = T.HC[:, 27:28]
+
+    fA()
+    ts(T.WM[:], T.MI[:], T.PCF[:, 3:4], T.PCF[:, 4:5], A.is_equal, A.mult, ["MI", "g15", "bB"], ["WM"])
+    rA()
+    eA()
+    hA(0, 16)
+    cp(T.HCF[0:8, :], T.HCI[0:8, :], ["HCI"], ["HCF"])
+    mm(T.PH[:, 0:28], T.E8[0:8, :], T.HCF[0:8, :], True, True, ["E8", "HCF"], ["PH"])
+    act(T.HC[:], T.PH[:, 0:28], ["PH"], ["HC"])
+    iota(T.CBM[:, 99:297], [[0, 6], [512, 33]], 0, 0, ["CBMB"])
+    iota(T.CBR[:, 99:297], [[32, 6], [1, 33]], 32, 0, ["CBRB"])
+    iota(T.K2[:, 6:24], [[66, 3], [198, 3], [0, 2]], 32, 0, ["K2B"])
+    zA()
+    sA()
+    iota(T.KB[:], [[-TT, 3], [-3 * TT, 3], [0, 32]], TT * rank, 0, ["KB"])
+    iota(T.PLC[:, 0:128], [[16, 128]], 0, 0, ["PL0"])
+    act(T.WIN[:, 0:P], T.WIN[:, 0:P], ["RING"], ["RING"], scale=1.0 / 256)
+
+    fB()
+    ts(T.IDB[:], T.MI[:, 0:128], pf, None, A.is_equal, None, ["MI", "pf"], ["IDB"])
+    ts(T.NC[:, 4:5], had, float(P), 1.0 / 4096, A.min, A.mult, ["HC"], ["C0"])
+    for k in range(3):
+        act(T.DG[:, 128 * k:128 * k + 128], T.IDB[:], ["IDB", "HC"], ["DG%d" % k], scale=T.HC[:, 24 + k:25 + k])
+    rB()
+    eB()
+    act(T.CNT[:, 0:3], T.CIA[:, 32:99:33], ["CIA"], ["CNTA"])
+    act(T.CNT[:, 3:12], T.CIB[:, 32:297:33], ["CIB"], ["CNTB"])
+    hB(0, 12)
+    hash_(0)
+    place(0)
+    for j in range(3):
+        for k in range(3 if j < 2 else 2):
+            gather("S", 0, j, k)
+    hB(12, 16)
+    zB()
+    sB()
+    weigh(0, (0, 1, 2))
+    reduce_send(0, 0)
+    gather("V", 0, 2, 2)
+    weigh(1, (0, 1, 2))
+    reduce_send(0, 1)
+    op("V", lambda: v.tensor_tensor_scan(T.EP[:, 2:14], T.CNT[:], T.CNT[:], 0.0, A.add, A.max), ["CNTA", "CNTB"], ["EP2"])
+    cp(T.HI[:, 0:1], had, ["HC"], ["HI0"])
+    weigh(2, (2, 0, 1))
+    reduce_send(0, 2)
+
+    act(T.MM[:], T.EP[:, 4:14:3], ["EP2", "HC"], ["MM"], bias=had)
+    act(T.NEP[:, 1:14], T.EP[:, 1:14], ["EP1", "EP2"], ["NEP"], scale=-1.0)
+    act(T.NC[:, 8:12], T.MM[:], ["MM"], ["NR"], func=AF.Relu, scale=-1.0, bias=float(P))
+    act(T.DL[:, 2:13], T.CNT[:, 0:11], ["CNTA", "CNTB"], ["DL2"], bias=-float(CAP))
+    act(T.NC[:, 0:4], T.NC[:, 8:12], ["NR"], ["NC"], scale=1.0 / 4096, bias=-0.5)
+    ts(T.HI[:, 1:2], T.HI[:, 0:1], P - 1, None, A.bitwise_and, None, ["HI0"], ["HI1"])
+    ts(T.MUI[:, 0:4], T.MM[:], -1.0, None, A.add, None, ["MM"], ["MU0"])
+    ts(T.EP[:, 0:1], T.HI[:, 1:2], -1.0, None, A.mult, None, ["HI1"], ["EP0"])
+    ts(T.MUI[:, 4:8], T.MUI[:, 0:4], P - 1, None, A.bitwise_and, None, ["MU0"], ["MU1"])
+    ts(T.IDH[:], T.MI[:, 0:128], pf, None, A.is_equal, None, ["MI", "pf"], ["IDH"])
+    ts(T.MU[:], T.MUI[:, 4:8], 0.5 - EPS, None, A.add, None, ["MU1"], ["MU"])
+    act(T.DL[:, 1:2], T.EP[:, 0:1], ["EP0"], ["DL1"], scale=-1.0, bias=-float(P))
+    for e in range(1, NR + 1):
+        act(T.TH[:, 16 * (e - 1):16 * (e - 1) + 13], T.EP[:, 0:13], ["EP0", "EP1", "EP2", "NEP"], ["TH%d" % e],
+            bias=T.NEP[:, 1 + 3 * e:2 + 3 * e])
+    act(T.PLC[:], T.PLC[:], ["PL0", "pf"], ["PLC"], bias=bf)
+    deps("Y", ["MM"], [])
+    g.sync.dma_start(T.now[:], T.MM[0:128:16, 3:4]).then_inc(T.sem.st, 16)
+
+    for e in range(1, NR):
+        hash_(e)
+        place(e)
+        for j in range(3):
+            gather("V", e, j, 2)
+        gather("S", e, 0, 0)
+        gather("S", e, 0, 1)
+        weigh(0, (2, 0, 1))
+        gather("S", e, 1, 0)
+        gather("S", e, 1, 1)
+        reduce_send(e, 0)
+        weigh(1, (2, 0, 1))
+        gather("S", e, 2, 0)
+        gather("S", e, 2, 1, 0, CW // 2)
+        gather("V", e, 2, 1, CW // 2, CW)
+        reduce_send(e, 1)
+        weigh(2, (2, 0, 1))
+        reduce_send(e, 2)
+
+    place(NR)
+    r = ["RING", "OFF4"] + ["W%d" % i for i in range(NR)]
+    pieces = (("V", 0, 256), ("S", 256, 512), ("V", 512, 896), ("S", 896, 1280), ("V", 1280, 1664), ("S", 1664, 2048))
+    for q, lo, hi in pieces:
+        win = T.WIN[:].indirect(T.OFF[:, 720 + lo // 16:720 + hi // 16])
+        if q == "V":
+            ts(T.YY[:, lo:hi], win, 256.0, None, A.mult, None, r, ["Y%d" % lo])
+        else:
+            act(T.YY[:, lo:hi], win, r, ["Y%d" % lo], scale=256.0)
+        dq = "S" if hi == P else "Y"
+        deps(dq, ["Y%d" % lo], [])
+        Q[dq].dma_start(T.y[:, lo:hi], T.YY[:, lo:hi]).then_inc(T.sem.st, 16)
+
+    g.sync.wait_ge(T.sem.st, 16 * (1 + len(pieces)))
+    g.wait_ge(T.sem.loc, sent[0])
+    for q in cnt:
+        wait("G", ("s" + q, cnt[q]))

@@ -5,6 +5,7 @@ NR, P, CAP, TT = 4, 2048, 320, 512
 CW = CAP // 16
 EPS = 2.0 ** -13
 BIG = 1024.0
+BATCH = {"A": (0, 3, 0), "B": (3, 9, 128)}
 
 
 def _sb(n, t):
@@ -14,7 +15,7 @@ def _sb(n, t):
 SCRATCH = {
     "WIN": _sb(P + 12 * CAP, "bfloat16"), "OUT": _sb(12 * CAP, "bfloat16"), "GG": _sb(9 * CAP, "bfloat16"),
     "KI": _sb(3 * CAP, "int32"), "YY": _sb(P, "float32"),
-    "CMA": _sb([3, 32], "int32"), "CMB": _sb([9, 32], "int32"), "FA": _sb([3, 33], "bfloat16"), "FB": _sb([9, 33], "bfloat16"),
+    "CMA": _sb([3, 32], "int32"), "CMB": _sb([9, 32], "int32"),
     "HCI": _sb(28, "int32"), "HCF": _sb(28, "float32"), "HC": _sb(28, "float32"),
     "PCI": _sb(4, "int32"), "PCF": _sb(8, "float32"),
     "MG": _sb(128, "bfloat16"), "MI": _sb(144, "float32"), "BON": _sb(128, "bfloat16"), "UT": _sb(128, "bfloat16"),
@@ -23,19 +24,20 @@ SCRATCH = {
     "CBM": _sb(297, "float32"), "CBR": _sb(297, "bfloat16"), "K2": _sb(24, "float32"), "KA": _sb(96, "float32"),
     "KB": _sb(288, "float32"), "PLC": _sb(128, "float32"),
     "JK": _sb(24 * 32, "bfloat16"), "ACC": _sb(24, "float32"), "AC2": _sb(24, "float32"),
-    "OFA": _sb(6, "uint16"), "OFB": _sb(18, "uint16"),
-    "XA": _sb(96, "float32"), "XB": _sb(288, "float32"), "LA": _sb([3, CW], "float32"), "LB": _sb([3, 96], "float32"),
+    "LA": _sb([3, CW], "float32"), "LB": _sb([3, 96], "float32"),
+    "FZ": _sb([12, 33], "bfloat16"),
     "CNT": _sb(12, "float32"), "EP": _sb(14, "float32"), "NEP": _sb(14, "float32"), "DL": _sb(13, "float32"),
     "MM": _sb(4, "float32"), "NC": _sb(12, "float32"), "MUI": _sb(8, "int32"), "MU": _sb(4, "float32"), "HI": _sb(2, "int32"),
     "TH": _sb(4 * 16, "float32"),
-    "Z1": _sb(180, "int32"), "Z2": _sb(180, "int32"), "Z3": _sb(180, "int32"), "Z4": _sb(180, "int32"),
+    "Z1": _sb(180, "int32"), "Z2": _sb(180, "int32"), "Z3": _sb(180, "int32"), "Z4": _sb(4 * 180, "int32"),
     "Z5": _sb(180, "int32"), "Z6": _sb(180, "int32"), "NA": _sb(180, "float16"), "TM": _sb(13 * 180, "float16"),
     "OFF": _sb(5 * 180, "uint16"),
     "PCS": ("psum", [128, 512], "float32"), "PU": ("psum", [128, 512], "float32"), "PD": ("psum", [128, 512], "float32"),
     "PX0": ("psum", [128, 512], "float32"), "PX1": ("psum", [128, 512], "float32"), "PX2": ("psum", [128, 512], "float32"),
     "PM": ("psum", [128, 512], "float32"), "PH": ("psum", [128, 512], "float32"),
 }
-for _n, _w in (("A", 99), ("B", 297)):
+for _n in BATCH:
+    _w = 33 * BATCH[_n][1]
     SCRATCH["CI" + _n] = _sb(_w, "float32")
     SCRATCH["RM" + _n] = _sb(_w, "int32")
     SCRATCH["RB" + _n] = _sb(_w, "int32")
@@ -46,6 +48,8 @@ for _n, _w in (("A", 99), ("B", 297)):
     SCRATCH["HB" + _n] = _sb(_w, "float32")
     SCRATCH["VL" + _n] = _sb(_w, "float32")
     SCRATCH["MX" + _n] = _sb(_w, "float32")
+    SCRATCH["OF" + _n] = _sb(2 * BATCH[_n][1], "uint16")
+    SCRATCH["X" + _n] = _sb(32 * BATCH[_n][1], "float32")
 
 SEMAPHORES = ["sV", "sS", "sP", "sG", "ldA", "ldB", "ldH", "ldR", "st", "loc", "arA", "arB", "ar0", "ar1", "ar2", "ar3"]
 PSUM = ("PCS", "PU", "PD", "PX0", "PX1", "PX2", "PM", "PH")
@@ -77,6 +81,13 @@ def _peers(T, topo, q):
         en = [x for x in topo.engines(me, T.cores[r]) if x not in used]
         res.append((r, en, en[:k], en))
     return res
+
+
+def _mix(*chains):
+    for i in range(max(len(c) for c in chains)):
+        for c in chains:
+            if i < len(c):
+                c[i]()
 
 
 def rank_program(g, core, T, topo):
@@ -179,8 +190,7 @@ def rank_program(g, core, T, topo):
     iota(T.PCI[:, 0:1], [[0, 1]], 0, 1, ["p"], flt=False)
     iota(T.MG[:], [[16, 8], [0, 16]], 0, 0, ["MG"])
     iota(T.CBM[:, 0:99], [[0, 3], [512, 33]], 0, 0, ["CBMA"])
-    op("V", lambda: v.memset(T.FA[:, :, 32:33], 0.0), [], ["FA"])
-    op("V", lambda: v.memset(T.FB[:, :, 32:33], 0.0), [], ["FB"])
+    op("V", lambda: v.memset(T.FZ[:, :, 32:33], 0.0), [], ["FA", "FB"])
     op("V", lambda: v.memset(T.PD[:, 0:129:128], -BIG), [], ["PD"])
     pf, gf, bf = T.PCF[:, 0:1], T.PCF[:, 1:2], T.PCF[:, 2:3]
     ts(T.PCI[:, 1:2], T.PCI[:, 0:1], 112, None, A.bitwise_and, None, ["p"], ["gi"])
@@ -201,102 +211,113 @@ def rank_program(g, core, T, topo):
     ts(T.PCF[:, 6:7], bf, 16.0, 271.5, A.mult, A.add, ["pf"], ["th1"])
     ts(T.E8[0:8, :], T.MG[0:8, :], 1.0 / 16, T.PCF[0:8, 0:1], A.mult, A.is_equal, ["MG", "pf"], ["E8"])
 
-    def lists(b, ns, c0):
+    def lists(b):
+        s0, ns, c0 = BATCH[b]
         w = 33 * ns
-        F, CM = T["F" + b], T["CM" + b]
+        F = T.FZ[:, s0:s0 + ns, :]
         CI, RM, RB, RH, OH, CJ, CK, HB, VL, MX = [T[x + b] for x in ("CI", "RM", "RB", "RH", "OH", "CJ", "CK", "HB", "VL", "MX")]
-        a0 = 0 if b == "A" else 6
+        a0 = 2 * s0
         OF, X, K = T["OF" + b], T["X" + b], T["K" + b]
+        ne = ns // 3
 
         def flags():
-            cp(F[:, :, 0:32], CM[:], ["CM" + b], ["F" + b])
-            mm(T.PCS[:, c0:c0 + w], T.BON[:], F[:], True, True, ["BON", "F" + b], ["PCS"])
-            mm(T.PU[:, c0:c0 + w], T.UU[:], F[:], True, True, ["UU", "F" + b], ["PU"])
+            cp(T.FZ[:, s0:s0 + ns, 0:32], T["CM" + b][:], ["CM" + b], ["F" + b])
+            mm(T.PCS[:, c0:c0 + w], T.BON[:], F, True, True, ["BON", "F" + b], ["PCS"])
+            mm(T.PU[:, c0:c0 + w], T.UU[:], F, True, True, ["UU", "F" + b], ["PU"])
 
         def ranks():
             op("V", lambda: v.tensor_tensor_scan(CI[:], T.CBM[:, 0:w], T.PCS[:, c0:c0 + w], 0.0, A.min, A.add),
                ["CBMA", "CBM" + b, "PCS"], ["CI" + b])
             tt(RM[:], CI[:], T.PU[:, c0:c0 + w], A.subtract, ["CI" + b, "PU"], ["RM" + b])
+            cp(CJ[:], CI[:], ["CI" + b], ["CJ" + b])
             ts(RB[:], RM[:], 527, None, A.bitwise_and, None, ["RM" + b], ["RB" + b])
+            ts(CK[:], CJ[:], 15, None, A.bitwise_and, None, ["CJ" + b], ["CK" + b])
             cp(RH[:], RB[:], ["RB" + b], ["RH" + b])
+            ts(HB[:], CK[:], bf, BIG, A.is_gt, A.mult, ["CK" + b, "pf"], ["HB" + b])
             mm(T.PD[:, c0 + 1:c0 + 1 + w], T.BON[:], T.CBR[:, 0:w], True, False, ["BON", "CBRA", "CBR" + b], ["PD"])
 
         def ends():
             for i in range(2 * ns):
                 h = i % 2
-                sl = i // 2 if b == "A" else 3 * ((i // 2) % 3) + i // 6
+                sl = 3 * ((i // 2) % ne) + i // (2 * ne)
                 act(T.JK[:, 32 * (a0 + i):32 * (a0 + i + 1)], CI[:, 33 * sl:33 * sl + 32], ["CI" + b, "th%d" % h],
                     ["ACC%d" % (a0 + i)], func=AF.Sign, scale=-1.0, bias=T.PCF[:, 5 + h:6 + h],
                     accum_out=T.ACC[:, a0 + i:a0 + i + 1])
 
-        def hot(lo, hi):
-            for k in range(lo, hi):
+        def hot():
+            for k in range(16):
                 o = OH[:, k * (w + 1):k * (w + 1) + w]
                 ts(o, RH[:], float(512 + ((k + 1) & 15)), None, A.is_equal, None, ["RH" + b], ["OH%s%d" % (b, k)])
                 mm(T.PD[:, c0 + 1:c0 + 1 + w], T.WM[:, 15 - k:143 - k], o, False, k == 15, ["WM", "OH%s%d" % (b, k)], ["PD"])
-
-        def finish():
-            cp(CJ[:], CI[:], ["CI" + b], ["CJ" + b])
             tt(T.AC2[:, a0:a0 + 2 * ns], T.ACC[:, a0:a0 + 2 * ns], T.K2[:, a0:a0 + 2 * ns], A.add,
                ["ACC%d" % (a0 + i) for i in range(2 * ns)] + ["K2" + b], ["AC2" + b])
-            ts(CK[:], CJ[:], 15, None, A.bitwise_and, None, ["CJ" + b], ["CK" + b])
-            ts(OF[:], T.AC2[:, a0:a0 + 2 * ns], 0.5, None, A.mult, None, ["AC2" + b], ["OF" + b])
-            ts(HB[:], CK[:], bf, BIG, A.is_gt, A.mult, ["CK" + b, "pf"], ["HB" + b])
-            tt(VL[:], T.PD[:, c0 + 1:c0 + 1 + w], HB[:], A.subtract, ["PD", "HB" + b], ["VL" + b])
-            op("V", lambda: v.tensor_tensor_scan(MX[:], T.PD[:, c0:c0 + w], VL[:], -BIG, A.max, A.max),
-               ["PD", "VL" + b], ["MX" + b])
-            tt(X[:], MX[:].indirect(OF[:]), K[:], A.add, ["MX" + b, "OF" + b, "K" + b], ["X" + b])
+
+        finish = [lambda: ts(OF[:], T.AC2[:, a0:a0 + 2 * ns], 0.5, None, A.mult, None, ["AC2" + b], ["OF" + b]),
+                  lambda: tt(VL[:], T.PD[:, c0 + 1:c0 + 1 + w], HB[:], A.subtract, ["PD", "HB" + b], ["VL" + b]),
+                  lambda: op("V", lambda: v.tensor_tensor_scan(MX[:], T.PD[:, c0:c0 + w], VL[:], -BIG, A.max, A.max),
+                             ["PD", "VL" + b], ["MX" + b]),
+                  lambda: tt(X[:], MX[:].indirect(OF[:]), K[:], A.add, ["MX" + b, "OF" + b, "K" + b], ["X" + b])]
 
         def send():
             deps("G", ["X" + b], [])
             trs = []
+            wid = 32 * (ne - 1) + CW
             for pr in peers:
                 q = pr[0]
                 el = pr[2] if b == "A" else pr[3]
-                d = (q - rank) % n
+                c = 32 * ne * ((q - rank) % n - 1)
                 rid, pid = topo.addr(T.cores[q], core)
-                if b == "A":
-                    src, dst = X[:, 32 * (d - 1):32 * (d - 1) + CW], T.LA[:, slot[q], :]
-                else:
-                    src, dst = X[:, 96 * (d - 1):96 * (d - 1) + 64 + CW], T.LB[:, slot[q], 0:64 + CW]
                 trs.append(RemoteDMATransfer(dst_ids=[DstId(rid=rid, pnc=pid)], dma_engine_mask=_bits(el),
-                                             remote_sem=T.sem["ar" + b], src=src, dst=dst))
+                                             remote_sem=T.sem["ar" + b], src=X[:, c:c + wid], dst=T["L" + b][:, slot[q], 0:wid]))
                 sent[0] += len(el)
             g.remote_dma_fused(trs, local_sem=T.sem.loc)
 
         return flags, ranks, ends, hot, finish, send
 
     def hash_(e):
-        x = T.LA[:] if e == 0 else T.LB[:, :, 32 * (e - 1):32 * (e - 1) + CW]
-        for k in range(3):
-            ts(T.Z1[:, 60 * k:60 * k + 60], x, T.HC[:, 6 * e + k:6 * e + k + 1], T.HC[:, 6 * e + 3 + k:6 * e + 4 + k],
-               A.mult, A.add, ["LA" if e == 0 else "LB", "HC"], ["Z1%d" % k])
-        ts(T.Z2[:], T.Z1[:], 4095, None, A.bitwise_and, None, ["Z10", "Z11", "Z12"], ["Z2"])
-        ts(T.PH[:, 64:244], T.Z2[:], 2.0, -4095.0, A.mult, A.add, ["Z2"], ["PH"])
-        tt(T.Z3[:], T.Z2[:], T.PH[:, 64:244], A.mult, ["Z2", "PH"], ["Z3"])
-        ts(T.Z4[:], T.Z3[:], 4095, None, A.bitwise_and, None, ["Z3"], ["Z4"])
+        key = "LB" if e else "LA"
+        x = T.LB[:, :, 32 * (e - 1):32 * (e - 1) + CW] if e else T.LA[:]
+        h = T.Z4[:, 180 * e:180 * e + 180]
+
+        def lin():
+            for k in range(3):
+                ts(T.Z1[:, 60 * k:60 * k + 60], x, T.HC[:, 6 * e + k:6 * e + k + 1], T.HC[:, 6 * e + 3 + k:6 * e + 4 + k],
+                   A.mult, A.add, [key, "HC"], ["Z1%d" % k])
+
+        return [lin,
+                lambda: ts(T.Z2[:], T.Z1[:], 4095, None, A.bitwise_and, None, ["Z10", "Z11", "Z12"], ["Z2"]),
+                lambda: ts(T.PH[:, 64:244], T.Z2[:], 2.0, -4095.0, A.mult, A.add, ["Z2"], ["PH"]),
+                lambda: tt(T.Z3[:], T.Z2[:], T.PH[:, 64:244], A.mult, ["Z2", "PH"], ["Z3"]),
+                lambda: ts(h, T.Z3[:], 4095, None, A.bitwise_and, None, ["Z3"], ["Z4%d" % e])]
 
     def place(e):
         off = T.OFF[:, 180 * e:180 * e + 180]
         if e == 0:
-            ts(off, T.Z4[:], T.NC[:, 4:5], EPS - 0.5, A.mult, A.add, ["Z4", "C0"], ["OFF0"])
-            return
+            return [lambda: ts(off, T.Z4[:, 0:180], T.NC[:, 4:5], EPS - 0.5, A.mult, A.add, ["Z40", "C0"], ["OFF0"])]
         w = 180 if e < NR else 128
-        if e < NR:
-            ts(T.Z5[:], T.Z4[:], T.NC[:, e - 1:e], T.MU[:, e - 1:e], A.mult, A.add, ["Z4", "NC", "MU"], ["Z5"])
-        else:
-            ts(T.Z5[:, 0:w], T.PLC[:], -1.0, T.MU[:, e - 1:e], A.mult, A.add, ["PLC", "MU"], ["Z5"])
-        ts(T.Z6[:, 0:w], T.Z5[:, 0:w], P - 1, None, A.bitwise_and, None, ["Z5"], ["Z6"])
-        ts(T.NA[:, 0:w], T.Z6[:, 0:w], -1.0, None, A.mult, None, ["Z6"], ["NA"])
-        mm(T.PM[:, 0:w], T.IDH[:], T.NA[:, 0:w], True, False, ["IDH", "NA"], ["PM"])
-        for i in range(3 * e + 1):
-            o = T.TM[:, 180 * i:180 * i + w]
-            c = 16 * (e - 1) + i
-            ts(o, T.NA[:, 0:w], T.TH[:, c:c + 1], T.DL[:, i:i + 1], A.is_le, A.mult,
-               ["NA", "TH%d" % e, "DL0", "DL1", "DL2"], ["TM%d" % i])
-            mm(T.PM[:, 0:w], T.IDH[:], o, False, i == 3 * e, ["IDH", "TM%d" % i], ["PM"])
-        ts(off[:, 0:w], T.PM[:, 0:w], T.CNT[:, 3 * e - 1:3 * e], float(P - 1 + CAP * (3 * e - 1)), A.add, A.add,
-           ["PM", "CNTA", "CNTB"], ["OFF%d" % e])
+
+        def age():
+            if e < NR:
+                ts(T.Z5[:], T.Z4[:, 180 * e:180 * e + 180], T.NC[:, e - 1:e], T.MU[:, e - 1:e], A.mult, A.add,
+                   ["Z4%d" % e, "NC", "MU"], ["Z5"])
+            else:
+                ts(T.Z5[:, 0:w], T.PLC[:], -1.0, T.MU[:, e - 1:e], A.mult, A.add, ["PLC", "MU"], ["Z5"])
+
+        def steps():
+            mm(T.PM[:, 0:w], T.IDH[:], T.NA[:, 0:w], True, False, ["IDH", "NA"], ["PM"])
+            for i in range(3 * e + 1):
+                o = T.TM[:, 180 * i:180 * i + w]
+                c = 16 * (e - 1) + i
+                ts(o, T.NA[:, 0:w], T.TH[:, c:c + 1], T.DL[:, i:i + 1], A.is_le, A.mult,
+                   ["NA", "TH%d" % e, "DL0", "DL1", "DL2"], ["TM%d" % i])
+                mm(T.PM[:, 0:w], T.IDH[:], o, False, i == 3 * e, ["IDH", "TM%d" % i], ["PM"])
+
+        return [age,
+                lambda: ts(T.Z6[:, 0:w], T.Z5[:, 0:w], P - 1, None, A.bitwise_and, None, ["Z5"], ["Z6"]),
+                lambda: ts(T.NA[:, 0:w], T.Z6[:, 0:w], -1.0, None, A.mult, None, ["Z6"], ["NA"]),
+                steps,
+                lambda: ts(off[:, 0:w], T.PM[:, 0:w], T.CNT[:, 3 * e - 1:3 * e], float(P - 1 + CAP * (3 * e - 1)),
+                           A.add, A.add, ["PM", "CNTA", "CNTB"], ["OFF%d" % e])]
 
     def gather(q, e, j, k, lo=0, hi=CW):
         c = 180 * e + 60 * k + CW * j
@@ -314,10 +335,11 @@ def rank_program(g, core, T, topo):
             mm(T["PX%d" % j][:, 0:CAP], T.DG[:, 128 * k:128 * k + 128], T.GG[:, CAP * (3 * j + k):CAP * (3 * j + k + 1)],
                i == 0, i == 2, ["DG%d" % k, "G%d%da" % (j, k), "G%d%db" % (j, k)], ["PX%d" % j])
 
-    def reduce_send(e, j):
+    def reduce_send(e, j, between):
         px, ki = T["PX%d" % j][:, 0:CAP], T.KI[:, CAP * j:CAP * (j + 1)]
         o = T.OUT[:, CAP * (3 * e + j):CAP * (3 * e + j + 1)]
         ts(ki, px, -127.5 / 256, None, A.add, None, ["PX%d" % j], ["KI%d" % j])
+        between()
         tt(o, px, ki, A.subtract, ["PX%d" % j, "KI%d" % j], ["O%d%d" % (e, j)])
         r, en = peers[j][0:2]
         rid, pid = topo.addr(T.cores[r], core)
@@ -326,66 +348,82 @@ def rank_program(g, core, T, topo):
         g.remote_dma(T.WIN[:, c:c + CAP], o, T.sem["ar%d" % e], T.sem.loc, pid, rid, _bits(en))
         sent[0] += len(en)
 
-    fA, rA, eA, hA, zA, sA = lists("A", 3, 0)
-    fB, rB, eB, hB, zB, sB = lists("B", 9, 128)
+    def round_(e, fill):
+        h = CW // 2
+        gather("V", e, 0, 2)
+        gather("S", e, 0, 0)
+        gather("V", e, 0, 1, h, CW)
+        gather("S", e, 0, 1, 0, h)
+        weigh(0, (2, 0, 1))
+        gather("V", e, 1, 2, 0, h)
+        gather("S", e, 1, 0)
+        gather("S", e, 1, 1)
+        gather("S", e, 1, 2, h, CW)
+        reduce_send(e, 0, fill[0])
+        weigh(1, (0, 1, 2))
+        gather("V", e, 2, 2)
+        gather("S", e, 2, 0)
+        gather("S", e, 2, 1)
+        fill[1]()
+        reduce_send(e, 1, fill[2])
+        weigh(2, (2, 0, 1))
+        fill[3]()
+        reduce_send(e, 2, fill[4])
+
+    fA, rA, eA, hA, zA, sA = lists("A")
+    fB, rB, eB, hB, zB, sB = lists("B")
     had = T.HC[:, 27:28]
 
     fA()
     ts(T.WM[:], T.MI[:], T.PCF[:, 3:4], T.PCF[:, 4:5], A.is_equal, A.mult, ["MI", "g15", "bB"], ["WM"])
     rA()
     eA()
-    hA(0, 16)
+    hA()
     cp(T.HCF[0:8, :], T.HCI[0:8, :], ["HCI"], ["HCF"])
     mm(T.PH[:, 0:28], T.E8[0:8, :], T.HCF[0:8, :], True, True, ["E8", "HCF"], ["PH"])
     act(T.HC[:], T.PH[:, 0:28], ["PH"], ["HC"])
     iota(T.CBM[:, 99:297], [[0, 6], [512, 33]], 0, 0, ["CBMB"])
     iota(T.CBR[:, 99:297], [[32, 6], [1, 33]], 32, 0, ["CBRB"])
     iota(T.K2[:, 6:24], [[66, 3], [198, 3], [0, 2]], 32, 0, ["K2B"])
-    zA()
+    _mix(zA[0:2] + [fB] + zA[2:4])
     sA()
     iota(T.KB[:], [[-TT, 3], [-3 * TT, 3], [0, 32]], TT * rank, 0, ["KB"])
     iota(T.PLC[:, 0:128], [[16, 128]], 0, 0, ["PL0"])
     act(T.WIN[:, 0:P], T.WIN[:, 0:P], ["RING"], ["RING"], scale=1.0 / 256)
 
-    fB()
     ts(T.IDB[:], T.MI[:, 0:128], pf, None, A.is_equal, None, ["MI", "pf"], ["IDB"])
-    ts(T.NC[:, 4:5], had, float(P), 1.0 / 4096, A.min, A.mult, ["HC"], ["C0"])
-    for k in range(3):
-        act(T.DG[:, 128 * k:128 * k + 128], T.IDB[:], ["IDB", "HC"], ["DG%d" % k], scale=T.HC[:, 24 + k:25 + k])
     rB()
     eB()
+    for k in range(3):
+        act(T.DG[:, 128 * k:128 * k + 128], T.IDB[:], ["IDB", "HC"], ["DG%d" % k], scale=T.HC[:, 24 + k:25 + k])
     act(T.CNT[:, 0:3], T.CIA[:, 32:99:33], ["CIA"], ["CNTA"])
     act(T.CNT[:, 3:12], T.CIB[:, 32:297:33], ["CIB"], ["CNTB"])
-    hB(0, 12)
-    hash_(0)
-    place(0)
-    for j in range(3):
-        for k in range(3 if j < 2 else 2):
-            gather("S", 0, j, k)
-    hB(12, 16)
-    zB()
-    sB()
-    weigh(0, (0, 1, 2))
-    reduce_send(0, 0)
-    gather("V", 0, 2, 2)
-    weigh(1, (0, 1, 2))
-    reduce_send(0, 1)
-    op("V", lambda: v.tensor_tensor_scan(T.EP[:, 2:14], T.CNT[:], T.CNT[:], 0.0, A.add, A.max), ["CNTA", "CNTB"], ["EP2"])
+    hB()
+    ts(T.NC[:, 4:5], had, float(P), 1.0 / 4096, A.min, A.mult, ["HC"], ["C0"])
     cp(T.HI[:, 0:1], had, ["HC"], ["HI0"])
-    weigh(2, (2, 0, 1))
-    reduce_send(0, 2)
+    zB[0]()
+    _mix(zB[1:4] + [sB], hash_(0) + place(0))
 
+    def sums():
+        op("V", lambda: v.tensor_tensor_scan(T.EP[:, 2:14], T.CNT[:], T.CNT[:], 0.0, A.add, A.max), ["CNTA", "CNTB"], ["EP2"])
+        ts(T.HI[:, 1:2], T.HI[:, 0:1], P - 1, None, A.bitwise_and, None, ["HI0"], ["HI1"])
+
+    def firsts():
+        ts(T.MUI[:, 0:4], T.EP[:, 4:14:3], had, -1.0, A.add, A.add, ["EP2", "HC"], ["MU0"])
+        ts(T.EP[:, 0:1], T.HI[:, 1:2], -1.0, None, A.mult, None, ["HI1"], ["EP0"])
+
+    def masks():
+        ts(T.MUI[:, 4:8], T.MUI[:, 0:4], P - 1, None, A.bitwise_and, None, ["MU0"], ["MU1"])
+        ts(T.IDH[:], T.MI[:, 0:128], pf, None, A.is_equal, None, ["MI", "pf"], ["IDH"])
+
+    h1, h2, h3 = hash_(1), hash_(2), hash_(3)
+    round_(0, [sums, firsts, masks,
+               lambda: ts(T.MU[:], T.MUI[:, 4:8], 0.5 - EPS, None, A.add, None, ["MU1"], ["MU"]), h1[0]])
     act(T.MM[:], T.EP[:, 4:14:3], ["EP2", "HC"], ["MM"], bias=had)
     act(T.NEP[:, 1:14], T.EP[:, 1:14], ["EP1", "EP2"], ["NEP"], scale=-1.0)
     act(T.NC[:, 8:12], T.MM[:], ["MM"], ["NR"], func=AF.Relu, scale=-1.0, bias=float(P))
     act(T.DL[:, 2:13], T.CNT[:, 0:11], ["CNTA", "CNTB"], ["DL2"], bias=-float(CAP))
     act(T.NC[:, 0:4], T.NC[:, 8:12], ["NR"], ["NC"], scale=1.0 / 4096, bias=-0.5)
-    ts(T.HI[:, 1:2], T.HI[:, 0:1], P - 1, None, A.bitwise_and, None, ["HI0"], ["HI1"])
-    ts(T.MUI[:, 0:4], T.MM[:], -1.0, None, A.add, None, ["MM"], ["MU0"])
-    ts(T.EP[:, 0:1], T.HI[:, 1:2], -1.0, None, A.mult, None, ["HI1"], ["EP0"])
-    ts(T.MUI[:, 4:8], T.MUI[:, 0:4], P - 1, None, A.bitwise_and, None, ["MU0"], ["MU1"])
-    ts(T.IDH[:], T.MI[:, 0:128], pf, None, A.is_equal, None, ["MI", "pf"], ["IDH"])
-    ts(T.MU[:], T.MUI[:, 4:8], 0.5 - EPS, None, A.add, None, ["MU1"], ["MU"])
     act(T.DL[:, 1:2], T.EP[:, 0:1], ["EP0"], ["DL1"], scale=-1.0, bias=-float(P))
     for e in range(1, NR + 1):
         act(T.TH[:, 16 * (e - 1):16 * (e - 1) + 13], T.EP[:, 0:13], ["EP0", "EP1", "EP2", "NEP"], ["TH%d" % e],
@@ -394,26 +432,15 @@ def rank_program(g, core, T, topo):
     deps("Y", ["MM"], [])
     g.sync.dma_start(T.now[:], T.MM[0:128:16, 3:4]).then_inc(T.sem.st, 16)
 
-    for e in range(1, NR):
-        hash_(e)
-        place(e)
-        for j in range(3):
-            gather("V", e, j, 2)
-        gather("S", e, 0, 0)
-        gather("S", e, 0, 1)
-        weigh(0, (2, 0, 1))
-        gather("S", e, 1, 0)
-        gather("S", e, 1, 1)
-        reduce_send(e, 0)
-        weigh(1, (2, 0, 1))
-        gather("S", e, 2, 0)
-        gather("S", e, 2, 1, 0, CW // 2)
-        gather("V", e, 2, 1, CW // 2, CW)
-        reduce_send(e, 1)
-        weigh(2, (2, 0, 1))
-        reduce_send(e, 2)
+    _mix(h1[1:5] + place(1))
+    round_(1, h2)
+    _mix(place(2))
+    round_(2, h3)
+    _mix(place(3))
+    p4 = place(NR)
+    round_(3, [p4[0], lambda: None, p4[1], lambda: None, p4[2]])
 
-    place(NR)
+    _mix(p4[3:5])
     r = ["RING", "OFF4"] + ["W%d" % i for i in range(NR)]
     pieces = (("V", 0, 256), ("S", 256, 512), ("V", 512, 896), ("S", 896, 1280), ("V", 1280, 1664), ("S", 1664, 2048))
     for q, lo, hi in pieces:

@@ -6,6 +6,7 @@ CW = CAP // 16
 EPS = 2.0 ** -13
 BIG = 1024.0
 BATCH = {"A": (0, 3, 0), "B": (3, 9, 128)}
+F4, B2, I4, H2, U2 = "float32", "bfloat16", "int32", "float16", "uint16"
 
 
 def _sb(n, t):
@@ -13,46 +14,29 @@ def _sb(n, t):
 
 
 SCRATCH = {
-    "WIN": _sb(P + 12 * CAP, "bfloat16"), "OUT": _sb(12 * CAP, "bfloat16"), "GG": _sb(9 * CAP, "bfloat16"),
-    "KI": _sb(3 * CAP, "int32"), "YY": _sb(P, "float32"),
-    "CMA": _sb([3, 32], "int32"), "CMB": _sb([9, 32], "int32"),
-    "HCI": _sb(28, "int32"), "HCF": _sb(28, "float32"), "HC": _sb(28, "float32"),
-    "PCI": _sb(4, "int32"), "PCF": _sb(8, "float32"),
-    "MG": _sb(128, "bfloat16"), "MI": _sb(144, "float32"), "BON": _sb(128, "bfloat16"), "UT": _sb(128, "bfloat16"),
-    "UU": _sb(128, "bfloat16"), "WM": _sb(144, "float16"), "E8": _sb(128, "float32"), "IDB": _sb(128, "bfloat16"),
-    "IDH": _sb(128, "float16"), "DG": _sb(3 * 128, "bfloat16"),
-    "CBM": _sb(297, "float32"), "CBR": _sb(297, "bfloat16"), "K2": _sb(24, "float32"), "KA": _sb(96, "float32"),
-    "KB": _sb(288, "float32"), "PLC": _sb(128, "float32"),
-    "JK": _sb(24 * 32, "bfloat16"), "ACC": _sb(24, "float32"), "AC2": _sb(24, "float32"),
-    "LA": _sb([3, CW], "float32"), "LB": _sb([3, 96], "float32"),
-    "FZ": _sb([12, 33], "bfloat16"),
-    "CNT": _sb(12, "float32"), "EP": _sb(14, "float32"), "NEP": _sb(14, "float32"), "DL": _sb(13, "float32"),
-    "MM": _sb(4, "float32"), "NC": _sb(12, "float32"), "MUI": _sb(8, "int32"), "MU": _sb(4, "float32"), "HI": _sb(2, "int32"),
-    "TH": _sb(4 * 16, "float32"),
-    "Z1": _sb(180, "int32"), "Z2": _sb(180, "int32"), "Z3": _sb(180, "int32"), "Z4": _sb(4 * 180, "int32"),
-    "Z5": _sb(180, "int32"), "Z6": _sb(180, "int32"), "NA": _sb(180, "float16"), "TM": _sb(13 * 180, "float16"),
-    "OFF": _sb(5 * 180, "uint16"),
-    "PCS": ("psum", [128, 512], "float32"), "PU": ("psum", [128, 512], "float32"), "PD": ("psum", [128, 512], "float32"),
-    "PX0": ("psum", [128, 512], "float32"), "PX1": ("psum", [128, 512], "float32"), "PX2": ("psum", [128, 512], "float32"),
-    "PM": ("psum", [128, 512], "float32"), "PH": ("psum", [128, 512], "float32"),
+    "WIN": _sb(P + 12 * CAP, B2), "OUT": _sb(12 * CAP, B2), "GG": _sb(9 * CAP, B2), "KI": _sb(3 * CAP, I4), "YY": _sb(P, F4),
+    "CMA": _sb([3, 32], I4), "CMB": _sb([9, 32], I4), "HCI": _sb(28, I4), "HCF": _sb(28, F4), "HC": _sb(28, F4),
+    "PCI": _sb(4, I4), "PCF": _sb(8, F4), "MG": _sb(128, B2), "MI": _sb(144, F4), "BON": _sb(128, B2), "UT": _sb(128, B2),
+    "UU": _sb(128, B2), "WM": _sb(144, H2), "E8": _sb(128, F4), "IDB": _sb(128, B2), "IDH": _sb(128, H2), "DG": _sb(384, B2),
+    "CBM": _sb(297, F4), "CBR": _sb(297, B2), "K2": _sb(24, F4), "KA": _sb(96, F4), "KB": _sb(288, F4), "PLC": _sb(128, F4),
+    "JK": _sb(768, B2), "ACC": _sb(24, F4), "AC2": _sb(24, F4), "LA": _sb([3, CW], F4), "LB": _sb([3, 96], F4),
+    "FZ": _sb([12, 33], B2), "CNT": _sb(12, F4), "EP": _sb(14, F4), "NEP": _sb(14, F4), "DL": _sb(13, F4),
+    "MM": _sb(4, F4), "NC": _sb(12, F4), "MUI": _sb(8, I4), "MU": _sb(4, F4), "HI": _sb(2, I4), "TH": _sb(64, F4),
+    "Z1": _sb(720, I4), "Z2": _sb(720, I4), "Z3": _sb(720, I4), "Z4": _sb(720, I4),
+    "Z5": _sb(180, I4), "Z6": _sb(180, I4), "NA": _sb(180, H2), "TM": _sb(13 * 180, H2), "OFF": _sb(900, U2),
 }
+PSUM = ("PCS", "PU", "PD", "PX0", "PX1", "PX2", "PM", "PH")
+for _n in PSUM:
+    SCRATCH[_n] = ("psum", [128, 512], F4)
 for _n in BATCH:
     _w = 33 * BATCH[_n][1]
-    SCRATCH["CI" + _n] = _sb(_w, "float32")
-    SCRATCH["RM" + _n] = _sb(_w, "int32")
-    SCRATCH["RB" + _n] = _sb(_w, "int32")
-    SCRATCH["RH" + _n] = _sb(_w, "float16")
-    SCRATCH["OH" + _n] = _sb(16 * (_w + 1), "float16")
-    SCRATCH["CJ" + _n] = _sb(_w, "int32")
-    SCRATCH["CK" + _n] = _sb(_w, "int32")
-    SCRATCH["HB" + _n] = _sb(_w, "float32")
-    SCRATCH["VL" + _n] = _sb(_w, "float32")
-    SCRATCH["MX" + _n] = _sb(_w, "float32")
-    SCRATCH["OF" + _n] = _sb(2 * BATCH[_n][1], "uint16")
-    SCRATCH["X" + _n] = _sb(32 * BATCH[_n][1], "float32")
+    for _k, _t in (("CI", F4), ("RM", I4), ("RB", I4), ("RH", H2), ("CJ", I4), ("CK", I4), ("HB", F4), ("VL", F4), ("MX", F4)):
+        SCRATCH[_k + _n] = _sb(_w, _t)
+    SCRATCH["OH" + _n] = _sb(16 * (_w + 1), H2)
+    SCRATCH["OF" + _n] = _sb(2 * BATCH[_n][1], U2)
+    SCRATCH["X" + _n] = _sb(32 * BATCH[_n][1], F4)
 
 SEMAPHORES = ["sV", "sS", "sP", "sG", "ldA", "ldB", "ldH", "ldR", "st", "loc", "arA", "arB", "ar0", "ar1", "ar2", "ar3"]
-PSUM = ("PCS", "PU", "PD", "PX0", "PX1", "PX2", "PM", "PH")
 
 
 def _bits(engs):
@@ -120,13 +104,6 @@ def rank_program(g, core, T, topo):
         for s in need:
             wait(q, (s, need[s]))
 
-    def done(tok, r, w):
-        for k in r:
-            rd.setdefault(k, []).append(tok)
-        for k in w:
-            wr[k] = tok
-            rd[k] = []
-
     def op(q, f, r, w, last=True):
         deps(q, r, w)
         ins = f()
@@ -138,7 +115,11 @@ def rank_program(g, core, T, topo):
         if q == "P":
             r = list(r) + pend
             del pend[:]
-        done(("s" + q, cnt[q]), r, w)
+        for k in r:
+            rd.setdefault(k, []).append(("s" + q, cnt[q]))
+        for k in w:
+            wr[k] = ("s" + q, cnt[q])
+            rd[k] = []
 
     v, s, pe = g.vector, g.scalar, g.tensor
 
@@ -160,11 +141,8 @@ def rank_program(g, core, T, topo):
     def mm(out, l, rh, st, sp, r, w):
         op("P", lambda: pe.matmul(out, l, rh, st, sp), r, w, last=sp)
 
-    def iota(out, pat, base, cm, w, flt=True):
-        if flt:
-            op("G", lambda: g.iota(out, pat, base, cm, allow_small_or_imprecise_dtypes=True), [], w)
-        else:
-            op("G", lambda: g.iota(out, pat, base, cm), [], w)
+    def iota(out, pat, base, cm, w):
+        op("G", lambda: g.iota(out, pat, base, cm, allow_small_or_imprecise_dtypes=True), [], w)
 
     peers = _peers(T, topo, rank)
     got = [0, 0, 0]
@@ -187,7 +165,7 @@ def rank_program(g, core, T, topo):
     g.sync.dma_start(T.WIN[:, 0:P], T.ring[:]).then_inc(T.sem.ldR, 16)
     wr["CMA"], wr["CMB"], wr["HCI"], wr["RING"] = ("ldA", 16), ("ldB", 16), ("ldH", 32), ("ldR", 16)
 
-    iota(T.PCI[:, 0:1], [[0, 1]], 0, 1, ["p"], flt=False)
+    op("G", lambda: g.iota(T.PCI[:, 0:1], [[0, 1]], 0, 1), [], ["p"])
     iota(T.MG[:], [[16, 8], [0, 16]], 0, 0, ["MG"])
     iota(T.CBM[:, 0:99], [[0, 3], [512, 33]], 0, 0, ["CBMA"])
     op("V", lambda: v.memset(T.FZ[:, :, 32:33], 0.0), [], ["FA", "FB"])
@@ -219,22 +197,25 @@ def rank_program(g, core, T, topo):
         a0 = 2 * s0
         OF, X, K = T["OF" + b], T["X" + b], T["K" + b]
         ne = ns // 3
+        pd = T.PD[:, c0 + 1:c0 + 1 + w]
 
         def flags():
             cp(T.FZ[:, s0:s0 + ns, 0:32], T["CM" + b][:], ["CM" + b], ["F" + b])
             mm(T.PCS[:, c0:c0 + w], T.BON[:], F, True, True, ["BON", "F" + b], ["PCS"])
             mm(T.PU[:, c0:c0 + w], T.UU[:], F, True, True, ["UU", "F" + b], ["PU"])
 
-        def ranks():
+        def sums():
             op("V", lambda: v.tensor_tensor_scan(CI[:], T.CBM[:, 0:w], T.PCS[:, c0:c0 + w], 0.0, A.min, A.add),
                ["CBMA", "CBM" + b, "PCS"], ["CI" + b])
+
+        def ranks():
             tt(RM[:], CI[:], T.PU[:, c0:c0 + w], A.subtract, ["CI" + b, "PU"], ["RM" + b])
             cp(CJ[:], CI[:], ["CI" + b], ["CJ" + b])
             ts(RB[:], RM[:], 527, None, A.bitwise_and, None, ["RM" + b], ["RB" + b])
             ts(CK[:], CJ[:], 15, None, A.bitwise_and, None, ["CJ" + b], ["CK" + b])
             cp(RH[:], RB[:], ["RB" + b], ["RH" + b])
             ts(HB[:], CK[:], bf, BIG, A.is_gt, A.mult, ["CK" + b, "pf"], ["HB" + b])
-            mm(T.PD[:, c0 + 1:c0 + 1 + w], T.BON[:], T.CBR[:, 0:w], True, False, ["BON", "CBRA", "CBR" + b], ["PD"])
+            mm(pd, T.BON[:], T.CBR[:, 0:w], True, False, ["BON", "CBRA", "CBR" + b], ["PD"])
 
         def ends():
             for i in range(2 * ns):
@@ -248,12 +229,12 @@ def rank_program(g, core, T, topo):
             for k in range(16):
                 o = OH[:, k * (w + 1):k * (w + 1) + w]
                 ts(o, RH[:], float(512 + ((k + 1) & 15)), None, A.is_equal, None, ["RH" + b], ["OH%s%d" % (b, k)])
-                mm(T.PD[:, c0 + 1:c0 + 1 + w], T.WM[:, 15 - k:143 - k], o, False, k == 15, ["WM", "OH%s%d" % (b, k)], ["PD"])
+                mm(pd, T.WM[:, 15 - k:143 - k], o, False, k == 15, ["WM", "OH%s%d" % (b, k)], ["PD"])
             tt(T.AC2[:, a0:a0 + 2 * ns], T.ACC[:, a0:a0 + 2 * ns], T.K2[:, a0:a0 + 2 * ns], A.add,
                ["ACC%d" % (a0 + i) for i in range(2 * ns)] + ["K2" + b], ["AC2" + b])
 
         finish = [lambda: ts(OF[:], T.AC2[:, a0:a0 + 2 * ns], 0.5, None, A.mult, None, ["AC2" + b], ["OF" + b]),
-                  lambda: tt(VL[:], T.PD[:, c0 + 1:c0 + 1 + w], HB[:], A.subtract, ["PD", "HB" + b], ["VL" + b]),
+                  lambda: tt(VL[:], pd, HB[:], A.subtract, ["PD", "HB" + b], ["VL" + b]),
                   lambda: op("V", lambda: v.tensor_tensor_scan(MX[:], T.PD[:, c0:c0 + w], VL[:], -BIG, A.max, A.max),
                              ["PD", "VL" + b], ["MX" + b]),
                   lambda: tt(X[:], MX[:].indirect(OF[:]), K[:], A.add, ["MX" + b, "OF" + b, "K" + b], ["X" + b])]
@@ -272,23 +253,26 @@ def rank_program(g, core, T, topo):
                 sent[0] += len(el)
             g.remote_dma_fused(trs, local_sem=T.sem.loc)
 
-        return flags, ranks, ends, hot, finish, send
+        return flags, sums, ranks, ends, hot, finish, send
 
     def hash_(e):
         key = "LB" if e else "LA"
         x = T.LB[:, :, 32 * (e - 1):32 * (e - 1) + CW] if e else T.LA[:]
-        h = T.Z4[:, 180 * e:180 * e + 180]
+        c = 180 * e
+        z1, z2, z3, h = [z[:, c:c + 180] for z in (T.Z1, T.Z2, T.Z3, T.Z4)]
+        bank = "PH" if e % 2 == 0 else "PU"
+        ph = T[bank][:, 64:244]
 
         def lin():
             for k in range(3):
-                ts(T.Z1[:, 60 * k:60 * k + 60], x, T.HC[:, 6 * e + k:6 * e + k + 1], T.HC[:, 6 * e + 3 + k:6 * e + 4 + k],
-                   A.mult, A.add, [key, "HC"], ["Z1%d" % k])
+                ts(T.Z1[:, c + 60 * k:c + 60 * k + 60], x, T.HC[:, 6 * e + k:6 * e + k + 1],
+                   T.HC[:, 6 * e + 3 + k:6 * e + 4 + k], A.mult, A.add, [key, "HC"], ["Z1%d%d" % (e, k)])
 
         return [lin,
-                lambda: ts(T.Z2[:], T.Z1[:], 4095, None, A.bitwise_and, None, ["Z10", "Z11", "Z12"], ["Z2"]),
-                lambda: ts(T.PH[:, 64:244], T.Z2[:], 2.0, -4095.0, A.mult, A.add, ["Z2"], ["PH"]),
-                lambda: tt(T.Z3[:], T.Z2[:], T.PH[:, 64:244], A.mult, ["Z2", "PH"], ["Z3"]),
-                lambda: ts(h, T.Z3[:], 4095, None, A.bitwise_and, None, ["Z3"], ["Z4%d" % e])]
+                lambda: ts(z2, z1, 4095, None, A.bitwise_and, None, ["Z1%d%d" % (e, k) for k in range(3)], ["Z2%d" % e]),
+                lambda: ts(ph, z2, 2.0, -4095.0, A.mult, A.add, ["Z2%d" % e], [bank]),
+                lambda: tt(z3, z2, ph, A.mult, ["Z2%d" % e, bank], ["Z3%d" % e]),
+                lambda: ts(h, z3, 4095, None, A.bitwise_and, None, ["Z3%d" % e], ["Z4%d" % e])]
 
     def place(e):
         off = T.OFF[:, 180 * e:180 * e + 180]
@@ -370,12 +354,17 @@ def rank_program(g, core, T, topo):
         fill[3]()
         reduce_send(e, 2, fill[4])
 
-    fA, rA, eA, hA, zA, sA = lists("A")
-    fB, rB, eB, hB, zB, sB = lists("B")
+    def idle():
+        return None
+
+    fA, cA, rA, eA, hA, zA, sA = lists("A")
+    fB, cB, rB, eB, hB, zB, sB = lists("B")
     had = T.HC[:, 27:28]
 
     fA()
     ts(T.WM[:], T.MI[:], T.PCF[:, 3:4], T.PCF[:, 4:5], A.is_equal, A.mult, ["MI", "g15", "bB"], ["WM"])
+    cA()
+    ts(T.IDB[:], T.MI[:, 0:128], pf, None, A.is_equal, None, ["MI", "pf"], ["IDB"])
     rA()
     eA()
     hA()
@@ -385,13 +374,28 @@ def rank_program(g, core, T, topo):
     iota(T.CBM[:, 99:297], [[0, 6], [512, 33]], 0, 0, ["CBMB"])
     iota(T.CBR[:, 99:297], [[32, 6], [1, 33]], 32, 0, ["CBRB"])
     iota(T.K2[:, 6:24], [[66, 3], [198, 3], [0, 2]], 32, 0, ["K2B"])
-    _mix(zA[0:2] + [fB] + zA[2:4])
+    _mix(zA[0:2] + [fB, zA[2], lambda: cp(T.HI[:, 0:1], had, ["HC"], ["HI0"]), zA[3]])
     sA()
     iota(T.KB[:], [[-TT, 3], [-3 * TT, 3], [0, 32]], TT * rank, 0, ["KB"])
     iota(T.PLC[:, 0:128], [[16, 128]], 0, 0, ["PL0"])
     act(T.WIN[:, 0:P], T.WIN[:, 0:P], ["RING"], ["RING"], scale=1.0 / 256)
 
-    ts(T.IDB[:], T.MI[:, 0:128], pf, None, A.is_equal, None, ["MI", "pf"], ["IDB"])
+    def sums():
+        op("V", lambda: v.tensor_tensor_scan(T.EP[:, 2:14], T.CNT[:], T.CNT[:], 0.0, A.add, A.max), ["CNTA", "CNTB"], ["EP2"])
+
+    def firsts():
+        ts(T.MUI[:, 0:4], T.EP[:, 4:14:3], had, -1.0, A.add, A.add, ["EP2", "HC"], ["MU0"])
+
+    def tail():
+        sB()
+        ts(T.HI[:, 1:2], T.HI[:, 0:1], P - 1, None, A.bitwise_and, None, ["HI0"], ["HI1"])
+
+    def masks():
+        ts(T.EP[:, 0:1], T.HI[:, 1:2], -1.0, None, A.mult, None, ["HI1"], ["EP0"])
+        ts(T.MUI[:, 4:8], T.MUI[:, 0:4], P - 1, None, A.bitwise_and, None, ["MU0"], ["MU1"])
+
+    cB()
+    ts(T.NC[:, 4:5], had, float(P), 1.0 / 4096, A.min, A.mult, ["HC"], ["C0"])
     rB()
     eB()
     for k in range(3):
@@ -399,26 +403,14 @@ def rank_program(g, core, T, topo):
     act(T.CNT[:, 0:3], T.CIA[:, 32:99:33], ["CIA"], ["CNTA"])
     act(T.CNT[:, 3:12], T.CIB[:, 32:297:33], ["CIB"], ["CNTB"])
     hB()
-    ts(T.NC[:, 4:5], had, float(P), 1.0 / 4096, A.min, A.mult, ["HC"], ["C0"])
-    cp(T.HI[:, 0:1], had, ["HC"], ["HI0"])
     zB[0]()
-    _mix(zB[1:4] + [sB], hash_(0) + place(0))
-
-    def sums():
-        op("V", lambda: v.tensor_tensor_scan(T.EP[:, 2:14], T.CNT[:], T.CNT[:], 0.0, A.add, A.max), ["CNTA", "CNTB"], ["EP2"])
-        ts(T.HI[:, 1:2], T.HI[:, 0:1], P - 1, None, A.bitwise_and, None, ["HI0"], ["HI1"])
-
-    def firsts():
-        ts(T.MUI[:, 0:4], T.EP[:, 4:14:3], had, -1.0, A.add, A.add, ["EP2", "HC"], ["MU0"])
-        ts(T.EP[:, 0:1], T.HI[:, 1:2], -1.0, None, A.mult, None, ["HI1"], ["EP0"])
-
-    def masks():
-        ts(T.MUI[:, 4:8], T.MUI[:, 0:4], P - 1, None, A.bitwise_and, None, ["MU0"], ["MU1"])
-        ts(T.IDH[:], T.MI[:, 0:128], pf, None, A.is_equal, None, ["MI", "pf"], ["IDH"])
+    _mix(zB[1:4] + [tail, sums, firsts], hash_(0) + place(0))
 
     h1, h2, h3 = hash_(1), hash_(2), hash_(3)
-    round_(0, [sums, firsts, masks,
-               lambda: ts(T.MU[:], T.MUI[:, 4:8], 0.5 - EPS, None, A.add, None, ["MU1"], ["MU"]), h1[0]])
+    p1, p2, p3, p4 = place(1), place(2), place(3), place(NR)
+    round_(0, [masks, idle,
+               lambda: ts(T.MU[:], T.MUI[:, 4:8], 0.5 - EPS, None, A.add, None, ["MU1"], ["MU"]), idle,
+               lambda: ts(T.IDH[:], T.MI[:, 0:128], pf, None, A.is_equal, None, ["MI", "pf"], ["IDH"])])
     act(T.MM[:], T.EP[:, 4:14:3], ["EP2", "HC"], ["MM"], bias=had)
     act(T.NEP[:, 1:14], T.EP[:, 1:14], ["EP1", "EP2"], ["NEP"], scale=-1.0)
     act(T.NC[:, 8:12], T.MM[:], ["MM"], ["NR"], func=AF.Relu, scale=-1.0, bias=float(P))
@@ -432,13 +424,12 @@ def rank_program(g, core, T, topo):
     deps("Y", ["MM"], [])
     g.sync.dma_start(T.now[:], T.MM[0:128:16, 3:4]).then_inc(T.sem.st, 16)
 
-    _mix(h1[1:5] + place(1))
-    round_(1, h2)
-    _mix(place(2))
-    round_(2, h3)
-    _mix(place(3))
-    p4 = place(NR)
-    round_(3, [p4[0], lambda: None, p4[1], lambda: None, p4[2]])
+    _mix(h1 + p1, [idle, h2[0], h2[1], h2[2], idle, h2[3], h2[4]])
+    round_(1, [p2[0], h3[0], p2[1], h3[1], p2[2]])
+    _mix([p2[3], h3[2], p2[4]])
+    round_(2, [h3[3], h3[4], p3[0], p3[1], p3[2]])
+    _mix([p3[3], p4[0], p3[4]])
+    round_(3, [p4[1], idle, p4[2], idle, idle])
 
     _mix(p4[3:5])
     r = ["RING", "OFF4"] + ["W%d" % i for i in range(NR)]

@@ -16,27 +16,32 @@ def _sb(n, t):
 SCRATCH = {
     "WIN": _sb(P + 12 * CAP, B2), "OUT": _sb(12 * CAP, B2), "GG": _sb(9 * CAP, B2), "KI": _sb(3 * CAP, I4), "YY": _sb(P, F4),
     "CMA": _sb([3, 32], I4), "CMB": _sb([9, 32], I4), "HCI": _sb(28, I4), "HCF": _sb(28, F4), "HC": _sb(28, F4),
-    "PCI": _sb(4, I4), "PCF": _sb(8, F4), "MG": _sb(128, B2), "MI": _sb(144, F4), "BON": _sb(128, B2), "UT": _sb(128, B2),
+    "PCI": _sb(4, I4), "PCF": _sb(12, F4), "MG": _sb(128, B2), "MI": _sb(144, F4), "BON": _sb(128, B2), "UT": _sb(128, B2),
     "UU": _sb(128, B2), "WM": _sb(144, H2), "E8": _sb(128, F4), "IDB": _sb(128, B2), "IDH": _sb(128, H2), "DG": _sb(384, B2),
+    "EH": _sb(128, H2), "EB": _sb(128, B2),
     "CBM": _sb(297, F4), "CBR": _sb(297, B2), "K2": _sb(24, F4), "KA": _sb(96, F4), "KB": _sb(288, F4), "PLC": _sb(128, F4),
     "JK": _sb(768, B2), "ACC": _sb(24, F4), "AC2": _sb(24, F4), "LA": _sb([3, CW], F4), "LB": _sb([3, 96], F4),
-    "FZ": _sb([12, 33], B2), "CNT": _sb(12, F4), "EP": _sb(14, F4), "NEP": _sb(14, F4), "DL": _sb(13, F4),
-    "MM": _sb(4, F4), "NC": _sb(12, F4), "MUI": _sb(8, I4), "MU": _sb(4, F4), "HI": _sb(2, I4), "TH": _sb(64, F4),
+    "FZ": _sb([12, 33], B2), "CI": _sb(396, F4), "NE": _sb(14, F4), "DL": _sb(13, F4), "FC": _sb(4, F4), "FB": _sb(4, F4),
+    "MM": _sb(6, F4), "NC": _sb(9, F4), "MUI": _sb(8, I4), "MU": _sb(4, F4), "TH": _sb(64, F4),
     "Z1": _sb(720, I4), "Z2": _sb(720, I4), "Z3": _sb(720, I4), "Z4": _sb(720, I4),
-    "Z5": _sb(180, I4), "Z6": _sb(180, I4), "NA": _sb(180, H2), "TM": _sb(13 * 180, H2), "OFF": _sb(900, U2),
+    "Z5": _sb(720, I4), "Z6": _sb(720, I4), "NA": _sb(720, H2), "TM": _sb(13 * 180, H2), "OFF": _sb(900, U2),
 }
 PSUM = ("PCS", "PU", "PD", "PX0", "PX1", "PX2", "PM", "PH")
 for _n in PSUM:
     SCRATCH[_n] = ("psum", [128, 512], F4)
 for _n in BATCH:
     _w = 33 * BATCH[_n][1]
-    for _k, _t in (("CI", F4), ("RM", I4), ("RB", I4), ("RH", H2), ("CJ", I4), ("CK", I4), ("HB", F4), ("VL", F4), ("MX", F4)):
+    for _k, _t in (("RM", I4), ("RB", I4), ("HB", F4), ("VL", F4), ("MX", F4)):
         SCRATCH[_k + _n] = _sb(_w, _t)
-    SCRATCH["OH" + _n] = _sb(16 * (_w + 1), H2)
+    SCRATCH["RH" + _n] = _sb([2, _w + 1], H2)
+    SCRATCH["OH" + _n] = _sb([16, _w + 1], H2)
     SCRATCH["OF" + _n] = _sb(2 * BATCH[_n][1], U2)
     SCRATCH["X" + _n] = _sb(32 * BATCH[_n][1], F4)
 
 SEMAPHORES = ["sV", "sS", "sP", "sG", "ldA", "ldB", "ldH", "ldR", "st", "loc", "arA", "arB", "ar0", "ar1", "ar2", "ar3"]
+
+ROUND = ("Vg02 Sg00 Vg01b Sg01a w0 Vg12 Sg10 Sc0 Vg11b Sg11a w1 Vg22 r0 Sg20 Vg21b Sg21a w2 Vc1 r1 Sc2 r2").split()
+WEIGH = ((2, 0, 1), (2, 0, 1), (2, 0, 1))
 
 
 def _bits(engs):
@@ -132,11 +137,20 @@ def rank_program(g, core, T, topo):
     def tt(out, a, b, o, r, w):
         op("V", lambda: v.tensor_tensor(out, a, b, o), r, w)
 
-    def cp(out, i, r, w):
-        op("V", lambda: v.tensor_copy(out, i), r, w)
-
     def act(out, i, r, w, func=AF.Identity, **kw):
         op("S", lambda: s.activation(out, i, func, **kw), r, w)
+
+    def lin(q, out, i, a, b, r, w):
+        if q == "V":
+            ts(out, i, a, b, A.mult, A.add, r, w)
+        else:
+            act(out, i, r, w, scale=a, bias=b)
+
+    def band(out, i, m, r, w):
+        ts(out, i, m, None, A.bitwise_and, None, r, w)
+
+    def scan(out, a, b, first, o0, o1, r, w):
+        op("V", lambda: v.tensor_tensor_scan(out, a, b, first, o0, o1), r, w)
 
     def mm(out, l, rh, st, sp, r, w):
         op("P", lambda: pe.matmul(out, l, rh, st, sp), r, w, last=sp)
@@ -163,81 +177,84 @@ def rank_program(g, core, T, topo):
     s.dma_start(T.HCI[0:8, 27:28], T.had[:]).then_inc(T.sem.ldH, 16)
     g.sync.dma_start(T.CMB[:], T.came[:, 96:384]).then_inc(T.sem.ldB, 16)
     g.sync.dma_start(T.WIN[:, 0:P], T.ring[:]).then_inc(T.sem.ldR, 16)
-    wr["CMA"], wr["CMB"], wr["HCI"], wr["RING"] = ("ldA", 16), ("ldB", 16), ("ldH", 32), ("ldR", 16)
+    wr["CMA"], wr["CMB"], wr["HCI"] = ("ldA", 16), ("ldB", 16), ("ldH", 32)
+    wr["RINGa"] = wr["RINGb"] = ("ldR", 16)
 
     op("G", lambda: g.iota(T.PCI[:, 0:1], [[0, 1]], 0, 1), [], ["p"])
     iota(T.MG[:], [[16, 8], [0, 16]], 0, 0, ["MG"])
-    iota(T.CBM[:, 0:99], [[0, 3], [512, 33]], 0, 0, ["CBMA"])
+    iota(T.MI[:], [[1, 144]], 0, 0, ["MI"])
     op("V", lambda: v.memset(T.FZ[:, :, 32:33], 0.0), [], ["FA", "FB"])
     op("V", lambda: v.memset(T.PD[:, 0:129:128], -BIG), [], ["PD"])
-    pf, gf, bf = T.PCF[:, 0:1], T.PCF[:, 1:2], T.PCF[:, 2:3]
-    ts(T.PCI[:, 1:2], T.PCI[:, 0:1], 112, None, A.bitwise_and, None, ["p"], ["gi"])
-    ts(T.PCI[:, 2:3], T.PCI[:, 0:1], 15, None, A.bitwise_and, None, ["p"], ["bi"])
-    cp(T.PCF[:, 0:3], T.PCI[:, 0:3], ["p", "gi", "bi"], ["pf"])
+    pf, gf, bf, g15, bB, th0, th1, p15, hb, g1 = [T.PCF[:, i:i + 1] for i in range(10)]
+    band(T.PCI[:, 1:2], T.PCI[:, 0:1], 112, ["p"], ["gi"])
+    band(T.PCI[:, 2:3], T.PCI[:, 0:1], 15, ["p"], ["bi"])
+    lin("V", T.PCF[:, 0:3], T.PCI[:, 0:3], 1.0, 0.0, ["p", "gi", "bi"], ["pf"])
     ts(T.BON[:], T.MG[:], gf, None, A.is_equal, None, ["MG", "pf"], ["BON"])
     op("G", lambda: g.affine_select(T.UT[:], T.BON[:], [[-1, 128]], A.is_gt, 0.0, 0, 1), ["BON"], ["UT"])
     op("G", lambda: g.affine_select(T.UU[:], T.UT[:], [[-1, 128]], A.not_equal, -512.0, 0, 1), ["UT"], ["UU"])
-    iota(T.MI[:], [[1, 144]], 0, 0, ["MI"])
+    iota(T.CBM[:, 0:99], [[0, 3], [512, 33]], 0, 0, ["CBMA"])
     iota(T.CBR[:, 0:99], [[32, 3], [1, 33]], -64, 0, ["CBRA"])
     iota(T.K2[:, 0:6], [[66, 3], [0, 2]], 32, 0, ["K2A"])
-    iota(T.KA[:], [[-TT, 3], [0, 32]], TT * rank, 0, ["KA"])
-    op("V", lambda: v.memset(T.EP[:, 1:2], 0.0), [], ["EP1"])
+    iota(T.CBM[:, 99:297], [[0, 6], [512, 33]], 0, 0, ["CBMB"])
+    iota(T.KA[:], [[-TT, 3], [0, 32]], TT * rank + 2048, 0, ["KA"])
+    iota(T.CBR[:, 99:297], [[32, 6], [1, 33]], 32, 0, ["CBRB"])
+    iota(T.K2[:, 6:24], [[66, 3], [198, 3], [0, 2]], 32, 0, ["K2B"])
+    iota(T.FC[:], [[3 * CAP, 4]], P - 1 + 2 * CAP, 0, ["FC"])
+    for out, i, a, b, key in ((g15, gf, 1.0, 15.0, "g15"), (bB, bf, 1.0, BIG, "bB"), (p15, pf, 1.0, -15.0, "p15"),
+                              (th0, bf, 16.0, 15.5, "th0"), (th1, bf, 16.0, 271.5, "th1"), (hb, bf, -BIG, 0.0, "hb"),
+                              (g1, gf, 1.0, -1.0, "g1")):
+        lin("S", out, i, a, b, ["pf"], [key])
+    op("V", lambda: v.memset(T.NE[:, 1:2], 0.0), [], ["NE1"])
     op("V", lambda: v.memset(T.DL[:, 0:1], float(P)), [], ["DL0"])
-    ts(T.PCF[:, 3:4], gf, 15.0, None, A.add, None, ["pf"], ["g15"])
-    ts(T.PCF[:, 4:5], bf, BIG, None, A.add, None, ["pf"], ["bB"])
-    ts(T.PCF[:, 5:6], bf, 16.0, 15.5, A.mult, A.add, ["pf"], ["th0"])
-    ts(T.PCF[:, 6:7], bf, 16.0, 271.5, A.mult, A.add, ["pf"], ["th1"])
     ts(T.E8[0:8, :], T.MG[0:8, :], 1.0 / 16, T.PCF[0:8, 0:1], A.mult, A.is_equal, ["MG", "pf"], ["E8"])
+    ts(T.WM[:], T.MI[:], g15, bB, A.is_equal, A.mult, ["MI", "g15", "bB"], ["WM"])
+    ts(T.IDB[:], T.MI[:, 0:128], pf, None, A.is_equal, None, ["MI", "pf"], ["IDB"])
+    ts(T.EH[:], T.MG[:], p15, None, A.is_equal, None, ["MG", "p15"], ["EH"])
+    ts(T.EB[:], T.MG[:], p15, -512.0, A.is_equal, A.mult, ["MG", "p15"], ["EB"])
+    lin("S", T.IDH[:], T.IDB[:], 1.0, 0.0, ["IDB"], ["IDH"])
 
     def lists(b):
         s0, ns, c0 = BATCH[b]
         w = 33 * ns
         F = T.FZ[:, s0:s0 + ns, :]
-        CI, RM, RB, RH, OH, CJ, CK, HB, VL, MX = [T[x + b] for x in ("CI", "RM", "RB", "RH", "OH", "CJ", "CK", "HB", "VL", "MX")]
+        CI = T.CI[:, 33 * s0:33 * s0 + w]
+        RM, RB, RH, OH, HB, VL, MX = [T[x + b] for x in ("RM", "RB", "RH", "OH", "HB", "VL", "MX")]
         a0 = 2 * s0
         OF, X, K = T["OF" + b], T["X" + b], T["K" + b]
         ne = ns // 3
-        pd = T.PD[:, c0 + 1:c0 + 1 + w]
+        pd, pc = T.PD[:, c0 + 1:c0 + 1 + w], T.PX1[:, c0:c0 + w]
 
-        def flags():
-            cp(T.FZ[:, s0:s0 + ns, 0:32], T["CM" + b][:], ["CM" + b], ["F" + b])
+        def flags(q):
+            lin(q, T.FZ[:, s0:s0 + ns, 0:32], T["CM" + b][:], 1.0, 0.0, ["CM" + b], ["F" + b])
             mm(T.PCS[:, c0:c0 + w], T.BON[:], F, True, True, ["BON", "F" + b], ["PCS"])
             mm(T.PU[:, c0:c0 + w], T.UU[:], F, True, True, ["UU", "F" + b], ["PU"])
 
-        def sums():
-            op("V", lambda: v.tensor_tensor_scan(CI[:], T.CBM[:, 0:w], T.PCS[:, c0:c0 + w], 0.0, A.min, A.add),
-               ["CBMA", "CBM" + b, "PCS"], ["CI" + b])
-
-        def ranks():
-            tt(RM[:], CI[:], T.PU[:, c0:c0 + w], A.subtract, ["CI" + b, "PU"], ["RM" + b])
-            cp(CJ[:], CI[:], ["CI" + b], ["CJ" + b])
-            ts(RB[:], RM[:], 527, None, A.bitwise_and, None, ["RM" + b], ["RB" + b])
-            ts(CK[:], CJ[:], 15, None, A.bitwise_and, None, ["CJ" + b], ["CK" + b])
-            cp(RH[:], RB[:], ["RB" + b], ["RH" + b])
-            ts(HB[:], CK[:], bf, BIG, A.is_gt, A.mult, ["CK" + b, "pf"], ["HB" + b])
+        def halves(q0, q1):
+            lin(q0, RH[:, 0, 0:w], RB[:], 1.0, 0.0, ["RB" + b], ["RH0" + b])
+            lin(q1, RH[:, 1, 0:w], RB[:], 1.0, -8.0, ["RB" + b], ["RH1" + b])
+            mm(pc, T.EH[:], RH[:, 0, 0:w], True, False, ["EH", "RH0" + b], ["PX1"])
+            mm(pc, T.EB[:], F, False, True, ["EB", "F" + b], ["PX1"])
             mm(pd, T.BON[:], T.CBR[:, 0:w], True, False, ["BON", "CBRA", "CBR" + b], ["PD"])
 
-        def ends():
-            for i in range(2 * ns):
+        def ends(lo, hi):
+            for i in range(lo, hi):
                 h = i % 2
-                sl = 3 * ((i // 2) % ne) + i // (2 * ne)
-                act(T.JK[:, 32 * (a0 + i):32 * (a0 + i + 1)], CI[:, 33 * sl:33 * sl + 32], ["CI" + b, "th%d" % h],
-                    ["ACC%d" % (a0 + i)], func=AF.Sign, scale=-1.0, bias=T.PCF[:, 5 + h:6 + h],
-                    accum_out=T.ACC[:, a0 + i:a0 + i + 1])
+                sl = s0 + 3 * ((i // 2) % ne) + i // (2 * ne)
+                act(T.JK[:, 32 * (a0 + i):32 * (a0 + i + 1)], T.CI[:, 33 * sl:33 * sl + 32], ["CI" + b, "th%d" % h],
+                    ["ACC%d" % (a0 + i)], func=AF.Sign, scale=-1.0, bias=(th0, th1)[h], accum_out=T.ACC[:, a0 + i:a0 + i + 1])
 
-        def hot():
-            for k in range(16):
-                o = OH[:, k * (w + 1):k * (w + 1) + w]
-                ts(o, RH[:], float(512 + ((k + 1) & 15)), None, A.is_equal, None, ["RH" + b], ["OH%s%d" % (b, k)])
-                mm(pd, T.WM[:, 15 - k:143 - k], o, False, k == 15, ["WM", "OH%s%d" % (b, k)], ["PD"])
+        def hot(lo=0, hi=8):
+            for j in range(lo, hi):
+                ts(OH[:, j:16:8, 0:w], RH[:, :, 0:w], float(512 + j), None, A.is_equal, None, ["RH0" + b, "RH1" + b],
+                   ["OH%s%d" % (b, j)])
+                for m in (j, j + 8):
+                    k = (m - 1) % 16
+                    mm(pd, T.WM[:, 15 - k:143 - k], OH[:, m, 0:w], False, m == 15, ["WM", "OH%s%d" % (b, j)], ["PD"])
+
+        def cols(q):
             tt(T.AC2[:, a0:a0 + 2 * ns], T.ACC[:, a0:a0 + 2 * ns], T.K2[:, a0:a0 + 2 * ns], A.add,
                ["ACC%d" % (a0 + i) for i in range(2 * ns)] + ["K2" + b], ["AC2" + b])
-
-        finish = [lambda: ts(OF[:], T.AC2[:, a0:a0 + 2 * ns], 0.5, None, A.mult, None, ["AC2" + b], ["OF" + b]),
-                  lambda: tt(VL[:], pd, HB[:], A.subtract, ["PD", "HB" + b], ["VL" + b]),
-                  lambda: op("V", lambda: v.tensor_tensor_scan(MX[:], T.PD[:, c0:c0 + w], VL[:], -BIG, A.max, A.max),
-                             ["PD", "VL" + b], ["MX" + b]),
-                  lambda: tt(X[:], MX[:].indirect(OF[:]), K[:], A.add, ["MX" + b, "OF" + b, "K" + b], ["X" + b])]
+            lin(q, OF[:], T.AC2[:, a0:a0 + 2 * ns], 0.5, 0.0, ["AC2" + b], ["OF" + b])
 
         def send():
             deps("G", ["X" + b], [])
@@ -253,78 +270,85 @@ def rank_program(g, core, T, topo):
                 sent[0] += len(el)
             g.remote_dma_fused(trs, local_sem=T.sem.loc)
 
-        return flags, sums, ranks, ends, hot, finish, send
+        return {
+            "flags": flags, "halves": halves, "ends": ends, "hot": hot, "cols": cols, "send": send,
+            "sums": lambda: scan(CI, T.CBM[:, 0:w], T.PCS[:, c0:c0 + w], 0.0, A.min, A.add, ["CBMA", "CBM" + b, "PCS"], ["CI" + b]),
+            "rank": lambda: tt(RM[:], CI, T.PU[:, c0:c0 + w], A.subtract, ["CI" + b, "PU"], ["RM" + b]),
+            "mask": lambda: band(RB[:], RM[:], 527, ["RM" + b], ["RB" + b]),
+            "next": lambda: act(HB[:], pc, ["PX1", "hb"], ["HB" + b], func=AF.Relu, scale=BIG, bias=hb),
+            "drop": lambda: tt(VL[:], pd, HB[:], A.subtract, ["PD", "HB" + b], ["VL" + b]),
+            "run": lambda: scan(MX[:], T.PD[:, c0:c0 + w], VL[:], -BIG, A.max, A.max, ["PD", "VL" + b], ["MX" + b]),
+            "pick": lambda: tt(X[:], MX[:].indirect(OF[:]), K[:], A.add, ["MX" + b, "OF" + b, "K" + b], ["X" + b]),
+        }
 
-    def hash_(e):
+    def hash_(e, qs="SSS"):
         key = "LB" if e else "LA"
         x = T.LB[:, :, 32 * (e - 1):32 * (e - 1) + CW] if e else T.LA[:]
         c = 180 * e
         z1, z2, z3, h = [z[:, c:c + 180] for z in (T.Z1, T.Z2, T.Z3, T.Z4)]
-        bank = "PH" if e % 2 == 0 else "PU"
-        ph = T[bank][:, 64:244]
 
-        def lin():
+        def first():
             for k in range(3):
-                ts(T.Z1[:, c + 60 * k:c + 60 * k + 60], x, T.HC[:, 6 * e + k:6 * e + k + 1],
-                   T.HC[:, 6 * e + 3 + k:6 * e + 4 + k], A.mult, A.add, [key, "HC"], ["Z1%d%d" % (e, k)])
+                lin(qs[k], T.Z1[:, c + 60 * k:c + 60 * k + 60], x, T.HC[:, 6 * e + k:6 * e + k + 1],
+                    T.HC[:, 6 * e + 3 + k:6 * e + 4 + k], [key, "HC"], ["Z1%d%d" % (e, k)])
 
-        return [lin,
-                lambda: ts(z2, z1, 4095, None, A.bitwise_and, None, ["Z1%d%d" % (e, k) for k in range(3)], ["Z2%d" % e]),
-                lambda: ts(ph, z2, 2.0, -4095.0, A.mult, A.add, ["Z2%d" % e], [bank]),
-                lambda: tt(z3, z2, ph, A.mult, ["Z2%d" % e, bank], ["Z3%d" % e]),
-                lambda: ts(h, z3, 4095, None, A.bitwise_and, None, ["Z3%d" % e], ["Z4%d" % e])]
+        return [first,
+                lambda: band(z2, z1, 4095, ["Z1%d%d" % (e, k) for k in range(3)], ["Z2%d" % e]),
+                lambda: act(z3, z2, ["Z2%d" % e], ["Z3%d" % e], func=AF.Square, scale=2.0, bias=-4095.5),
+                lambda: band(h, z3, 8190, ["Z3%d" % e], ["Z4%d" % e])]
 
     def place(e):
-        off = T.OFF[:, 180 * e:180 * e + 180]
         if e == 0:
-            return [lambda: ts(off, T.Z4[:, 0:180], T.NC[:, 4:5], EPS - 0.5, A.mult, A.add, ["Z40", "C0"], ["OFF0"])]
+            return [lambda: lin("S", T.OFF[:, 0:180], T.Z4[:, 0:180], T.NC[:, 8:9], EPS - 0.5, ["Z40", "C0"], ["OFF0"])]
         w = 180 if e < NR else 128
+        c = 180 * (e - 1)
+        z5, z6, na = T.Z5[:, c:c + w], T.Z6[:, c:c + w], T.NA[:, c:c + w]
 
         def age():
             if e < NR:
-                ts(T.Z5[:], T.Z4[:, 180 * e:180 * e + 180], T.NC[:, e - 1:e], T.MU[:, e - 1:e], A.mult, A.add,
-                   ["Z4%d" % e, "NC", "MU"], ["Z5"])
+                lin("S", z5, T.Z4[:, 180 * e:180 * e + 180], T.NC[:, e:e + 1], T.MU[:, e:e + 1], ["Z4%d" % e, "NC", "MU"],
+                    ["Z5%d" % e])
             else:
-                ts(T.Z5[:, 0:w], T.PLC[:], -1.0, T.MU[:, e - 1:e], A.mult, A.add, ["PLC", "MU"], ["Z5"])
+                lin("S", z5, T.PLC[:], -1.0, T.MM[:, 5:6], ["PLC", "MUG"], ["Z5%d" % e])
 
         def steps():
-            mm(T.PM[:, 0:w], T.IDH[:], T.NA[:, 0:w], True, False, ["IDH", "NA"], ["PM"])
+            mm(T.PM[:, 0:w], T.IDH[:], na, True, False, ["IDH", "NA%d" % e], ["PM"])
             for i in range(3 * e + 1):
                 o = T.TM[:, 180 * i:180 * i + w]
-                c = 16 * (e - 1) + i
-                ts(o, T.NA[:, 0:w], T.TH[:, c:c + 1], T.DL[:, i:i + 1], A.is_le, A.mult,
-                   ["NA", "TH%d" % e, "DL0", "DL1", "DL2"], ["TM%d" % i])
+                t = 16 * (e - 1) + i
+                ts(o, na, T.TH[:, t:t + 1], T.DL[:, i:i + 1], A.is_le, A.mult,
+                   ["NA%d" % e, "TH%d" % e, "DL0", "DL1", "DL2"], ["TM%d" % i])
                 mm(T.PM[:, 0:w], T.IDH[:], o, False, i == 3 * e, ["IDH", "TM%d" % i], ["PM"])
 
         return [age,
-                lambda: ts(T.Z6[:, 0:w], T.Z5[:, 0:w], P - 1, None, A.bitwise_and, None, ["Z5"], ["Z6"]),
-                lambda: ts(T.NA[:, 0:w], T.Z6[:, 0:w], -1.0, None, A.mult, None, ["Z6"], ["NA"]),
+                lambda: band(z6, z5, P - 1, ["Z5%d" % e], ["Z6%d" % e]),
+                lambda: lin("S", na, z6, -1.0, 0.0, ["Z6%d" % e], ["NA%d" % e]),
                 steps,
-                lambda: ts(off[:, 0:w], T.PM[:, 0:w], T.CNT[:, 3 * e - 1:3 * e], float(P - 1 + CAP * (3 * e - 1)),
-                           A.add, A.add, ["PM", "CNTA", "CNTB"], ["OFF%d" % e])]
+                lambda: lin("S", T.OFF[:, 180 * e:180 * e + w], T.PM[:, 0:w], 1.0, T.FB[:, e - 1:e], ["PM", "FB"], ["OFF%d" % e])]
 
-    def gather(q, e, j, k, lo=0, hi=CW):
+    def gather(q, e, j, k, part):
+        lo, hi = {"": (0, CW), "a": (0, CW // 2), "b": (CW // 2, CW)}[part]
         c = 180 * e + 60 * k + CW * j
         win = T.WIN[:, 0:P + 3 * CAP * e].indirect(T.OFF[:, c + lo:c + hi])
         o = T.GG[:, CAP * (3 * j + k) + 16 * lo:CAP * (3 * j + k) + 16 * hi]
-        r = ["RING", "OFF%d" % e] + ["W%d" % i for i in range(e)]
-        w = ["G%d%d%s" % (j, k, h) for h in ("a" if lo == 0 else "") + ("b" if hi == CW else "")]
+        r = ["RINGa", "RINGb", "OFF%d" % e] + ["W%d" % i for i in range(e)]
+        w = ["G%d%d%s" % (j, k, h) for h in (part or "ab")]
         if q == "V":
-            cp(o, win, r, w)
+            op("V", lambda: v.tensor_copy(o, win), r, w)
         else:
             act(o, win, r, w, func=AF.Copy)
 
-    def weigh(j, order):
-        for i, k in enumerate(order):
+    def weigh(j):
+        for i, k in enumerate(WEIGH[j]):
             mm(T["PX%d" % j][:, 0:CAP], T.DG[:, 128 * k:128 * k + 128], T.GG[:, CAP * (3 * j + k):CAP * (3 * j + k + 1)],
                i == 0, i == 2, ["DG%d" % k, "G%d%da" % (j, k), "G%d%db" % (j, k)], ["PX%d" % j])
 
-    def reduce_send(e, j, between):
-        px, ki = T["PX%d" % j][:, 0:CAP], T.KI[:, CAP * j:CAP * (j + 1)]
+    def whole(q, j):
+        lin(q, T.KI[:, CAP * j:CAP * (j + 1)], T["PX%d" % j][:, 0:CAP], 1.0, -127.5 / 256, ["PX%d" % j], ["KI%d" % j])
+
+    def rest(e, j):
         o = T.OUT[:, CAP * (3 * e + j):CAP * (3 * e + j + 1)]
-        ts(ki, px, -127.5 / 256, None, A.add, None, ["PX%d" % j], ["KI%d" % j])
-        between()
-        tt(o, px, ki, A.subtract, ["PX%d" % j, "KI%d" % j], ["O%d%d" % (e, j)])
+        tt(o, T["PX%d" % j][:, 0:CAP], T.KI[:, CAP * j:CAP * (j + 1)], A.subtract, ["PX%d" % j, "KI%d" % j], ["O%d%d" % (e, j)])
         r, en = peers[j][0:2]
         rid, pid = topo.addr(T.cores[r], core)
         c = P + CAP * (3 * e + (rank - r) % n - 1)
@@ -332,114 +356,94 @@ def rank_program(g, core, T, topo):
         g.remote_dma(T.WIN[:, c:c + CAP], o, T.sem["ar%d" % e], T.sem.loc, pid, rid, _bits(en))
         sent[0] += len(en)
 
-    def round_(e, fill):
-        h = CW // 2
-        gather("V", e, 0, 2)
-        gather("S", e, 0, 0)
-        gather("V", e, 0, 1, h, CW)
-        gather("S", e, 0, 1, 0, h)
-        weigh(0, (2, 0, 1))
-        gather("V", e, 1, 2, 0, h)
-        gather("S", e, 1, 0)
-        gather("S", e, 1, 1)
-        gather("S", e, 1, 2, h, CW)
-        reduce_send(e, 0, fill[0])
-        weigh(1, (0, 1, 2))
-        gather("V", e, 2, 2)
-        gather("S", e, 2, 0)
-        gather("S", e, 2, 1)
-        fill[1]()
-        reduce_send(e, 1, fill[2])
-        weigh(2, (2, 0, 1))
-        fill[3]()
-        reduce_send(e, 2, fill[4])
+    def round_(e, fill=None):
+        for st in ROUND:
+            if st[0] == "w":
+                weigh(int(st[1]))
+            elif st[0] == "r":
+                rest(e, int(st[1]))
+            elif st[1] == "c":
+                whole(st[0], int(st[2]))
+            else:
+                gather(st[0], e, int(st[2]), int(st[3]), st[4:])
+            for f in (fill or {}).get(st, []):
+                f()
 
-    def idle():
-        return None
-
-    fA, cA, rA, eA, hA, zA, sA = lists("A")
-    fB, cB, rB, eB, hB, zB, sB = lists("B")
+    a, b = lists("A"), lists("B")
     had = T.HC[:, 27:28]
 
-    fA()
-    ts(T.WM[:], T.MI[:], T.PCF[:, 3:4], T.PCF[:, 4:5], A.is_equal, A.mult, ["MI", "g15", "bB"], ["WM"])
-    cA()
-    ts(T.IDB[:], T.MI[:, 0:128], pf, None, A.is_equal, None, ["MI", "pf"], ["IDB"])
-    rA()
-    eA()
-    hA()
-    cp(T.HCF[0:8, :], T.HCI[0:8, :], ["HCI"], ["HCF"])
+    a["flags"]("V")
+    lin("V", T.HCF[0:8, :], T.HCI[0:8, :], 1.0, 0.0, ["HCI"], ["HCF"])
     mm(T.PH[:, 0:28], T.E8[0:8, :], T.HCF[0:8, :], True, True, ["E8", "HCF"], ["PH"])
+    a["sums"]()
+    a["rank"]()
+    b["flags"]("S")
+    a["ends"](0, 2)
+    a["mask"]()
+    a["halves"]("V", "S")
+    a["ends"](2, 6)
+    a["next"]()
+    a["hot"]()
     act(T.HC[:], T.PH[:, 0:28], ["PH"], ["HC"])
-    iota(T.CBM[:, 99:297], [[0, 6], [512, 33]], 0, 0, ["CBMB"])
-    iota(T.CBR[:, 99:297], [[32, 6], [1, 33]], 32, 0, ["CBRB"])
-    iota(T.K2[:, 6:24], [[66, 3], [198, 3], [0, 2]], 32, 0, ["K2B"])
-    _mix(zA[0:2] + [fB, zA[2], lambda: cp(T.HI[:, 0:1], had, ["HC"], ["HI0"]), zA[3]])
-    sA()
-    iota(T.KB[:], [[-TT, 3], [-3 * TT, 3], [0, 32]], TT * rank, 0, ["KB"])
-    iota(T.PLC[:, 0:128], [[16, 128]], 0, 0, ["PL0"])
-    act(T.WIN[:, 0:P], T.WIN[:, 0:P], ["RING"], ["RING"], scale=1.0 / 256)
+    a["cols"]("S")
+    b["sums"]()
+    a["drop"]()
+    b["rank"]()
+    a["run"]()
+    b["mask"]()
+    a["pick"]()
+    a["send"]()
+    iota(T.KB[:], [[-TT, 3], [-3 * TT, 3], [0, 32]], TT * rank + 2048, 0, ["KB"])
+    iota(T.PLC[:], [[16, 128]], 0, 1, ["PLC"])
 
-    def sums():
-        op("V", lambda: v.tensor_tensor_scan(T.EP[:, 2:14], T.CNT[:], T.CNT[:], 0.0, A.add, A.max), ["CNTA", "CNTB"], ["EP2"])
-
-    def firsts():
-        ts(T.MUI[:, 0:4], T.EP[:, 4:14:3], had, -1.0, A.add, A.add, ["EP2", "HC"], ["MU0"])
-
-    def tail():
-        sB()
-        ts(T.HI[:, 1:2], T.HI[:, 0:1], P - 1, None, A.bitwise_and, None, ["HI0"], ["HI1"])
-
-    def masks():
-        ts(T.EP[:, 0:1], T.HI[:, 1:2], -1.0, None, A.mult, None, ["HI1"], ["EP0"])
-        ts(T.MUI[:, 4:8], T.MUI[:, 0:4], P - 1, None, A.bitwise_and, None, ["MU0"], ["MU1"])
-
-    cB()
-    ts(T.NC[:, 4:5], had, float(P), 1.0 / 4096, A.min, A.mult, ["HC"], ["C0"])
-    rB()
-    eB()
-    for k in range(3):
-        act(T.DG[:, 128 * k:128 * k + 128], T.IDB[:], ["IDB", "HC"], ["DG%d" % k], scale=T.HC[:, 24 + k:25 + k])
-    act(T.CNT[:, 0:3], T.CIA[:, 32:99:33], ["CIA"], ["CNTA"])
-    act(T.CNT[:, 3:12], T.CIB[:, 32:297:33], ["CIB"], ["CNTB"])
-    hB()
-    zB[0]()
-    _mix(zB[1:4] + [tail, sums, firsts], hash_(0) + place(0))
-
-    h1, h2, h3 = hash_(1), hash_(2), hash_(3)
+    lin("S", T.WIN[:, 0:P // 2], T.WIN[:, 0:P // 2], 1.0 / 256, 0.0, ["RINGa"], ["RINGa"])
+    b["halves"]("S", "V")
+    cn = T.CI[:, 32:396:33]
+    scan(T.NE[:, 2:14], cn, cn, 0.0, A.min, A.subtract, ["CIA", "CIB"], ["NE2"])
+    b["ends"](0, 18)
+    b["next"]()
+    b["hot"]()
+    lin("S", T.MM[:, 0:5], T.NE[:, 1:14:3], -1.0, had, ["NE1", "NE2", "HC"], ["MM"])
+    b["cols"]("S")
+    lin("V", T.WIN[:, P // 2:P], T.WIN[:, P // 2:P], 1.0 / 256, 0.0, ["RINGb"], ["RINGb"])
+    act(T.NC[:, 4:8], T.MM[:, 0:4], ["MM"], ["NR"], func=AF.Relu, scale=-1.0, bias=float(P))
+    lin("S", T.MUI[:, 0:4], T.MM[:, 0:4], 1.0, -1.0, ["MM"], ["MU0"])
+    lin("S", T.NC[:, 8:9], T.NC[:, 4:5], -1.0 / 8192, 0.25, ["NR"], ["C0"])
+    h0, h1, h2, h3 = hash_(0), hash_(1), hash_(2), hash_(3)
     p1, p2, p3, p4 = place(1), place(2), place(3), place(NR)
-    round_(0, [masks, idle,
-               lambda: ts(T.MU[:], T.MUI[:, 4:8], 0.5 - EPS, None, A.add, None, ["MU1"], ["MU"]), idle,
-               lambda: ts(T.IDH[:], T.MI[:, 0:128], pf, None, A.is_equal, None, ["MI", "pf"], ["IDH"])])
-    act(T.MM[:], T.EP[:, 4:14:3], ["EP2", "HC"], ["MM"], bias=had)
-    act(T.NEP[:, 1:14], T.EP[:, 1:14], ["EP1", "EP2"], ["NEP"], scale=-1.0)
-    act(T.NC[:, 8:12], T.MM[:], ["MM"], ["NR"], func=AF.Relu, scale=-1.0, bias=float(P))
-    act(T.DL[:, 2:13], T.CNT[:, 0:11], ["CNTA", "CNTB"], ["DL2"], bias=-float(CAP))
-    act(T.NC[:, 0:4], T.NC[:, 8:12], ["NR"], ["NC"], scale=1.0 / 4096, bias=-0.5)
-    act(T.DL[:, 1:2], T.EP[:, 0:1], ["EP0"], ["DL1"], scale=-1.0, bias=-float(P))
-    for e in range(1, NR + 1):
-        act(T.TH[:, 16 * (e - 1):16 * (e - 1) + 13], T.EP[:, 0:13], ["EP0", "EP1", "EP2", "NEP"], ["TH%d" % e],
-            bias=T.NEP[:, 1 + 3 * e:2 + 3 * e])
-    act(T.PLC[:], T.PLC[:], ["PL0", "pf"], ["PLC"], bias=bf)
-    deps("Y", ["MM"], [])
-    g.sync.dma_start(T.now[:], T.MM[0:128:16, 3:4]).then_inc(T.sem.st, 16)
 
-    _mix(h1 + p1, [idle, h2[0], h2[1], h2[2], idle, h2[3], h2[4]])
-    round_(1, [p2[0], h3[0], p2[1], h3[1], p2[2]])
-    _mix([p2[3], h3[2], p2[4]])
-    round_(2, [h3[3], h3[4], p3[0], p3[1], p3[2]])
-    _mix([p3[3], p4[0], p3[4]])
-    round_(3, [p4[1], idle, p4[2], idle, idle])
+    def weight(k):
+        return lambda: lin("S", T.DG[:, 128 * k:128 * k + 128], T.IDB[:], T.HC[:, 24 + k:25 + k], 0.0, ["IDB", "HC"], ["DG%d" % k])
+
+    def bound(e):
+        return lambda: lin("S", T.TH[:, 16 * (e - 1):16 * (e - 1) + 13], T.NE[:, 0:13], -1.0, T.NE[:, 1 + 3 * e:2 + 3 * e],
+                           ["NE0", "NE1", "NE2"], ["TH%d" % e])
+
+    _mix([b["drop"], h0[0], b["run"], h0[1], weight(2), h0[2], b["pick"], b["send"], weight(0), h0[3],
+          lambda: band(T.MUI[:, 4:8], T.MUI[:, 0:4], P - 1, ["MU0"], ["MU1"]), weight(1), place(0)[0]])
+    deps("Y", ["MM"], [])
+    g.sync.dma_start(T.now[:], T.MM[0:128:16, 4:5]).then_inc(T.sem.st, 16)
+    counts = [lambda: lin("V", T.NE[:, 0:1], T.MUI[:, 4:5], 1.0, 1.0, ["MU1"], ["NE0"]),
+              lambda: lin("V", T.DL[:, 1:2], T.MUI[:, 4:5], 1.0, 1.0 - P, ["MU1"], ["DL1"]),
+              lambda: lin("V", T.MU[:], T.MUI[:, 4:8], 1.0, 0.5 - EPS, ["MU1"], ["MU"]),
+              lambda: lin("V", T.NC[:, 0:4], T.NC[:, 4:8], 1.0 / 8192, -0.25, ["NR"], ["NC"]),
+              lambda: lin("V", T.DL[:, 2:13], T.CI[:, 32:363:33], 1.0, -float(CAP), ["CIA", "CIB"], ["DL2"]),
+              lambda: tt(T.FB[:], T.CI[:, 98:396:99], T.FC[:], A.add, ["CIA", "CIB", "FC"], ["FB"])]
+    _mix(counts[0:2])
+
+    round_(0, {"Sg21a": h1[0:1], "Vc1": counts[2:3], "r1": h1[1:2], "Sc2": h1[2:3], "r2": h1[3:4]})
+    _mix([counts[3], p1[0], counts[4], bound(1), p1[1], h2[0], counts[5], p1[2], h2[1], p1[3], h2[2], bound(2), h2[3], p1[4]])
+    round_(1, {"Sg21a": [p2[0], bound(3)], "r1": p2[1:2], "Sc2": [p2[2], h3[0]]})
+    _mix([p2[3], h3[1], p2[4], h3[2], h3[3]])
+    round_(2, {"Sg21a": [p3[0], bound(4)], "r1": p3[1:2], "Sc2": p3[2:3]})
+    _mix([p3[3], lambda: lin("S", T.MM[:, 5:6], T.MM[:, 4:5], 1.0, g1, ["MM", "g1"], ["MUG"]), p4[0], p3[4]])
+    round_(3, {"Vc1": p4[1:2], "Sc2": p4[2:3]})
 
     _mix(p4[3:5])
-    r = ["RING", "OFF4"] + ["W%d" % i for i in range(NR)]
+    r = ["RINGa", "RINGb", "OFF4"] + ["W%d" % i for i in range(NR)]
     pieces = (("V", 0, 256), ("S", 256, 512), ("V", 512, 896), ("S", 896, 1280), ("V", 1280, 1664), ("S", 1664, 2048))
     for q, lo, hi in pieces:
-        win = T.WIN[:].indirect(T.OFF[:, 720 + lo // 16:720 + hi // 16])
-        if q == "V":
-            ts(T.YY[:, lo:hi], win, 256.0, None, A.mult, None, r, ["Y%d" % lo])
-        else:
-            act(T.YY[:, lo:hi], win, r, ["Y%d" % lo], scale=256.0)
+        lin(q, T.YY[:, lo:hi], T.WIN[:].indirect(T.OFF[:, 720 + lo // 16:720 + hi // 16]), 256.0, 0.0, r, ["Y%d" % lo])
         dq = "S" if hi == P else "Y"
         deps(dq, ["Y%d" % lo], [])
         Q[dq].dma_start(T.y[:, lo:hi], T.YY[:, lo:hi]).then_inc(T.sem.st, 16)

@@ -19,12 +19,12 @@ SCRATCH = {
     "PCI": _sb(4, I4), "PCF": _sb(12, F4), "MG": _sb(128, B2), "MI": _sb(144, F4), "BON": _sb(128, B2), "UT": _sb(128, B2),
     "UU": _sb(128, B2), "WM": _sb(144, H2), "E8": _sb(128, F4), "IDB": _sb(128, B2), "IDH": _sb(128, H2), "DG": _sb(384, B2),
     "EH": _sb(128, H2), "EB": _sb(128, B2),
-    "CBM": _sb(297, F4), "CBR": _sb(297, B2), "K2": _sb(24, F4), "KA": _sb(96, F4), "KB": _sb(288, F4), "PLC": _sb(128, F4),
-    "JK": _sb(768, B2), "ACC": _sb(24, F4), "AC2": _sb(24, F4), "LA": _sb([3, CW], F4), "LB": _sb([3, 96], F4),
+    "CBM": _sb(297, B2), "CBR": _sb(297, B2), "K2": _sb(24, F4), "KA": _sb(96, F4), "KB": _sb(288, F4), "PLC": _sb(128, F4),
+    "JK": _sb(768, B2), "ACC": _sb(24, F4), "AC2": _sb(24, F4), "LA": _sb([3, CW], U2), "LB": _sb([3, 96], U2),
     "FZ": _sb([12, 33], B2), "CI": _sb(396, F4), "NE": _sb(14, F4), "DL": _sb(13, F4), "FC": _sb(4, F4), "FB": _sb(4, F4),
     "MM": _sb(6, F4), "NC": _sb(9, F4), "MUI": _sb(8, I4), "MU": _sb(4, F4), "TH": _sb(64, F4),
     "Z1": _sb(720, I4), "Z2": _sb(720, I4), "Z3": _sb(720, I4), "Z4": _sb(720, I4),
-    "Z5": _sb(720, I4), "Z6": _sb(720, I4), "NA": _sb(720, H2), "TM": _sb(13 * 180, H2), "OFF": _sb(900, U2),
+    "Z5": _sb(900, I4), "Z6": _sb(900, I4), "NA": _sb(900, H2), "TM": _sb(13 * 180, H2), "OFF": _sb(900, U2),
 }
 PSUM = ("PCS", "PU", "PD", "PX0", "PX1", "PX2", "PM", "PH")
 for _n in PSUM:
@@ -36,12 +36,13 @@ for _n in BATCH:
     SCRATCH["RH" + _n] = _sb([2, _w + 1], H2)
     SCRATCH["OH" + _n] = _sb([16, _w + 1], H2)
     SCRATCH["OF" + _n] = _sb(2 * BATCH[_n][1], U2)
-    SCRATCH["X" + _n] = _sb(32 * BATCH[_n][1], F4)
+    SCRATCH["X" + _n] = _sb(32 * BATCH[_n][1], U2)
 
 SEMAPHORES = ["sV", "sS", "sP", "sG", "ldA", "ldB", "ldH", "ldR", "st", "loc", "arA", "arB", "ar0", "ar1", "ar2", "ar3"]
 
-ROUND = ("Vg02 Sg00 Vg01b Sg01a w0 Vg12 Sg10 Sc0 Vg11b Sg11a w1 Vg22 r0 Sg20 Vg21b Sg21a w2 Vc1 r1 Sc2 r2").split()
-WEIGH = ((2, 0, 1), (2, 0, 1), (2, 0, 1))
+ROUND = ("Vg00 Sg02 Vg01 Sg10 w0 Vg12 Sg11 w1 Vg22 Sc0 Sg20 r0 Vg21a Sc1 Vg21b w2ab r1 Sc2a Sc2b r2a r2b").split()
+WHOLE, THIRDS = ((0, 3),), ((0, 1), (1, 2), (2, 3))
+WEIGH = ((0, 2, 1), (0, 2, 1), (2, 0, 1))
 
 
 def _bits(engs):
@@ -68,7 +69,7 @@ def _peers(T, topo, q):
         res.append((r, en, en[i * k:(i + 1) * k], en[i * k:(i + 1) * k]))
     for r in near:
         en = [x for x in topo.engines(me, T.cores[r]) if x not in used]
-        res.append((r, en, en[:k], en))
+        res.append((r, topo.engines(me, T.cores[r]), en[:k], en))
     return res
 
 
@@ -188,14 +189,14 @@ def rank_program(g, core, T, topo):
     pf, gf, bf, g15, bB, th0, th1, p15, hb, g1 = [T.PCF[:, i:i + 1] for i in range(10)]
     band(T.PCI[:, 1:2], T.PCI[:, 0:1], 112, ["p"], ["gi"])
     band(T.PCI[:, 2:3], T.PCI[:, 0:1], 15, ["p"], ["bi"])
+    op("V", lambda: v.memset(T.CBM[:], float(TT)), [], ["CBM"])
     lin("V", T.PCF[:, 0:3], T.PCI[:, 0:3], 1.0, 0.0, ["p", "gi", "bi"], ["pf"])
+    op("V", lambda: v.memset(T.CBM[:, 0:297:33], 0.0), [], ["CBM"])
     ts(T.BON[:], T.MG[:], gf, None, A.is_equal, None, ["MG", "pf"], ["BON"])
     op("G", lambda: g.affine_select(T.UT[:], T.BON[:], [[-1, 128]], A.is_gt, 0.0, 0, 1), ["BON"], ["UT"])
     op("G", lambda: g.affine_select(T.UU[:], T.UT[:], [[-1, 128]], A.not_equal, -512.0, 0, 1), ["UT"], ["UU"])
-    iota(T.CBM[:, 0:99], [[0, 3], [512, 33]], 0, 0, ["CBMA"])
     iota(T.CBR[:, 0:99], [[32, 3], [1, 33]], -64, 0, ["CBRA"])
     iota(T.K2[:, 0:6], [[66, 3], [0, 2]], 32, 0, ["K2A"])
-    iota(T.CBM[:, 99:297], [[0, 6], [512, 33]], 0, 0, ["CBMB"])
     iota(T.KA[:], [[-TT, 3], [0, 32]], TT * rank + 2048, 0, ["KA"])
     iota(T.CBR[:, 99:297], [[32, 6], [1, 33]], 32, 0, ["CBRB"])
     iota(T.K2[:, 6:24], [[66, 3], [198, 3], [0, 2]], 32, 0, ["K2B"])
@@ -222,19 +223,19 @@ def rank_program(g, core, T, topo):
         a0 = 2 * s0
         OF, X, K = T["OF" + b], T["X" + b], T["K" + b]
         ne = ns // 3
+        cs, cu = ("PCS", "PU") if b == "A" else ("PX0", "PX2")
         pd, pc = T.PD[:, c0 + 1:c0 + 1 + w], T.PX1[:, c0:c0 + w]
 
         def flags(q):
             lin(q, T.FZ[:, s0:s0 + ns, 0:32], T["CM" + b][:], 1.0, 0.0, ["CM" + b], ["F" + b])
-            mm(T.PCS[:, c0:c0 + w], T.BON[:], F, True, True, ["BON", "F" + b], ["PCS"])
-            mm(T.PU[:, c0:c0 + w], T.UU[:], F, True, True, ["UU", "F" + b], ["PU"])
+            mm(T[cs][:, 0:w], T.BON[:], F, True, True, ["BON", "F" + b], [cs])
+            mm(T[cu][:, 0:w], T.UU[:], F, True, True, ["UU", "F" + b], [cu])
 
         def halves(q0, q1):
             lin(q0, RH[:, 0, 0:w], RB[:], 1.0, 0.0, ["RB" + b], ["RH0" + b])
             lin(q1, RH[:, 1, 0:w], RB[:], 1.0, -8.0, ["RB" + b], ["RH1" + b])
             mm(pc, T.EH[:], RH[:, 0, 0:w], True, False, ["EH", "RH0" + b], ["PX1"])
             mm(pc, T.EB[:], F, False, True, ["EB", "F" + b], ["PX1"])
-            mm(pd, T.BON[:], T.CBR[:, 0:w], True, False, ["BON", "CBRA", "CBR" + b], ["PD"])
 
         def ends(lo, hi):
             for i in range(lo, hi):
@@ -271,9 +272,10 @@ def rank_program(g, core, T, topo):
             g.remote_dma_fused(trs, local_sem=T.sem.loc)
 
         return {
+            "ramp": lambda: mm(pd, T.BON[:], T.CBR[:, 0:w], True, False, ["BON", "CBRA", "CBR" + b], ["PD"]),
             "flags": flags, "halves": halves, "ends": ends, "hot": hot, "cols": cols, "send": send,
-            "sums": lambda: scan(CI, T.CBM[:, 0:w], T.PCS[:, c0:c0 + w], 0.0, A.min, A.add, ["CBMA", "CBM" + b, "PCS"], ["CI" + b]),
-            "rank": lambda: tt(RM[:], CI, T.PU[:, c0:c0 + w], A.subtract, ["CI" + b, "PU"], ["RM" + b]),
+            "sums": lambda: scan(CI, T.CBM[:, 0:w], T[cs][:, 0:w], 0.0, A.min, A.add, ["CBM", cs], ["CI" + b]),
+            "rank": lambda: tt(RM[:], CI, T[cu][:, 0:w], A.subtract, ["CI" + b, cu], ["RM" + b]),
             "mask": lambda: band(RB[:], RM[:], 527, ["RM" + b], ["RB" + b]),
             "next": lambda: act(HB[:], pc, ["PX1", "hb"], ["HB" + b], func=AF.Relu, scale=BIG, bias=hb),
             "drop": lambda: tt(VL[:], pd, HB[:], A.subtract, ["PD", "HB" + b], ["VL" + b]),
@@ -281,89 +283,101 @@ def rank_program(g, core, T, topo):
             "pick": lambda: tt(X[:], MX[:].indirect(OF[:]), K[:], A.add, ["MX" + b, "OF" + b, "K" + b], ["X" + b]),
         }
 
-    def hash_(e, qs="SSS"):
+    def stage(f, e, src, dst, cut, w=180):
+        def run():
+            for lo, hi in cut:
+                a, b = 180 * e + 60 * lo, 180 * e + min(w, 60 * hi)
+                f(T[dst][:, a:b], T[src][:, a:b], ["%s%d%d" % (src, e, k) for k in range(lo, hi)],
+                  ["%s%d%d" % (dst, e, k) for k in range(lo, hi)])
+        return run
+
+    def hash_(e, cut=WHOLE):
         key = "LB" if e else "LA"
         x = T.LB[:, :, 32 * (e - 1):32 * (e - 1) + CW] if e else T.LA[:]
-        c = 180 * e
-        z1, z2, z3, h = [z[:, c:c + 180] for z in (T.Z1, T.Z2, T.Z3, T.Z4)]
 
         def first():
             for k in range(3):
-                lin(qs[k], T.Z1[:, c + 60 * k:c + 60 * k + 60], x, T.HC[:, 6 * e + k:6 * e + k + 1],
+                lin("S", T.Z1[:, 180 * e + 60 * k:180 * e + 60 * k + 60], x, T.HC[:, 6 * e + k:6 * e + k + 1],
                     T.HC[:, 6 * e + 3 + k:6 * e + 4 + k], [key, "HC"], ["Z1%d%d" % (e, k)])
 
         return [first,
-                lambda: band(z2, z1, 4095, ["Z1%d%d" % (e, k) for k in range(3)], ["Z2%d" % e]),
-                lambda: act(z3, z2, ["Z2%d" % e], ["Z3%d" % e], func=AF.Square, scale=2.0, bias=-4095.5),
-                lambda: band(h, z3, 8190, ["Z3%d" % e], ["Z4%d" % e])]
+                stage(lambda o, i, r, w: band(o, i, 4095, r, w), e, "Z1", "Z2", cut),
+                stage(lambda o, i, r, w: act(o, i, r, w, func=AF.Square, scale=2.0, bias=-4095.5), e, "Z2", "Z3", cut),
+                stage(lambda o, i, r, w: band(o, i, 8190, r, w), e, "Z3", "Z4", cut)]
 
-    def place(e):
+    def place(e, cut=WHOLE):
         if e == 0:
-            return [lambda: lin("S", T.OFF[:, 0:180], T.Z4[:, 0:180], T.NC[:, 8:9], EPS - 0.5, ["Z40", "C0"], ["OFF0"])]
+            return [stage(lambda o, i, r, w: lin("S", o, i, T.NC[:, 8:9], EPS - 0.5, r + ["C0"], w), e, "Z4", "OFF", cut)]
         w = 180 if e < NR else 128
-        c = 180 * (e - 1)
-        z5, z6, na = T.Z5[:, c:c + w], T.Z6[:, c:c + w], T.NA[:, c:c + w]
-
-        def age():
-            if e < NR:
-                lin("S", z5, T.Z4[:, 180 * e:180 * e + 180], T.NC[:, e:e + 1], T.MU[:, e:e + 1], ["Z4%d" % e, "NC", "MU"],
-                    ["Z5%d" % e])
-            else:
-                lin("S", z5, T.PLC[:], -1.0, T.MM[:, 5:6], ["PLC", "MUG"], ["Z5%d" % e])
+        na = T.NA[:, 180 * e:180 * e + w]
+        nk = ["NA%d%d" % (e, k) for k in range(3)]
+        if e < NR:
+            age = stage(lambda o, i, r, w: lin("S", o, i, T.NC[:, e:e + 1], T.MU[:, e:e + 1], r + ["NC", "MU"], w), e, "Z4", "Z5", cut)
+        else:
+            age = stage(lambda o, i, r, w: lin("S", o, T.PLC[:], -1.0, T.MM[:, 5:6], ["PLC", "MUG"], w), e, "Z5", "Z5", cut, w)
 
         def steps():
-            mm(T.PM[:, 0:w], T.IDH[:], na, True, False, ["IDH", "NA%d" % e], ["PM"])
+            mm(T.PM[:, 0:w], T.IDH[:], na, True, False, ["IDH"] + nk, ["PM"])
             for i in range(3 * e + 1):
                 o = T.TM[:, 180 * i:180 * i + w]
                 t = 16 * (e - 1) + i
-                ts(o, na, T.TH[:, t:t + 1], T.DL[:, i:i + 1], A.is_le, A.mult,
-                   ["NA%d" % e, "TH%d" % e, "DL0", "DL1", "DL2"], ["TM%d" % i])
+                ts(o, na, T.TH[:, t:t + 1], T.DL[:, i:i + 1], A.is_le, A.mult, nk + ["TH%d" % e, "DL0", "DL1", "DL2"], ["TM%d" % i])
                 mm(T.PM[:, 0:w], T.IDH[:], o, False, i == 3 * e, ["IDH", "TM%d" % i], ["PM"])
 
         return [age,
-                lambda: band(z6, z5, P - 1, ["Z5%d" % e], ["Z6%d" % e]),
-                lambda: lin("S", na, z6, -1.0, 0.0, ["Z6%d" % e], ["NA%d" % e]),
+                stage(lambda o, i, r, w: band(o, i, P - 1, r, w), e, "Z5", "Z6", cut, w),
+                stage(lambda o, i, r, w: lin("S", o, i, -1.0, 0.0, r, w), e, "Z6", "NA", cut, w),
                 steps,
-                lambda: lin("S", T.OFF[:, 180 * e:180 * e + w], T.PM[:, 0:w], 1.0, T.FB[:, e - 1:e], ["PM", "FB"], ["OFF%d" % e])]
+                stage(lambda o, i, r, x: lin("S", o, T.PM[:, 0:w], 1.0, T.FB[:, e - 1:e], ["PM", "FB"], x), e, "NA", "OFF", WHOLE, w)]
 
     def gather(q, e, j, k, part):
         lo, hi = {"": (0, CW), "a": (0, CW // 2), "b": (CW // 2, CW)}[part]
         c = 180 * e + 60 * k + CW * j
         win = T.WIN[:, 0:P + 3 * CAP * e].indirect(T.OFF[:, c + lo:c + hi])
         o = T.GG[:, CAP * (3 * j + k) + 16 * lo:CAP * (3 * j + k) + 16 * hi]
-        r = ["RINGa", "RINGb", "OFF%d" % e] + ["W%d" % i for i in range(e)]
+        r = ["RINGa", "RINGb", "OFF%d%d" % (e, k)] + ["W%d" % i for i in range(e)]
         w = ["G%d%d%s" % (j, k, h) for h in (part or "ab")]
         if q == "V":
             op("V", lambda: v.tensor_copy(o, win), r, w)
         else:
             act(o, win, r, w, func=AF.Copy)
 
-    def weigh(j):
+    def piece(j, part):
+        return ("PCS" if part == "b" else "PX%d" % j), CAP * j + (CAP // 2 if part == "b" else 0), CAP // (2 if part else 1)
+
+    def weigh(j, parts):
         for i, k in enumerate(WEIGH[j]):
-            mm(T["PX%d" % j][:, 0:CAP], T.DG[:, 128 * k:128 * k + 128], T.GG[:, CAP * (3 * j + k):CAP * (3 * j + k + 1)],
-               i == 0, i == 2, ["DG%d" % k, "G%d%da" % (j, k), "G%d%db" % (j, k)], ["PX%d" % j])
+            for part in parts or ("",):
+                bank, c, w = piece(j, part)
+                c += CAP * (2 * j + k)
+                mm(T[bank][:, 0:w], T.DG[:, 128 * k:128 * k + 128], T.GG[:, c:c + w], i == 0, i == 2,
+                   ["DG%d" % k] + ["G%d%d%s" % (j, k, h) for h in (part or "ab")], [bank])
 
-    def whole(q, j):
-        lin(q, T.KI[:, CAP * j:CAP * (j + 1)], T["PX%d" % j][:, 0:CAP], 1.0, -127.5 / 256, ["PX%d" % j], ["KI%d" % j])
+    def whole(q, j, part):
+        bank, c, w = piece(j, part)
+        lin(q, T.KI[:, c:c + w], T[bank][:, 0:w], 1.0, -127.5 / 256, [bank], ["KI%d%s" % (j, part)])
 
-    def rest(e, j):
-        o = T.OUT[:, CAP * (3 * e + j):CAP * (3 * e + j + 1)]
-        tt(o, T["PX%d" % j][:, 0:CAP], T.KI[:, CAP * j:CAP * (j + 1)], A.subtract, ["PX%d" % j, "KI%d" % j], ["O%d%d" % (e, j)])
-        r, en = peers[j][0:2]
-        rid, pid = topo.addr(T.cores[r], core)
-        c = P + CAP * (3 * e + (rank - r) % n - 1)
-        deps("G", ["O%d%d" % (e, j)], [])
-        g.remote_dma(T.WIN[:, c:c + CAP], o, T.sem["ar%d" % e], T.sem.loc, pid, rid, _bits(en))
-        sent[0] += len(en)
+    def rest(e, j, part):
+        bank, c, w = piece(j, part)
+        tt(T.OUT[:, 3 * CAP * e + c:3 * CAP * e + c + w], T[bank][:, 0:w], T.KI[:, c:c + w], A.subtract,
+           [bank, "KI%d%s" % (j, part)], ["O%d%d%s" % (e, j, part)])
+        if part != "a":
+            r, en = peers[j][0:2]
+            rid, pid = topo.addr(T.cores[r], core)
+            c = P + CAP * (3 * e + (rank - r) % n - 1)
+            deps("G", ["O%d%d%s" % (e, j, h) for h in ("", "a", "b")], [])
+            g.remote_dma(T.WIN[:, c:c + CAP], T.OUT[:, CAP * (3 * e + j):CAP * (3 * e + j + 1)], T.sem["ar%d" % e], T.sem.loc,
+                         pid, rid, _bits(en))
+            sent[0] += len(en)
 
     def round_(e, fill=None):
         for st in ROUND:
             if st[0] == "w":
-                weigh(int(st[1]))
+                weigh(int(st[1]), st[2:])
             elif st[0] == "r":
-                rest(e, int(st[1]))
+                rest(e, int(st[1]), st[2:])
             elif st[1] == "c":
-                whole(st[0], int(st[2]))
+                whole(st[0], int(st[2]), st[3:])
             else:
                 gather(st[0], e, int(st[2]), int(st[3]), st[4:])
             for f in (fill or {}).get(st, []):
@@ -380,67 +394,69 @@ def rank_program(g, core, T, topo):
     b["flags"]("S")
     a["ends"](0, 2)
     a["mask"]()
+    a["ramp"]()
     a["halves"]("V", "S")
+    b["sums"]()
     a["ends"](2, 6)
     a["next"]()
     a["hot"]()
     act(T.HC[:], T.PH[:, 0:28], ["PH"], ["HC"])
-    a["cols"]("S")
-    b["sums"]()
-    a["drop"]()
     b["rank"]()
-    a["run"]()
+    b["ends"](0, 4)
+    a["cols"]("S")
     b["mask"]()
+    b["ends"](4, 6)
+    a["drop"]()
+    b["halves"]("S", "V")
+    a["run"]()
+    cn = T.CI[:, 32:396:33]
+    scan(T.NE[:, 2:14], cn, cn, 0.0, A.min, A.subtract, ["CIA", "CIB"], ["NE2"])
+    b["ramp"]()
     a["pick"]()
     a["send"]()
     iota(T.KB[:], [[-TT, 3], [-3 * TT, 3], [0, 32]], TT * rank + 2048, 0, ["KB"])
     iota(T.PLC[:], [[16, 128]], 0, 1, ["PLC"])
 
-    lin("S", T.WIN[:, 0:P // 2], T.WIN[:, 0:P // 2], 1.0 / 256, 0.0, ["RINGa"], ["RINGa"])
-    b["halves"]("S", "V")
-    cn = T.CI[:, 32:396:33]
-    scan(T.NE[:, 2:14], cn, cn, 0.0, A.min, A.subtract, ["CIA", "CIB"], ["NE2"])
-    b["ends"](0, 18)
-    b["next"]()
-    b["hot"]()
-    lin("S", T.MM[:, 0:5], T.NE[:, 1:14:3], -1.0, had, ["NE1", "NE2", "HC"], ["MM"])
-    b["cols"]("S")
-    lin("V", T.WIN[:, P // 2:P], T.WIN[:, P // 2:P], 1.0 / 256, 0.0, ["RINGb"], ["RINGb"])
-    act(T.NC[:, 4:8], T.MM[:, 0:4], ["MM"], ["NR"], func=AF.Relu, scale=-1.0, bias=float(P))
-    lin("S", T.MUI[:, 0:4], T.MM[:, 0:4], 1.0, -1.0, ["MM"], ["MU0"])
-    lin("S", T.NC[:, 8:9], T.NC[:, 4:5], -1.0 / 8192, 0.25, ["NR"], ["C0"])
-    h0, h1, h2, h3 = hash_(0), hash_(1), hash_(2), hash_(3)
-    p1, p2, p3, p4 = place(1), place(2), place(3), place(NR)
-
-    def weight(k):
-        return lambda: lin("S", T.DG[:, 128 * k:128 * k + 128], T.IDB[:], T.HC[:, 24 + k:25 + k], 0.0, ["IDB", "HC"], ["DG%d" % k])
+    h0, h1, h2, h3 = hash_(0, THIRDS), hash_(1, THIRDS), hash_(2), hash_(3)
+    p1, p2, p3, p4 = place(1, THIRDS), place(2), place(3), place(NR)
 
     def bound(e):
         return lambda: lin("S", T.TH[:, 16 * (e - 1):16 * (e - 1) + 13], T.NE[:, 0:13], -1.0, T.NE[:, 1 + 3 * e:2 + 3 * e],
                            ["NE0", "NE1", "NE2"], ["TH%d" % e])
 
-    _mix([b["drop"], h0[0], b["run"], h0[1], weight(2), h0[2], b["pick"], b["send"], weight(0), h0[3],
-          lambda: band(T.MUI[:, 4:8], T.MUI[:, 0:4], P - 1, ["MU0"], ["MU1"]), weight(1), place(0)[0]])
-    deps("Y", ["MM"], [])
-    g.sync.dma_start(T.now[:], T.MM[0:128:16, 4:5]).then_inc(T.sem.st, 16)
+    b["ends"](6, 18)
+    b["next"]()
+    lin("S", T.MM[:, 0:5], T.NE[:, 1:14:3], -1.0, had, ["NE1", "NE2", "HC"], ["MM"])
+    lin("S", T.WIN[:, 0:P // 2], T.WIN[:, 0:P // 2], 1.0 / 256, 0.0, ["RINGa"], ["RINGa"])
+    act(T.NC[:, 4:8], T.MM[:, 0:4], ["MM"], ["NR"], func=AF.Relu, scale=-1.0, bias=float(P))
+    lin("S", T.MUI[:, 0:4], T.MM[:, 0:4], 1.0, -1.0, ["MM"], ["MU0"])
+    b["hot"]()
+    b["cols"]("S")
+    lin("S", T.NC[:, 8:9], T.NC[:, 4:5], -1.0 / 8192, 0.25, ["NR"], ["C0"])
+    lin("S", T.NC[:, 0:4], T.NC[:, 4:8], 1.0 / 8192, -0.25, ["NR"], ["NC"])
+    lin("V", T.WIN[:, P // 2:P], T.WIN[:, P // 2:P], 1.0 / 256, 0.0, ["RINGb"], ["RINGb"])
+    band(T.MUI[:, 4:8], T.MUI[:, 0:4], P - 1, ["MU0"], ["MU1"])
+    for k in range(3):
+        lin("S", T.DG[:, 128 * k:128 * k + 128], T.IDB[:], T.HC[:, 24 + k:25 + k], 0.0, ["IDB", "HC"], ["DG%d" % k])
     counts = [lambda: lin("V", T.NE[:, 0:1], T.MUI[:, 4:5], 1.0, 1.0, ["MU1"], ["NE0"]),
               lambda: lin("V", T.DL[:, 1:2], T.MUI[:, 4:5], 1.0, 1.0 - P, ["MU1"], ["DL1"]),
               lambda: lin("V", T.MU[:], T.MUI[:, 4:8], 1.0, 0.5 - EPS, ["MU1"], ["MU"]),
-              lambda: lin("V", T.NC[:, 0:4], T.NC[:, 4:8], 1.0 / 8192, -0.25, ["NR"], ["NC"]),
               lambda: lin("V", T.DL[:, 2:13], T.CI[:, 32:363:33], 1.0, -float(CAP), ["CIA", "CIB"], ["DL2"]),
               lambda: tt(T.FB[:], T.CI[:, 98:396:99], T.FC[:], A.add, ["CIA", "CIB", "FC"], ["FB"])]
-    _mix(counts[0:2])
+    _mix([h0[0], b["drop"], counts[0], counts[1], b["run"], h0[1], h0[2], h0[3], b["pick"], b["send"], place(0, THIRDS)[0]])
+    deps("Y", ["MM"], [])
+    g.sync.dma_start(T.now[:], T.MM[0:128:16, 4:5]).then_inc(T.sem.st, 16)
 
-    round_(0, {"Sg21a": h1[0:1], "Vc1": counts[2:3], "r1": h1[1:2], "Sc2": h1[2:3], "r2": h1[3:4]})
-    _mix([counts[3], p1[0], counts[4], bound(1), p1[1], h2[0], counts[5], p1[2], h2[1], p1[3], h2[2], bound(2), h2[3], p1[4]])
-    round_(1, {"Sg21a": [p2[0], bound(3)], "r1": p2[1:2], "Sc2": [p2[2], h3[0]]})
+    round_(0, {"Sc1": h1[0:1], "Vg21b": counts[2:3], "r1": h1[1:2], "Sc2b": h1[2:3], "r2b": h1[3:4]})
+    _mix([p1[0], counts[3], bound(1), p1[1], counts[4], p1[2], h2[0], p1[3], h2[1], bound(2), p1[4], h2[2]])
+    round_(1, {"Vg01": h2[3:4], "Sc1": [p2[0], bound(3)], "r1": p2[1:2], "Sc2b": [p2[2], h3[0]]})
     _mix([p2[3], h3[1], p2[4], h3[2], h3[3]])
-    round_(2, {"Sg21a": [p3[0], bound(4)], "r1": p3[1:2], "Sc2": p3[2:3]})
+    round_(2, {"Sc1": [p3[0], bound(4)], "r1": p3[1:2], "Sc2b": p3[2:3]})
     _mix([p3[3], lambda: lin("S", T.MM[:, 5:6], T.MM[:, 4:5], 1.0, g1, ["MM", "g1"], ["MUG"]), p4[0], p3[4]])
-    round_(3, {"Vc1": p4[1:2], "Sc2": p4[2:3]})
+    round_(3, {"Vg21b": p4[1:2], "Sc2b": p4[2:3]})
 
     _mix(p4[3:5])
-    r = ["RINGa", "RINGb", "OFF4"] + ["W%d" % i for i in range(NR)]
+    r = ["RINGa", "RINGb", "OFF40"] + ["W%d" % i for i in range(NR)]
     pieces = (("V", 0, 256), ("S", 256, 512), ("V", 512, 896), ("S", 896, 1280), ("V", 1280, 1664), ("S", 1664, 2048))
     for q, lo, hi in pieces:
         lin(q, T.YY[:, lo:hi], T.WIN[:].indirect(T.OFF[:, 720 + lo // 16:720 + hi // 16]), 256.0, 0.0, r, ["Y%d" % lo])

@@ -5,7 +5,7 @@ NR, P, CAP, TT = 4, 2048, 320, 512
 CW = CAP // 16
 EPS = 2.0 ** -13
 BIG = 1024.0
-BATCH = {"A": (0, 3, 0), "B": (3, 9, 128)}
+BATCH = {"A": (0, 3), "B": (3, 9)}
 F4, B2, I4, H2, U2 = "float32", "bfloat16", "int32", "float16", "uint16"
 
 
@@ -18,13 +18,14 @@ SCRATCH = {
     "CMA": _sb([3, 32], I4), "CMB": _sb([9, 32], I4), "HCI": _sb(28, I4), "HCF": _sb(28, F4), "HC": _sb(28, F4),
     "PCI": _sb(4, I4), "PCF": _sb(12, F4), "MG": _sb(128, B2), "MI": _sb(144, F4), "BON": _sb(128, B2), "UT": _sb(128, B2),
     "UU": _sb(128, B2), "WM": _sb(144, H2), "E8": _sb(128, F4), "IDB": _sb(128, B2), "IDH": _sb(128, H2), "DG": _sb(384, B2),
-    "EH": _sb(128, H2), "EB": _sb(128, B2),
-    "CBM": _sb(297, B2), "CBR": _sb(297, B2), "K2": _sb(24, F4), "KA": _sb(96, F4), "KB": _sb(288, F4), "PLC": _sb(128, F4),
-    "JK": _sb(768, B2), "ACC": _sb(24, F4), "AC2": _sb(24, F4), "LA": _sb([3, CW], U2), "LB": _sb([3, 96], U2),
-    "FZ": _sb([12, 33], B2), "CI": _sb(396, F4), "NE": _sb(14, F4), "DL": _sb(13, F4), "FC": _sb(4, F4), "FB": _sb(4, F4),
-    "MM": _sb(6, F4), "NC": _sb(9, F4), "MUI": _sb(8, I4), "MU": _sb(4, F4), "TH": _sb(64, F4),
+    "EH": _sb(128, H2), "EB": _sb(128, B2), "CJ": _sb(297, I4), "CK": _sb(297, I4),
+    "CBM": _sb(297, B2), "CBR": _sb(396, B2), "K2": _sb(24, F4), "KB": _sb(288, F4), "PLC": _sb(128, F4),
+    "JK": _sb(768, B2), "ACC": _sb(24, F4), "AC2": _sb(24, F4), "LB": _sb([3, 96], U2),
+    "HR": _sb([3, 8], F4), "CR": _sb(3, F4), "Z0": _sb([9, 32], I4), "OS": _sb(180, U2), "OL": _sb([3, 60], U2), "XB": _sb(288, U2),
+    "FZ": _sb([12, 33], B2), "CI": _sb(396, F4), "NE": _sb(14, F4), "DL": _sb(13, F4), "FC": _sb(4, F4), "FE": _sb(4, F4),
+    "MM": _sb(6, F4), "NC": _sb(8, F4), "MUI": _sb(8, I4), "MU": _sb(4, F4), "TH": _sb(64, F4),
     "Z1": _sb(720, I4), "Z2": _sb(720, I4), "Z3": _sb(720, I4), "Z4": _sb(720, I4),
-    "Z5": _sb(900, I4), "Z6": _sb(900, I4), "NA": _sb(900, H2), "TM": _sb(13 * 180, H2), "OFF": _sb(900, U2),
+    "Z5": _sb(900, I4), "Z6": _sb(900, I4), "NA": _sb(900, H2), "TM": _sb(34 * 180, H2), "OFF": _sb(900, U2),
 }
 PSUM = ("PCS", "PU", "PD", "PX0", "PX1", "PX2", "PM", "PH")
 for _n in PSUM:
@@ -36,13 +37,23 @@ for _n in BATCH:
     SCRATCH["RH" + _n] = _sb([2, _w + 1], H2)
     SCRATCH["OH" + _n] = _sb([16, _w + 1], H2)
     SCRATCH["OF" + _n] = _sb(2 * BATCH[_n][1], U2)
-    SCRATCH["X" + _n] = _sb(32 * BATCH[_n][1], U2)
 
-SEMAPHORES = ["sV", "sS", "sP", "sG", "ldA", "ldB", "ldH", "ldR", "st", "loc", "arA", "arB", "ar0", "ar1", "ar2", "ar3"]
+SEMAPHORES = ["sV", "sS", "sP", "sG", "ldA", "ldB", "ldH", "ldR", "st", "loc", "arH", "arA", "arB", "ar0", "ar1", "ar2", "ar3"]
 
-ROUND = ("Vg00 Sg02 Vg01 Sg10 w0 Vg12 Sg11 w1 Vg22 Sc0 Sg20 r0 Vg21a Sc1 Vg21b w2ab r1 Sc2a Sc2b r2a r2b").split()
-WHOLE, THIRDS = ((0, 3),), ((0, 1), (1, 2), (2, 3))
-WEIGH = ((0, 2, 1), (0, 2, 1), (2, 0, 1))
+ROUND = ("Vg00a Vg02a Vg02b Sg01 Sg10 Vg00b Sg11a Sc0a Vg12a Vg12b Sg11b Vr0a Gw0a Vg22a Sc0b Sc1a Sg21 Sg20a Vr0b Gw0b Vc1b "
+         "Sg20b Sc2a Vr1a Gw1a Vr1b Gw1b Vg22b Sc2b Vr2a Gw2a Vr2b Gw2b").split()
+WHOLE, TWO, THIRDS = ((0, 3),), ((0, 1), (1, 3)), ((0, 1), (1, 2), (2, 3))
+CUTS = (THIRDS, TWO, WHOLE, WHOLE, WHOLE)
+
+CYC, HOP, SLACK, SPARE, PASSES = 0.00083, 0.15, 0.1, 0.1, 4
+FIX = {"V": 0.03, "S": 0.05, "P": 0.04, "G": 0.15, "Y": 0.05}
+PE, GATHER = 0.65, 1.56
+ISSUE, FIRST, LAND, FAR, NEAR, STORE = 0.2, 2.6, 1.0, 0.9, 0.2, 1.2
+LISTS = {"HR": 1.6, "OL": 1.6, "LB": 1.6}
+LOADED = {"CMA": 1.7, "HCI": 1.6, "CMB": 2.0, "RING0": 3.2, "RING1": 3.2, "RING2": 3.2, "RING3": 3.2, "later": 3.0}
+
+
+ORDER = []
 
 
 def _bits(engs):
@@ -61,23 +72,94 @@ def _peers(T, topo, q):
     near = [r for r in others if T.cores[r] in topo.cores_of(me)]
     res = []
     used = set()
-    k = 1
     for i, r in enumerate(far):
         en = topo.engines(me, T.cores[r])
         used |= set(en)
         k = len(en) // len(far)
-        res.append((r, en, en[i * k:(i + 1) * k], en[i * k:(i + 1) * k]))
+        res.append((r, en, en[i * k:(i + 1) * k]))
     for r in near:
-        en = [x for x in topo.engines(me, T.cores[r]) if x not in used]
-        res.append((r, topo.engines(me, T.cores[r]), en[:k], en))
+        en = topo.engines(me, T.cores[r])
+        res.append((r, en, [x for x in en if x not in used]))
     return res
 
 
-def _mix(*chains):
-    for i in range(max(len(c) for c in chains)):
-        for c in chains:
-            if i < len(c):
-                c[i]()
+def _order(calls):
+    pre = [set() for c in calls]
+    writers, readers = {}, {}
+    for i, c in enumerate(calls):
+        for k in c["r"]:
+            pre[i].update(writers.get(k, []))
+        for k in c["w"]:
+            ws = writers.get(k, [])
+            if c["sum"] is not None and ws and calls[ws[0]]["sum"] == c["sum"]:
+                pre[i].update(calls[ws[0]]["after"])
+                ws.append(i)
+            else:
+                c["after"] = set(ws) | set(readers.get(k, []))
+                pre[i].update(c["after"])
+                writers[k], readers[k] = [i], []
+        for k in c["r"]:
+            if k not in c["w"]:
+                readers.setdefault(k, []).append(i)
+        pre[i].discard(i)
+        c["soft"] = c.get("follows") if c.get("follows") not in pre[i] else None
+        if c["soft"] is not None:
+            pre[i].add(c["soft"])
+    post = [[] for c in calls]
+    for i in range(len(calls)):
+        for j in pre[i]:
+            post[j].append(i)
+
+    def run(pre, post, chain, back):
+        free = {q: 0.0 for q in "VSPGYLN"}
+        end, bank, res = {}, {}, []
+        left = [len(p) for p in pre]
+        ready = {}
+
+        def arrive(i):
+            c = calls[i]
+            lag = c["late"] if back else 0.0
+            ready[i] = max([lag] + [0.0 if back else LOADED.get(k, 0.0) for k in c["r"]]
+                           + [end[j][0] + lag + (0.0 if end[j][1] == "P" and "P" in c["t"] or c["soft"] == j
+                                                 or calls[j]["soft"] == i else HOP) for j in pre[i]])
+
+        for i in range(len(calls)):
+            if not left[i]:
+                arrive(i)
+        while ready:
+            best = []
+            for i in ready:
+                c = calls[i]
+                opts = []
+                for q in c["t"]:
+                    t = max([free[q], ready[i]] + [bank[k][0] + HOP for k in c["bank"] if k in bank and bank[k][1] != q])
+                    opts.append((t + c["t"][q] + (SPARE if q == "V" else 0.0), t, q))
+                best.append(min(opts)[1:] + (i,))
+            soon, q, _ = min(best)
+            t, q, i = max((b for b in best if b[0] <= soon + SLACK and b[1] == q), key=lambda b: (chain[b[2]], -b[2]))
+            c = calls[i]
+            free[q] = t + c["t"][q]
+            end[i] = (free[q] + (0.0 if back else c["late"]), q)
+            for k in c["bank"]:
+                bank[k] = (free[q], q)
+            res.append((i, q))
+            del ready[i]
+            for j in post[i]:
+                left[j] -= 1
+                if not left[j]:
+                    arrive(j)
+        return res, [end[i][0] for i in range(len(calls))]
+
+    chain = [0.0] * len(calls)
+    for i in reversed(range(len(calls))):
+        chain[i] = min(calls[i]["t"].values()) + calls[i]["late"] + max([HOP + chain[j] for j in post[i]] + [0.0])
+    best = None
+    for _ in range(PASSES):
+        res, end = run(pre, post, chain, False)
+        if best is None or max(end) < best[0]:
+            best = (max(end), res)
+        chain = run(post, pre, end, True)[1]
+    return best[1]
 
 
 def rank_program(g, core, T, topo):
@@ -85,386 +167,358 @@ def rank_program(g, core, T, topo):
     if rank is None:
         return
     n = len(T.cores)
-    Q = {"V": g.vector, "S": g.scalar, "P": g.tensor, "G": g, "Y": g.sync}
-    cnt = {"V": 0, "S": 0, "P": 0, "G": 0}
-    waited = {q: {} for q in Q}
-    wr, rd, pend = {}, {}, []
-
-    def wait(q, tok):
-        if waited[q].get(tok[0], 0) < tok[1]:
-            Q[q].wait_ge(T.sem[tok[0]], tok[1])
-            waited[q][tok[0]] = tok[1]
-
-    def deps(q, r, w):
-        need = {}
-        for k in r:
-            toks = [wr[k]] if k in wr else []
-            if k in PSUM:
-                toks += [t for t in rd.get(k, []) if t[0] != "s" + q]
-            for t in toks:
-                need[t[0]] = max(need.get(t[0], 0), t[1])
-        for k in w:
-            for t in ([wr[k]] if k in wr else []) + rd.get(k, []):
-                if not (q == "P" and t[0] == "sP"):
-                    need[t[0]] = max(need.get(t[0], 0), t[1])
-        for s in need:
-            wait(q, (s, need[s]))
-
-    def op(q, f, r, w, last=True):
-        deps(q, r, w)
-        ins = f()
-        if not last:
-            pend.extend(r)
-            return
-        cnt[q] += 1
-        ins.then_inc(T.sem["s" + q], 1)
-        if q == "P":
-            r = list(r) + pend
-            del pend[:]
-        for k in r:
-            rd.setdefault(k, []).append(("s" + q, cnt[q]))
-        for k in w:
-            wr[k] = ("s" + q, cnt[q])
-            rd[k] = []
-
     v, s, pe = g.vector, g.scalar, g.tensor
+    calls = []
 
-    def ts(out, i, a, b, o0, o1, r, w):
-        if o1 is None:
-            op("V", lambda: v.tensor_scalar(out, i, a, None, o0), r, w)
-        else:
-            op("V", lambda: v.tensor_scalar(out, i, a, b, o0, o1), r, w)
+    def size(ap):
+        m = 1
+        for d in ap.shape[1:]:
+            m *= d
+        return m
 
-    def tt(out, a, b, o, r, w):
-        op("V", lambda: v.tensor_tensor(out, a, b, o), r, w)
+    def call(f, t, r, w, kind="compute", late=0.0, group=None):
+        calls.append({"f": f, "t": t, "r": list(r), "w": list(w), "kind": kind, "late": late, "sum": group,
+                      "bank": [k for k in r if k in PSUM]})
 
-    def act(out, i, r, w, func=AF.Identity, **kw):
-        op("S", lambda: s.activation(out, i, func, **kw), r, w)
+    def cost(q, out, rate):
+        return FIX[q] + CYC * (size(out) * rate if rate == GATHER else max(64, size(out) * rate))
 
-    def lin(q, out, i, a, b, r, w):
-        if q == "V":
-            ts(out, i, a, b, A.mult, A.add, r, w)
-        else:
-            act(out, i, r, w, scale=a, bias=b)
+    def ts(out, i, a, b, o0, o1, r, w, rate=1.0):
+        args = (out, i, a, None, o0) if o1 is None else (out, i, a, b, o0, o1)
+        call(lambda q: v.tensor_scalar(*args), {"V": cost("V", out, rate)}, r, w)
+
+    def tt(out, a, b, o, r, w, rate=1.0):
+        call(lambda q: v.tensor_tensor(out, a, b, o), {"V": cost("V", out, rate)}, r, w)
+
+    def act(out, i, r, w, func, **kw):
+        call(lambda q: s.activation(out, i, func, **kw), {"S": cost("S", out, 1.0)}, r, w)
+
+    def lin(out, i, a, b, r, w, rate=1.0, qs="VS"):
+        def f(q):
+            if q == "V":
+                return v.tensor_scalar(out, i, a, b, A.mult, A.add)
+            return s.activation(out, i, AF.Identity, scale=a, bias=b)
+        call(f, {q: cost(q, out, rate if q == "V" else max(rate, 1.0)) for q in qs}, r, w)
 
     def band(out, i, m, r, w):
         ts(out, i, m, None, A.bitwise_and, None, r, w)
 
     def scan(out, a, b, first, o0, o1, r, w):
-        op("V", lambda: v.tensor_tensor_scan(out, a, b, first, o0, o1), r, w)
+        call(lambda q: v.tensor_tensor_scan(out, a, b, first, o0, o1), {"V": cost("V", out, 1.0)}, r, w)
 
-    def mm(out, l, rh, st, sp, r, w):
-        op("P", lambda: pe.matmul(out, l, rh, st, sp), r, w, last=sp)
+    def fill(out, x, w, rate=1.0):
+        call(lambda q: v.memset(out, x), {"V": cost("V", out, rate)}, [], w)
 
-    def iota(out, pat, base, cm, w):
-        op("G", lambda: g.iota(out, pat, base, cm, allow_small_or_imprecise_dtypes=True), [], w)
+    sums = {}
+
+    def mm(out, l, rh, name, r, bank, rate=PE):
+        c = sums.setdefault(name, [0, 0])
+        c[0] += 1
+
+        def f(q):
+            c[1] += 1
+            return pe.matmul(out, l, rh, c[1] == 1, c[1] == c[0])
+        call(f, {"P": FIX["P"] + CYC * rate * max(64, size(out))}, r, [bank], group=name)
+
+    def iota(out, pat, base, cm, w, r=()):
+        call(lambda q: g.iota(out, pat, base, cm, allow_small_or_imprecise_dtypes=True), {"G": cost("G", out, 2.0)}, r, w)
 
     peers = _peers(T, topo, rank)
-    got = [0, 0, 0]
+    got = [0, 0]
     slot = {}
+
+    def engines(prs, j, part):
+        return prs[j][2 if j == len(prs) - 1 and part == "a" else 1]
+
     for q in range(n):
         if q != rank:
-            for j, pr in enumerate(_peers(T, topo, q)):
+            prs = _peers(T, topo, q)
+            for j, pr in enumerate(prs):
                 if pr[0] == rank:
-                    got = [a + len(b) for a, b in zip(got, pr[1:])]
+                    got = [got[0] + sum(len(engines(prs, j, h)) for h in [st[3:] for st in ROUND if st[0:3] == "Gw%d" % j]), got[1] + len(pr[2])]
                     slot[q] = j
-    wr["LA"], wr["LB"] = ("arA", got[1]), ("arB", got[2])
+    wr = {"HR": ("arH", got[1]), "OL": ("arA", got[1]), "LB": ("arB", got[1])}
     for e in range(NR):
         wr["W%d" % e] = ("ar%d" % e, got[0])
     sent = [0]
 
+    def to_all(sem, key, r, src, dst, t=ISSUE):
+        trs = []
+        for q, _, el in peers:
+            rid, pid = topo.addr(T.cores[q], core)
+            trs.append(RemoteDMATransfer(dst_ids=[DstId(rid=rid, pnc=pid)], dma_engine_mask=_bits(el), remote_sem=T.sem[sem],
+                                         src=src(q), dst=dst(q)))
+            sent[0] += len(el)
+        call(lambda q: g.remote_dma_fused(trs, local_sem=T.sem.loc), {"G": t}, r, [key], "remote", LISTS[key] - HOP)
+
+    def store(out, i, r):
+        call(lambda q: g.sync.dma_start(out, i).then_inc(T.sem.st, 16), {"Y": FIX["Y"]}, r, [], "store", STORE)
+
     g.sync.dma_start(T.CMA[:], T.came[:, 0:96]).then_inc(T.sem.ldA, 16)
-    s.dma_start(T.HCI[0:8, 0:27], T.hc[:]).then_inc(T.sem.ldH, 16)
-    s.dma_start(T.HCI[0:8, 27:28], T.had[:]).then_inc(T.sem.ldH, 16)
+    s.dma_start(T.HCI[0:8, 1:28], T.hc[:]).then_inc(T.sem.ldH, 16)
+    s.dma_start(T.HCI[0:8, 0:1], T.had[:]).then_inc(T.sem.ldH, 16)
     g.sync.dma_start(T.CMB[:], T.came[:, 96:384]).then_inc(T.sem.ldB, 16)
     g.sync.dma_start(T.WIN[:, 0:P], T.ring[:]).then_inc(T.sem.ldR, 16)
     wr["CMA"], wr["CMB"], wr["HCI"] = ("ldA", 16), ("ldB", 16), ("ldH", 32)
-    wr["RINGa"] = wr["RINGb"] = ("ldR", 16)
+    RING = ["RING%d" % i for i in range(4)]
+    for key in RING:
+        wr[key] = ("ldR", 16)
 
-    op("G", lambda: g.iota(T.PCI[:, 0:1], [[0, 1]], 0, 1), [], ["p"])
+    iota(T.PCI[:, 0:1], [[0, 1]], 0, 1, ["p"])
     iota(T.MG[:], [[16, 8], [0, 16]], 0, 0, ["MG"])
     iota(T.MI[:], [[1, 144]], 0, 0, ["MI"])
-    op("V", lambda: v.memset(T.FZ[:, :, 32:33], 0.0), [], ["FA", "FB"])
-    op("V", lambda: v.memset(T.PD[:, 0:129:128], -BIG), [], ["PD"])
+    fill(T.FZ[:, :, 32:33], 0.0, ["FA", "FB"])
+    fill(T.PD[:, 0:1], -BIG, ["PD"])
+    fill(T.PM[:, 0:1], -BIG, ["PM"])
+    fill(T.CBM[:], float(TT), ["CBM"], 0.5)
+    fill(T.CBM[:, 0:297:33], 0.0, ["CBM"])
+    fill(T.NE[:, 1:2], 0.0, ["NE1"])
+    fill(T.DL[:, 0:1], float(P), ["DL0"])
     pf, gf, bf, g15, bB, th0, th1, p15, hb, g1 = [T.PCF[:, i:i + 1] for i in range(10)]
     band(T.PCI[:, 1:2], T.PCI[:, 0:1], 112, ["p"], ["gi"])
     band(T.PCI[:, 2:3], T.PCI[:, 0:1], 15, ["p"], ["bi"])
-    op("V", lambda: v.memset(T.CBM[:], float(TT)), [], ["CBM"])
-    lin("V", T.PCF[:, 0:3], T.PCI[:, 0:3], 1.0, 0.0, ["p", "gi", "bi"], ["pf"])
-    op("V", lambda: v.memset(T.CBM[:, 0:297:33], 0.0), [], ["CBM"])
-    ts(T.BON[:], T.MG[:], gf, None, A.is_equal, None, ["MG", "pf"], ["BON"])
-    op("G", lambda: g.affine_select(T.UT[:], T.BON[:], [[-1, 128]], A.is_gt, 0.0, 0, 1), ["BON"], ["UT"])
-    op("G", lambda: g.affine_select(T.UU[:], T.UT[:], [[-1, 128]], A.not_equal, -512.0, 0, 1), ["UT"], ["UU"])
-    iota(T.CBR[:, 0:99], [[32, 3], [1, 33]], -64, 0, ["CBRA"])
+    lin(T.PCF[:, 0:3], T.PCI[:, 0:3], 1.0, 0.0, ["p", "gi", "bi"], ["pf"])
+    ts(T.BON[:], T.MG[:], gf, None, A.is_equal, None, ["MG", "pf"], ["BON"], 0.5)
+    call(lambda q: g.affine_select(T.UT[:], T.BON[:], [[-1, 128]], A.is_gt, 0.0, 0, 1), {"G": cost("G", T.UT, 2.0)}, ["BON"], ["UT"])
+    call(lambda q: g.affine_select(T.UU[:], T.UT[:], [[-1, 128]], A.not_equal, -512.0, 0, 1), {"G": cost("G", T.UU, 2.0)},
+         ["UT"], ["UU"])
+    iota(T.CBR[:, 0:99], [[0, 3], [1, 33]], (TT * rank + 2048 - int(BIG)) // 16, 0, ["CBRA"])
     iota(T.K2[:, 0:6], [[66, 3], [0, 2]], 32, 0, ["K2A"])
-    iota(T.KA[:], [[-TT, 3], [0, 32]], TT * rank + 2048, 0, ["KA"])
-    iota(T.CBR[:, 99:297], [[32, 6], [1, 33]], 32, 0, ["CBRB"])
-    iota(T.K2[:, 6:24], [[66, 3], [198, 3], [0, 2]], 32, 0, ["K2B"])
-    iota(T.FC[:], [[3 * CAP, 4]], P - 1 + 2 * CAP, 0, ["FC"])
+    iota(T.CBR[:, 99:396], [[32, 9], [1, 33]], -64, 0, ["CBRB"], ["later"])
+    iota(T.K2[:, 6:24], [[66, 3], [198, 3], [0, 2]], 32, 0, ["K2B"], ["later"])
+    iota(T.KB[:], [[-TT, 3], [-3 * TT, 3], [0, 32]], TT * rank + 2048, 0, ["KB"], ["later"])
+    iota(T.FC[:], [[3 * CAP, 4]], P - 1 + 2 * CAP, 0, ["FC"], ["later"])
+    iota(T.PLC[:], [[16, 128]], 0, 1, ["PLC"], ["later"])
     for out, i, a, b, key in ((g15, gf, 1.0, 15.0, "g15"), (bB, bf, 1.0, BIG, "bB"), (p15, pf, 1.0, -15.0, "p15"),
                               (th0, bf, 16.0, 15.5, "th0"), (th1, bf, 16.0, 271.5, "th1"), (hb, bf, -BIG, 0.0, "hb"),
                               (g1, gf, 1.0, -1.0, "g1")):
-        lin("S", out, i, a, b, ["pf"], [key])
-    op("V", lambda: v.memset(T.NE[:, 1:2], 0.0), [], ["NE1"])
-    op("V", lambda: v.memset(T.DL[:, 0:1], float(P)), [], ["DL0"])
+        lin(out, i, a, b, ["pf"], [key], qs="S")
     ts(T.E8[0:8, :], T.MG[0:8, :], 1.0 / 16, T.PCF[0:8, 0:1], A.mult, A.is_equal, ["MG", "pf"], ["E8"])
     ts(T.WM[:], T.MI[:], g15, bB, A.is_equal, A.mult, ["MI", "g15", "bB"], ["WM"])
     ts(T.IDB[:], T.MI[:, 0:128], pf, None, A.is_equal, None, ["MI", "pf"], ["IDB"])
-    ts(T.EH[:], T.MG[:], p15, None, A.is_equal, None, ["MG", "p15"], ["EH"])
-    ts(T.EB[:], T.MG[:], p15, -512.0, A.is_equal, A.mult, ["MG", "p15"], ["EB"])
-    lin("S", T.IDH[:], T.IDB[:], 1.0, 0.0, ["IDB"], ["IDH"])
+    ts(T.EH[:], T.MG[:], p15, None, A.is_equal, None, ["MG", "p15"], ["EH"], 0.5)
+    ts(T.EB[:], T.MG[:], p15, -512.0, A.is_equal, A.mult, ["MG", "p15"], ["EB"], 0.5)
+    lin(T.IDH[:], T.IDB[:], 1.0, 0.0, ["IDB"], ["IDH"], 0.5)
+
+    lin(T.HCF[0:8, :], T.HCI[0:8, :], 1.0, 0.0, ["HCI"], ["HCF"])
+    mm(T.PH[:, 0:28], T.E8[0:8, :], T.HCF[0:8, :], "hc", ["E8", "HCF"], "PH", 4 * PE)
+    lin(T.HC[:], T.PH[:, 0:28], 1.0, 0.0, ["PH"], ["HC"])
+    to_all("arH", "HR", ["HC"], lambda q: T.HC[:, 0:8], lambda q: T.HR[:, (rank - q) % n - 1, :], ISSUE + FIRST)
+    for k in range(3):
+        lin(T.DG[:, 128 * k:128 * k + 128], T.IDB[:], T.HC[:, 25 + k:26 + k], 0.0, ["IDB", "HC"], ["DG%d" % k], 0.5)
+    for i in range(4):
+        c = T.WIN[:, i * P // 4:(i + 1) * P // 4]
+        lin(c, c, 1.0 / 256, 0.0, RING[i:i + 1], RING[i:i + 1], 0.5)
 
     def lists(b):
-        s0, ns, c0 = BATCH[b]
+        s0, ns = BATCH[b]
         w = 33 * ns
         F = T.FZ[:, s0:s0 + ns, :]
         CI = T.CI[:, 33 * s0:33 * s0 + w]
         RM, RB, RH, OH, HB, VL, MX = [T[x + b] for x in ("RM", "RB", "RH", "OH", "HB", "VL", "MX")]
-        a0 = 2 * s0
-        OF, X, K = T["OF" + b], T["X" + b], T["K" + b]
-        ne = ns // 3
-        cs, cu = ("PCS", "PU") if b == "A" else ("PX0", "PX2")
-        pd, pc = T.PD[:, c0 + 1:c0 + 1 + w], T.PX1[:, c0:c0 + w]
+        a0, ne = 2 * s0, ns // 3
+        cs, cu, cd = ("PCS", "PU", "PD") if b == "A" else ("PX0", "PX2", "PM")
+        pd, pc = T[cd][:, 1:1 + w], T.PX1[:, 0:w]
+        lin(T.FZ[:, s0:s0 + ns, 0:32], T["CM" + b][:], 1.0, 0.0, ["CM" + b], ["F" + b])
+        mm(T[cs][:, 0:w], T.BON[:], F, "cs" + b, ["BON", "F" + b], cs)
+        mm(T[cu][:, 0:w], T.UU[:], F, "cu" + b, ["UU", "F" + b], cu)
+        scan(CI, T.CBM[:, 0:w], T[cs][:, 0:w], 0.0, A.min, A.add, ["CBM", cs], ["CI" + b])
+        tt(RM[:], CI, T[cu][:, 0:w], A.subtract, ["CI" + b, cu], ["RM" + b])
+        band(RB[:], RM[:], 527, ["RM" + b], ["RB" + b])
+        lin(RH[:, 0, 0:w], RB[:], 1.0, 0.0, ["RB" + b], ["RH0" + b])
+        lin(RH[:, 1, 0:w], RB[:], 1.0, -8.0, ["RB" + b], ["RH1" + b])
+        if b == "A":
+            mm(pc, T.EH[:], RH[:, 0, 0:w], "pc", ["EH", "RH0" + b], "PX1")
+            mm(pc, T.EB[:], F, "pc", ["EB", "F" + b], "PX1")
+            act(HB[:], pc, ["PX1", "hb"], ["HB" + b], AF.Relu, scale=BIG, bias=hb)
+        else:
+            lin(T.CJ[:], CI, 1.0, 0.0, ["CI" + b], ["CJ"])
+            band(T.CK[:], T.CJ[:], 15, ["CJ"], ["CK"])
+            act(HB[:], T.CK[:], ["CK", "hb"], ["HB" + b], AF.Relu, scale=BIG, bias=hb)
+        for i in range(2 * ns):
+            h = i % 2
+            sl = s0 + 3 * ((i // 2) % ne) + i // (2 * ne)
+            act(T.JK[:, 32 * (a0 + i):32 * (a0 + i + 1)], T.CI[:, 33 * sl:33 * sl + 32], ["CI" + b, "th%d" % h],
+                ["ACC%d" % (a0 + i)], AF.Sign, scale=-1.0, bias=(th0, th1)[h], accum_out=T.ACC[:, a0 + i:a0 + i + 1])
+        tt(T.AC2[:, a0:a0 + 2 * ns], T.ACC[:, a0:a0 + 2 * ns], T.K2[:, a0:a0 + 2 * ns], A.add,
+           ["ACC%d" % (a0 + i) for i in range(2 * ns)] + ["K2" + b], ["AC2" + b])
+        lin(T["OF" + b][:], T.AC2[:, a0:a0 + 2 * ns], 0.5, 0.0, ["AC2" + b], ["OF" + b])
+        mm(pd, T.BON[:], T.CBR[:, 33 * s0:33 * s0 + w], "pd" + b, ["BON", "CBR" + b], cd)
+        for j in range(8):
+            ts(OH[:, j:16:8, 0:w], RH[:, :, 0:w], float(512 + j), None, A.is_equal, None, ["RH0" + b, "RH1" + b],
+               ["OH%s%d" % (b, j)], 0.5)
+            for m in (j, j + 8):
+                k = (m - 1) % 16
+                mm(pd, T.WM[:, 15 - k:143 - k], OH[:, m, 0:w], "pd" + b, ["WM", "OH%s%d" % (b, j)], cd)
+        tt(VL[:], pd, HB[:], A.subtract, [cd, "HB" + b], ["VL" + b])
+        for lo, hi in (THIRDS if b == "A" else ((0, ns),)):
+            scan(MX[:, 33 * lo:33 * hi], T[cd][:, 33 * lo:33 * hi], VL[:, 33 * lo:33 * hi], -BIG, A.max, A.max,
+                 [cd, "VL" + b], ["MX%s%d" % (b, lo)])
 
-        def flags(q):
-            lin(q, T.FZ[:, s0:s0 + ns, 0:32], T["CM" + b][:], 1.0, 0.0, ["CM" + b], ["F" + b])
-            mm(T[cs][:, 0:w], T.BON[:], F, True, True, ["BON", "F" + b], [cs])
-            mm(T[cu][:, 0:w], T.UU[:], F, True, True, ["UU", "F" + b], [cu])
+    def stage(f, e, src, dst, w=180):
+        for lo, hi in CUTS[e]:
+            a, b = 180 * e + 60 * lo, 180 * e + min(w, 60 * hi)
+            f(T[dst][:, a:b], T[src][:, a:b], ["%s%d%d" % (src, e, k) for k in range(lo, hi)],
+              ["%s%d%d" % (dst, e, k) for k in range(lo, hi)])
 
-        def halves(q0, q1):
-            lin(q0, RH[:, 0, 0:w], RB[:], 1.0, 0.0, ["RB" + b], ["RH0" + b])
-            lin(q1, RH[:, 1, 0:w], RB[:], 1.0, -8.0, ["RB" + b], ["RH1" + b])
-            mm(pc, T.EH[:], RH[:, 0, 0:w], True, False, ["EH", "RH0" + b], ["PX1"])
-            mm(pc, T.EB[:], F, False, True, ["EB", "F" + b], ["PX1"])
-
-        def ends(lo, hi):
-            for i in range(lo, hi):
-                h = i % 2
-                sl = s0 + 3 * ((i // 2) % ne) + i // (2 * ne)
-                act(T.JK[:, 32 * (a0 + i):32 * (a0 + i + 1)], T.CI[:, 33 * sl:33 * sl + 32], ["CI" + b, "th%d" % h],
-                    ["ACC%d" % (a0 + i)], func=AF.Sign, scale=-1.0, bias=(th0, th1)[h], accum_out=T.ACC[:, a0 + i:a0 + i + 1])
-
-        def hot(lo=0, hi=8):
-            for j in range(lo, hi):
-                ts(OH[:, j:16:8, 0:w], RH[:, :, 0:w], float(512 + j), None, A.is_equal, None, ["RH0" + b, "RH1" + b],
-                   ["OH%s%d" % (b, j)])
-                for m in (j, j + 8):
-                    k = (m - 1) % 16
-                    mm(pd, T.WM[:, 15 - k:143 - k], OH[:, m, 0:w], False, m == 15, ["WM", "OH%s%d" % (b, j)], ["PD"])
-
-        def cols(q):
-            tt(T.AC2[:, a0:a0 + 2 * ns], T.ACC[:, a0:a0 + 2 * ns], T.K2[:, a0:a0 + 2 * ns], A.add,
-               ["ACC%d" % (a0 + i) for i in range(2 * ns)] + ["K2" + b], ["AC2" + b])
-            lin(q, OF[:], T.AC2[:, a0:a0 + 2 * ns], 0.5, 0.0, ["AC2" + b], ["OF" + b])
-
-        def send():
-            deps("G", ["X" + b], [])
-            trs = []
-            wid = 32 * (ne - 1) + CW
-            for pr in peers:
-                q = pr[0]
-                el = pr[2] if b == "A" else pr[3]
-                c = 32 * ne * ((q - rank) % n - 1)
-                rid, pid = topo.addr(T.cores[q], core)
-                trs.append(RemoteDMATransfer(dst_ids=[DstId(rid=rid, pnc=pid)], dma_engine_mask=_bits(el),
-                                             remote_sem=T.sem["ar" + b], src=X[:, c:c + wid], dst=T["L" + b][:, slot[q], 0:wid]))
-                sent[0] += len(el)
-            g.remote_dma_fused(trs, local_sem=T.sem.loc)
-
-        return {
-            "ramp": lambda: mm(pd, T.BON[:], T.CBR[:, 0:w], True, False, ["BON", "CBRA", "CBR" + b], ["PD"]),
-            "flags": flags, "halves": halves, "ends": ends, "hot": hot, "cols": cols, "send": send,
-            "sums": lambda: scan(CI, T.CBM[:, 0:w], T[cs][:, 0:w], 0.0, A.min, A.add, ["CBM", cs], ["CI" + b]),
-            "rank": lambda: tt(RM[:], CI, T[cu][:, 0:w], A.subtract, ["CI" + b, cu], ["RM" + b]),
-            "mask": lambda: band(RB[:], RM[:], 527, ["RM" + b], ["RB" + b]),
-            "next": lambda: act(HB[:], pc, ["PX1", "hb"], ["HB" + b], func=AF.Relu, scale=BIG, bias=hb),
-            "drop": lambda: tt(VL[:], pd, HB[:], A.subtract, ["PD", "HB" + b], ["VL" + b]),
-            "run": lambda: scan(MX[:], T.PD[:, c0:c0 + w], VL[:], -BIG, A.max, A.max, ["PD", "VL" + b], ["MX" + b]),
-            "pick": lambda: tt(X[:], MX[:].indirect(OF[:]), K[:], A.add, ["MX" + b, "OF" + b, "K" + b], ["X" + b]),
-        }
-
-    def stage(f, e, src, dst, cut, w=180):
-        def run():
-            for lo, hi in cut:
-                a, b = 180 * e + 60 * lo, 180 * e + min(w, 60 * hi)
-                f(T[dst][:, a:b], T[src][:, a:b], ["%s%d%d" % (src, e, k) for k in range(lo, hi)],
-                  ["%s%d%d" % (dst, e, k) for k in range(lo, hi)])
-        return run
-
-    def hash_(e, cut=WHOLE):
-        key = "LB" if e else "LA"
-        x = T.LB[:, :, 32 * (e - 1):32 * (e - 1) + CW] if e else T.LA[:]
-
-        def first():
-            for k in range(3):
-                lin("S", T.Z1[:, 180 * e + 60 * k:180 * e + 60 * k + 60], x, T.HC[:, 6 * e + k:6 * e + k + 1],
-                    T.HC[:, 6 * e + 3 + k:6 * e + 4 + k], [key, "HC"], ["Z1%d%d" % (e, k)])
-
-        return [first,
-                stage(lambda o, i, r, w: band(o, i, 4095, r, w), e, "Z1", "Z2", cut),
-                stage(lambda o, i, r, w: act(o, i, r, w, func=AF.Square, scale=2.0, bias=-4095.5), e, "Z2", "Z3", cut),
-                stage(lambda o, i, r, w: band(o, i, 8190, r, w), e, "Z3", "Z4", cut)]
-
-    def place(e, cut=WHOLE):
+    def hash_(e):
         if e == 0:
-            return [stage(lambda o, i, r, w: lin("S", o, i, T.NC[:, 8:9], EPS - 0.5, r + ["C0"], w), e, "Z4", "OFF", cut)]
+            for j in range(3):
+                for k in range(3):
+                    lin(T.Z0[:, 3 * j + k, :], T.MXA[:].indirect(T.OFA[:, 2 * j:2 * j + 2]), T.HR[:, j, 1 + k:2 + k],
+                        T.HR[:, j, 4 + k:5 + k], ["MXA0", "MXA1", "MXA2", "OFA", "HR"], ["Z0%d%d" % (j, k)], GATHER)
+                band(T.Z2[:, 60 * j:60 * j + 60], T.Z0[:, 3 * j:3 * j + 3, 0:CW], 4095, ["Z0%d%d" % (j, k) for k in range(3)],
+                     ["Z20%d" % j])
+        else:
+            for k in range(3):
+                lin(T.Z1[:, 180 * e + 60 * k:180 * e + 60 * k + 60], T.LB[:, :, 32 * (e - 1):32 * (e - 1) + CW],
+                    T.HC[:, 6 * e + 1 + k:6 * e + 2 + k], T.HC[:, 6 * e + 4 + k:6 * e + 5 + k], ["LB", "HC"], ["Z1%d%d" % (e, k)])
+            stage(lambda o, i, r, w: band(o, i, 4095, r, w), e, "Z1", "Z2")
+        stage(lambda o, i, r, w: act(o, i, r, w, AF.Square, scale=2.0, bias=-4095.5), e, "Z2", "Z3")
+        stage(lambda o, i, r, w: band(o, i, 8190, r, w), e, "Z3", "Z4")
+
+    def place(e):
         w = 180 if e < NR else 128
         na = T.NA[:, 180 * e:180 * e + w]
         nk = ["NA%d%d" % (e, k) for k in range(3)]
+        lin(T.TH[:, 16 * (e - 1):16 * (e - 1) + 13], T.NE[:, 0:13], -1.0, T.NE[:, 1 + 3 * e:2 + 3 * e], ["NE0", "NE1", "NE2"],
+            ["TH%d" % e])
         if e < NR:
-            age = stage(lambda o, i, r, w: lin("S", o, i, T.NC[:, e:e + 1], T.MU[:, e:e + 1], r + ["NC", "MU"], w), e, "Z4", "Z5", cut)
+            stage(lambda o, i, r, x: lin(o, i, T.NC[:, e:e + 1], T.MU[:, e:e + 1], r + ["NC", "MU"], x), e, "Z4", "Z5")
         else:
-            age = stage(lambda o, i, r, w: lin("S", o, T.PLC[:], -1.0, T.MM[:, 5:6], ["PLC", "MUG"], w), e, "Z5", "Z5", cut, w)
+            stage(lambda o, i, r, x: lin(o, T.PLC[:], -1.0, T.MM[:, 5:6], ["PLC", "MUG"], x), e, "Z5", "Z5", w)
+        stage(lambda o, i, r, x: band(o, i, P - 1, r, x), e, "Z5", "Z6", w)
+        stage(lambda o, i, r, x: lin(o, i, -1.0, 0.0, r, x), e, "Z6", "NA", w)
+        bank = ("PH", "PM")[e % 2]
+        mm(T[bank][:, 0:w], T.IDH[:], na, "pl%d" % e, ["IDH"] + nk, bank)
+        for i in range(3 * e + 1):
+            t = 16 * (e - 1) + i
+            c = 180 * (3 * e * (e - 1) // 2 + e - 1 + i)
+            ts(T.TM[:, c:c + w], na, T.TH[:, t:t + 1], T.DL[:, i:i + 1], A.is_le, A.mult,
+               nk + ["TH%d" % e, "DL0", "DL1", "DL2"], ["TM%d" % t], 0.5)
+            mm(T[bank][:, 0:w], T.IDH[:], T.TM[:, c:c + w], "pl%d" % e, ["IDH", "TM%d" % t], bank)
+        lin(T.OFF[:, 180 * e:180 * e + w], T[bank][:, 0:w], 1.0, T.FE[:, e - 1:e], [bank, "FE"], ["OFF%d" % e])
 
-        def steps():
-            mm(T.PM[:, 0:w], T.IDH[:], na, True, False, ["IDH"] + nk, ["PM"])
-            for i in range(3 * e + 1):
-                o = T.TM[:, 180 * i:180 * i + w]
-                t = 16 * (e - 1) + i
-                ts(o, na, T.TH[:, t:t + 1], T.DL[:, i:i + 1], A.is_le, A.mult, nk + ["TH%d" % e, "DL0", "DL1", "DL2"], ["TM%d" % i])
-                mm(T.PM[:, 0:w], T.IDH[:], o, False, i == 3 * e, ["IDH", "TM%d" % i], ["PM"])
-
-        return [age,
-                stage(lambda o, i, r, w: band(o, i, P - 1, r, w), e, "Z5", "Z6", cut, w),
-                stage(lambda o, i, r, w: lin("S", o, i, -1.0, 0.0, r, w), e, "Z6", "NA", cut, w),
-                steps,
-                stage(lambda o, i, r, x: lin("S", o, T.PM[:, 0:w], 1.0, T.FB[:, e - 1:e], ["PM", "FB"], x), e, "NA", "OFF", WHOLE, w)]
-
-    def gather(q, e, j, k, part):
-        lo, hi = {"": (0, CW), "a": (0, CW // 2), "b": (CW // 2, CW)}[part]
-        c = 180 * e + 60 * k + CW * j
-        win = T.WIN[:, 0:P + 3 * CAP * e].indirect(T.OFF[:, c + lo:c + hi])
-        o = T.GG[:, CAP * (3 * j + k) + 16 * lo:CAP * (3 * j + k) + 16 * hi]
-        r = ["RINGa", "RINGb", "OFF%d%d" % (e, k)] + ["W%d" % i for i in range(e)]
-        w = ["G%d%d%s" % (j, k, h) for h in (part or "ab")]
-        if q == "V":
-            op("V", lambda: v.tensor_copy(o, win), r, w)
-        else:
-            act(o, win, r, w, func=AF.Copy)
-
-    def piece(j, part):
-        return ("PCS" if part == "b" else "PX%d" % j), CAP * j + (CAP // 2 if part == "b" else 0), CAP // (2 if part else 1)
-
-    def weigh(j, parts):
-        for i, k in enumerate(WEIGH[j]):
-            for part in parts or ("",):
-                bank, c, w = piece(j, part)
-                c += CAP * (2 * j + k)
-                mm(T[bank][:, 0:w], T.DG[:, 128 * k:128 * k + 128], T.GG[:, c:c + w], i == 0, i == 2,
-                   ["DG%d" % k] + ["G%d%d%s" % (j, k, h) for h in (part or "ab")], [bank])
-
-    def whole(q, j, part):
-        bank, c, w = piece(j, part)
-        lin(q, T.KI[:, c:c + w], T[bank][:, 0:w], 1.0, -127.5 / 256, [bank], ["KI%d%s" % (j, part)])
-
-    def rest(e, j, part):
-        bank, c, w = piece(j, part)
-        tt(T.OUT[:, 3 * CAP * e + c:3 * CAP * e + c + w], T[bank][:, 0:w], T.KI[:, c:c + w], A.subtract,
-           [bank, "KI%d%s" % (j, part)], ["O%d%d%s" % (e, j, part)])
-        if part != "a":
-            r, en = peers[j][0:2]
-            rid, pid = topo.addr(T.cores[r], core)
-            c = P + CAP * (3 * e + (rank - r) % n - 1)
-            deps("G", ["O%d%d%s" % (e, j, h) for h in ("", "a", "b")], [])
-            g.remote_dma(T.WIN[:, c:c + CAP], T.OUT[:, CAP * (3 * e + j):CAP * (3 * e + j + 1)], T.sem["ar%d" % e], T.sem.loc,
-                         pid, rid, _bits(en))
-            sent[0] += len(en)
-
-    def round_(e, fill=None):
+    def round_(e):
+        last = {}
         for st in ROUND:
-            if st[0] == "w":
-                weigh(int(st[1]), st[2:])
-            elif st[0] == "r":
-                rest(e, int(st[1]), st[2:])
+            j, h = int(st[2]), st[3:].strip("012")
+            bank = ("PU", "PD", "PCS")[j] if h == "b" else "PX%d" % j
+            c, w = CAP * j + (CAP // 2 if h == "b" else 0), CAP // (2 if h else 1)
+            px, ki, o = T[bank][:, 0:w], T.KI[:, c:c + w], T.OUT[:, 3 * CAP * e + c:3 * CAP * e + c + w]
+            if st[1] == "g":
+                k = int(st[3])
+                d = (c - CAP * j) // 16
+                a = 180 * e + 60 * k + CW * j + d
+                off = T.OFF[:, a:a + w // 16] if e else T.OL[:, j, CW * k + d:CW * k + d + w // 16]
+                lin(T.GG[:, c + CAP * (2 * j + k):c + CAP * (2 * j + k) + w], T.WIN[:, 0:P + 3 * CAP * e].indirect(off), 1.0, 0.0,
+                    RING + ["OFF%d" % e if e else "OL"] + ["W%d" % i for i in range(e)],
+                    ["G%d%d%s" % (j, k, x) for x in h or "ab"], GATHER, st[0].replace("E", "VS"))
             elif st[1] == "c":
-                whole(st[0], int(st[2]), st[3:])
+                for k in range(3):
+                    d = c + CAP * (2 * j + k)
+                    mm(px, T.DG[:, 128 * k:128 * k + 128], T.GG[:, d:d + w], "x%d%d%s" % (e, j, h),
+                       ["DG%d" % k] + ["G%d%d%s" % (j, k, x) for x in h or "ab"], bank)
+                lin(ki, px, 1.0, -127.5 / 256, [bank], ["KI%d%s" % (j, h)], qs=st[0].replace("E", "VS"))
+            elif st[1] == "r":
+                tt(o, px, ki, A.subtract, [bank, "KI%d%s" % (j, h)], ["O%d%d%s" % (e, j, h)])
             else:
-                gather(st[0], e, int(st[2]), int(st[3]), st[4:])
-            for f in (fill or {}).get(st, []):
-                f()
+                write(e, j, h, o, c, w, [h] if h else ["", "a", "b"])
+                continue
+            if st[0] in last and st[0] != "E":
+                calls[-1]["follows"] = last[st[0]]
+            last[st[0]] = len(calls) - 1
 
-    a, b = lists("A"), lists("B")
-    had = T.HC[:, 27:28]
+    def write(e, j, h, o, c, w, parts):
+        r = peers[j][0]
+        en = engines(peers, j, h)
+        rid, pid = topo.addr(T.cores[r], core)
+        d = P + CAP * (3 * e + (rank - r) % n - 1 - j) + c
+        sent[0] += len(en)
+        key = "O%d%d%s" % (e, j, h)
+        call(lambda q: g.remote_dma(T.WIN[:, d:d + w], o, T.sem["ar%d" % e], T.sem.loc, pid, rid, _bits(en)), {"G": ISSUE},
+             ["O%d%d%s" % (e, j, x) for x in parts], [key + "w"], "remote")
+        call(None, {"L": FAR * w / CAP} if j < 2 else {"N": NEAR}, [key + "w"], ["W%d" % e], "link", LAND - 2 * HOP,
+             "W%d" % e)
 
-    a["flags"]("V")
-    lin("V", T.HCF[0:8, :], T.HCI[0:8, :], 1.0, 0.0, ["HCI"], ["HCF"])
-    mm(T.PH[:, 0:28], T.E8[0:8, :], T.HCF[0:8, :], True, True, ["E8", "HCF"], ["PH"])
-    a["sums"]()
-    a["rank"]()
-    b["flags"]("S")
-    a["ends"](0, 2)
-    a["mask"]()
-    a["ramp"]()
-    a["halves"]("V", "S")
-    b["sums"]()
-    a["ends"](2, 6)
-    a["next"]()
-    a["hot"]()
-    act(T.HC[:], T.PH[:, 0:28], ["PH"], ["HC"])
-    b["rank"]()
-    b["ends"](0, 4)
-    a["cols"]("S")
-    b["mask"]()
-    b["ends"](4, 6)
-    a["drop"]()
-    b["halves"]("S", "V")
-    a["run"]()
+    lists("A")
+    hash_(0)
+    ts(T.CR[:], T.HR[:, :, 0:1], float(P), 1.0 / 8192, A.min, A.mult, ["HR"], ["CR"])
+    for j in range(3):
+        lin(T.OS[:, 60 * j:60 * j + 60], T.Z4[:, 60 * j:60 * j + 60], T.CR[:, j:j + 1], EPS - 0.5, ["Z40%d" % j, "CR"], ["OS%d" % j])
+    to_all("arA", "OL", ["OS0", "OS1", "OS2"], lambda q: T.OS[:, 60 * ((q - rank) % n - 1):60 * ((q - rank) % n)],
+           lambda q: T.OL[:, slot[q], :])
+    lists("B")
+    tt(T.XB[:], T.MXB[:].indirect(T.OFB[:]), T.KB[:], A.add, ["MXB0", "OFB", "KB"], ["XB"], GATHER)
+    to_all("arB", "LB", ["XB"], lambda q: T.XB[:, 96 * ((q - rank) % n - 1):96 * ((q - rank) % n - 1) + 84],
+           lambda q: T.LB[:, slot[q], 0:84])
+
     cn = T.CI[:, 32:396:33]
     scan(T.NE[:, 2:14], cn, cn, 0.0, A.min, A.subtract, ["CIA", "CIB"], ["NE2"])
-    b["ramp"]()
-    a["pick"]()
-    a["send"]()
-    iota(T.KB[:], [[-TT, 3], [-3 * TT, 3], [0, 32]], TT * rank + 2048, 0, ["KB"])
-    iota(T.PLC[:], [[16, 128]], 0, 1, ["PLC"])
-
-    h0, h1, h2, h3 = hash_(0, THIRDS), hash_(1, THIRDS), hash_(2), hash_(3)
-    p1, p2, p3, p4 = place(1, THIRDS), place(2), place(3), place(NR)
-
-    def bound(e):
-        return lambda: lin("S", T.TH[:, 16 * (e - 1):16 * (e - 1) + 13], T.NE[:, 0:13], -1.0, T.NE[:, 1 + 3 * e:2 + 3 * e],
-                           ["NE0", "NE1", "NE2"], ["TH%d" % e])
-
-    b["ends"](6, 18)
-    b["next"]()
-    lin("S", T.MM[:, 0:5], T.NE[:, 1:14:3], -1.0, had, ["NE1", "NE2", "HC"], ["MM"])
-    lin("S", T.WIN[:, 0:P // 2], T.WIN[:, 0:P // 2], 1.0 / 256, 0.0, ["RINGa"], ["RINGa"])
-    act(T.NC[:, 4:8], T.MM[:, 0:4], ["MM"], ["NR"], func=AF.Relu, scale=-1.0, bias=float(P))
-    lin("S", T.MUI[:, 0:4], T.MM[:, 0:4], 1.0, -1.0, ["MM"], ["MU0"])
-    b["hot"]()
-    b["cols"]("S")
-    lin("S", T.NC[:, 8:9], T.NC[:, 4:5], -1.0 / 8192, 0.25, ["NR"], ["C0"])
-    lin("S", T.NC[:, 0:4], T.NC[:, 4:8], 1.0 / 8192, -0.25, ["NR"], ["NC"])
-    lin("V", T.WIN[:, P // 2:P], T.WIN[:, P // 2:P], 1.0 / 256, 0.0, ["RINGb"], ["RINGb"])
+    lin(T.MM[:, 0:5], T.NE[:, 1:14:3], -1.0, T.HC[:, 0:1], ["NE1", "NE2", "HC"], ["MM"])
+    store(T.now[:], T.MM[0:128:16, 4:5], ["MM"])
+    act(T.NC[:, 4:8], T.MM[:, 0:4], ["MM"], ["NR"], AF.Relu, scale=-1.0, bias=float(P))
+    lin(T.NC[:, 0:4], T.NC[:, 4:8], 1.0 / 8192, -0.25, ["NR"], ["NC"])
+    lin(T.MUI[:, 0:4], T.MM[:, 0:4], 1.0, -1.0, ["MM"], ["MU0"])
     band(T.MUI[:, 4:8], T.MUI[:, 0:4], P - 1, ["MU0"], ["MU1"])
-    for k in range(3):
-        lin("S", T.DG[:, 128 * k:128 * k + 128], T.IDB[:], T.HC[:, 24 + k:25 + k], 0.0, ["IDB", "HC"], ["DG%d" % k])
-    counts = [lambda: lin("V", T.NE[:, 0:1], T.MUI[:, 4:5], 1.0, 1.0, ["MU1"], ["NE0"]),
-              lambda: lin("V", T.DL[:, 1:2], T.MUI[:, 4:5], 1.0, 1.0 - P, ["MU1"], ["DL1"]),
-              lambda: lin("V", T.MU[:], T.MUI[:, 4:8], 1.0, 0.5 - EPS, ["MU1"], ["MU"]),
-              lambda: lin("V", T.DL[:, 2:13], T.CI[:, 32:363:33], 1.0, -float(CAP), ["CIA", "CIB"], ["DL2"]),
-              lambda: tt(T.FB[:], T.CI[:, 98:396:99], T.FC[:], A.add, ["CIA", "CIB", "FC"], ["FB"])]
-    _mix([h0[0], b["drop"], counts[0], counts[1], b["run"], h0[1], h0[2], h0[3], b["pick"], b["send"], place(0, THIRDS)[0]])
-    deps("Y", ["MM"], [])
-    g.sync.dma_start(T.now[:], T.MM[0:128:16, 4:5]).then_inc(T.sem.st, 16)
+    lin(T.MU[:], T.MUI[:, 4:8], 1.0, 0.5 - EPS, ["MU1"], ["MU"])
+    lin(T.NE[:, 0:1], T.MUI[:, 4:5], 1.0, 1.0, ["MU1"], ["NE0"])
+    lin(T.DL[:, 1:2], T.MUI[:, 4:5], 1.0, 1.0 - P, ["MU1"], ["DL1"])
+    lin(T.DL[:, 2:13], T.CI[:, 32:363:33], 1.0, -float(CAP), ["CIA", "CIB"], ["DL2"])
+    lin(T.MM[:, 5:6], T.MM[:, 4:5], 1.0, g1, ["MM", "g1"], ["MUG"])
+    tt(T.FE[:], T.CI[:, 98:396:99], T.FC[:], A.add, ["CIA", "CIB", "FC"], ["FE"])
 
-    round_(0, {"Sc1": h1[0:1], "Vg21b": counts[2:3], "r1": h1[1:2], "Sc2b": h1[2:3], "r2b": h1[3:4]})
-    _mix([p1[0], counts[3], bound(1), p1[1], counts[4], p1[2], h2[0], p1[3], h2[1], bound(2), p1[4], h2[2]])
-    round_(1, {"Vg01": h2[3:4], "Sc1": [p2[0], bound(3)], "r1": p2[1:2], "Sc2b": [p2[2], h3[0]]})
-    _mix([p2[3], h3[1], p2[4], h3[2], h3[3]])
-    round_(2, {"Sc1": [p3[0], bound(4)], "r1": p3[1:2], "Sc2b": p3[2:3]})
-    _mix([p3[3], lambda: lin("S", T.MM[:, 5:6], T.MM[:, 4:5], 1.0, g1, ["MM", "g1"], ["MUG"]), p4[0], p3[4]])
-    round_(3, {"Vg21b": p4[1:2], "Sc2b": p4[2:3]})
+    for e in range(NR):
+        if e:
+            hash_(e)
+            place(e)
+        round_(e)
 
-    _mix(p4[3:5])
-    r = ["RINGa", "RINGb", "OFF40"] + ["W%d" % i for i in range(NR)]
-    pieces = (("V", 0, 256), ("S", 256, 512), ("V", 512, 896), ("S", 896, 1280), ("V", 1280, 1664), ("S", 1664, 2048))
-    for q, lo, hi in pieces:
-        lin(q, T.YY[:, lo:hi], T.WIN[:].indirect(T.OFF[:, 720 + lo // 16:720 + hi // 16]), 256.0, 0.0, r, ["Y%d" % lo])
-        dq = "S" if hi == P else "Y"
-        deps(dq, ["Y%d" % lo], [])
-        Q[dq].dma_start(T.y[:, lo:hi], T.YY[:, lo:hi]).then_inc(T.sem.st, 16)
+    place(NR)
+    pieces = ((0, 256), (256, 896), (896, 1600), (1600, P))
+    for lo, hi in pieces:
+        mid = (lo + hi) // 2
+        for q, c, d in (("V", lo, mid), ("S", mid, hi)):
+            lin(T.YY[:, c:d], T.WIN[:].indirect(T.OFF[:, 720 + c // 16:720 + d // 16]), 256.0, 0.0,
+                RING + ["OFF4"] + ["W%d" % i for i in range(NR)] + (["Y%s%d" % (q, lo)] if lo else []), ["Y%s%d" % (q, hi)], GATHER, q)
+        store(T.y[:, lo:hi], T.YY[:, lo:hi], ["YV%d" % hi, "YS%d" % hi])
+
+    Q = {"V": v, "S": s, "P": pe, "G": g, "Y": g.sync}
+    cnt = {"V": 0, "S": 0, "P": 0, "G": 0}
+    waited = {q: {} for q in Q}
+    rd = {}
+
+    def wait(q, sem, count):
+        if waited[q].get(sem, 0) < count:
+            Q[q].wait_ge(T.sem[sem], count)
+            waited[q][sem] = count
+
+    if not ORDER:
+        ORDER.extend(_order(calls))
+    for i, q in ORDER:
+        c = calls[i]
+        if c["kind"] == "link":
+            continue
+        toks = [wr[k] for k in c["r"] if k in wr and not (k[0] == "Y" and q != "Y")]
+        toks += [t for k in c["r"] if k in PSUM for t in rd.get(k, []) if t[0] != "s" + q]
+        if c["kind"] == "compute":
+            toks += [t for k in c["w"] for t in ([wr[k]] if k in wr else []) + rd.get(k, []) if not (q == "P" and t[0] == "sP")]
+        need = {}
+        for sem, count in toks:
+            need[sem] = max(need.get(sem, 0), count)
+        for sem in need:
+            wait(q, sem, need[sem])
+        ins = c["f"](q)
+        if c["kind"] == "compute":
+            cnt[q] += 1
+            ins.then_inc(T.sem["s" + q], 1)
+            for k in c["r"]:
+                rd.setdefault(k, []).append(("s" + q, cnt[q]))
+            for k in c["w"]:
+                wr[k] = ("s" + q, cnt[q])
+                rd[k] = []
 
     g.sync.wait_ge(T.sem.st, 16 * (1 + len(pieces)))
     g.wait_ge(T.sem.loc, sent[0])
     for q in cnt:
-        wait("G", ("s" + q, cnt[q]))
+        wait("G", "s" + q, cnt[q])

from concourse.bass import DstId, RemoteDMATransfer
from concourse.mybir import AluOpType as A, ActivationFunctionType as AF

NR, P, CAP, TT = 4, 2048, 320, 512
CW = CAP // 16
EPS = 2.0 ** -13
BIG = 1024.0
BATCH = {"A": (0, 3), "B": (3, 9)}
F4, B2, I4, H2, U2 = "float32", "bfloat16", "int32", "float16", "uint16"


def _sb(n, t):
    return ("sbuf", [128] + (n if isinstance(n, list) else [n]), t)


SCRATCH = {
    "WIN": _sb(P + 12 * CAP, B2), "OUT": _sb(12 * CAP, B2), "GG": _sb(9 * CAP, B2), "KI": _sb(3 * CAP, I4), "YY": _sb(P, F4),
    "CMA": _sb([3, 32], I4), "CMB": _sb([9, 32], I4), "HCI": _sb(28, I4), "HCF": _sb(28, F4), "HC": _sb(28, F4),
    "PCI": _sb(4, I4), "PCF": _sb(12, F4), "MG": _sb(128, B2), "MI": _sb(144, F4), "BON": _sb(128, B2), "UT": _sb(128, B2),
    "UU": _sb(128, B2), "WM": _sb(144, H2), "E8": _sb(128, F4), "IDB": _sb(128, B2), "IDH": _sb(128, H2), "DG": _sb(384, B2),
    "EH": _sb(128, H2), "EB": _sb(128, B2), "CJ": _sb(297, I4), "CK": _sb(297, I4),
    "CBM": _sb(297, B2), "CBR": _sb(396, B2), "K2": _sb(24, F4), "KB": _sb(288, F4), "PLC": _sb(128, F4),
    "JK": _sb(768, B2), "ACC": _sb(24, F4), "AC2": _sb(24, F4), "LB": _sb([3, 96], U2),
    "HR": _sb([3, 8], F4), "CR": _sb(3, F4), "Z0": _sb([9, 32], I4), "OS": _sb(180, U2), "OL": _sb([3, 60], U2), "XB": _sb(288, U2),
    "FZ": _sb([12, 33], B2), "CI": _sb(396, F4), "NE": _sb(14, F4), "DL": _sb(13, F4), "FC": _sb(4, F4), "FE": _sb(4, F4),
    "MM": _sb(6, F4), "NC": _sb(8, F4), "MUI": _sb(8, I4), "MU": _sb(4, F4), "TH": _sb(64, F4),
    "Z1": _sb(720, I4), "Z2": _sb(720, I4), "Z3": _sb(720, I4), "Z4": _sb(720, I4),
    "Z5": _sb(900, I4), "Z6": _sb(900, I4), "NA": _sb(900, H2), "TM": _sb(34 * 180, H2), "OFF": _sb(900, U2),
}
PSUM = ("PCS", "PU", "PD", "PX0", "PX1", "PX2", "PM", "PH")
for _n in PSUM:
    SCRATCH[_n] = ("psum", [128, 512], F4)
for _n in BATCH:
    _w = 33 * BATCH[_n][1]
    for _k, _t in (("RM", I4), ("RB", I4), ("HB", F4), ("VL", F4), ("MX", F4)):
        SCRATCH[_k + _n] = _sb(_w, _t)
    SCRATCH["RH" + _n] = _sb([2, _w + 1], H2)
    SCRATCH["OH" + _n] = _sb([16, _w + 1], H2)
    SCRATCH["OF" + _n] = _sb(2 * BATCH[_n][1], U2)

SEMAPHORES = ["sV", "sS", "sP", "sG", "ldA", "ldB", "ldH", "ldR", "st", "loc", "arH", "arA", "arB", "ar0", "ar1", "ar2", "ar3"]

ROUND = ("Vg00a Vg02a Vg02b Sg01 Sg10 Vg00b Sg11a Sc0a Vg12a Vg12b Sg11b Vr0a Gw0a Vg22a Sc0b Sc1a Sg21 Sg20a Vr0b Gw0b Vc1b "
         "Sg20b Sc2a Vr1a Gw1a Vr1b Gw1b Vg22b Sc2b Vr2a Gw2a Vr2b Gw2b").split()
WHOLE, TWO, THIRDS = ((0, 3),), ((0, 1), (1, 3)), ((0, 1), (1, 2), (2, 3))
CUTS = (THIRDS, TWO, WHOLE, WHOLE, WHOLE)

CYC, HOP, SLACK, SPARE, PASSES = 0.00083, 0.15, 0.1, 0.1, 4
FIX = {"V": 0.03, "S": 0.05, "P": 0.04, "G": 0.15, "Y": 0.05}
PE, GATHER = 0.65, 1.56
ISSUE, FIRST, LAND, FAR, NEAR, STORE = 0.2, 2.6, 1.0, 0.9, 0.2, 1.2
LISTS = {"HR": 1.6, "OL": 1.6, "LB": 1.6}
LOADED = {"CMA": 1.7, "HCI": 1.6, "CMB": 2.0, "RING0": 3.2, "RING1": 3.2, "RING2": 3.2, "RING3": 3.2, "later": 3.0}


ORDER = []


def _bits(engs):
    m = 0
    for e in engs:
        m |= 1 << e
    return m


def _peers(T, topo, q):
    me = T.cores[q]
    n = len(T.cores)
    others = [(q + d) % n for d in range(1, n)]
    far = [r for r in others if T.cores[r] not in topo.cores_of(me)]
    far.sort(key=lambda r: topo.die(T.cores[r]) == topo.die(me))
    near = [r for r in others if T.cores[r] in topo.cores_of(me)]
    res = []
    used = set()
    for i, r in enumerate(far):
        en = topo.engines(me, T.cores[r])
        used |= set(en)
        k = len(en) // len(far)
        res.append((r, en, en[i * k:(i + 1) * k]))
    for r in near:
        en = topo.engines(me, T.cores[r])
        res.append((r, en, [x for x in en if x not in used]))
    return res


def _order(calls):
    pre = [set() for c in calls]
    writers, readers = {}, {}
    for i, c in enumerate(calls):
        for k in c["r"]:
            pre[i].update(writers.get(k, []))
        for k in c["w"]:
            ws = writers.get(k, [])
            if c["sum"] is not None and ws and calls[ws[0]]["sum"] == c["sum"]:
                pre[i].update(calls[ws[0]]["after"])
                ws.append(i)
            else:
                c["after"] = set(ws) | set(readers.get(k, []))
                pre[i].update(c["after"])
                writers[k], readers[k] = [i], []
        for k in c["r"]:
            if k not in c["w"]:
                readers.setdefault(k, []).append(i)
        pre[i].discard(i)
        c["soft"] = c.get("follows") if c.get("follows") not in pre[i] else None
        if c["soft"] is not None:
            pre[i].add(c["soft"])
    post = [[] for c in calls]
    for i in range(len(calls)):
        for j in pre[i]:
            post[j].append(i)

    def run(pre, post, chain, back):
        free = {q: 0.0 for q in "VSPGYLN"}
        end, bank, res = {}, {}, []
        left = [len(p) for p in pre]
        ready = {}

        def arrive(i):
            c = calls[i]
            lag = c["late"] if back else 0.0
            ready[i] = max([lag] + [0.0 if back else LOADED.get(k, 0.0) for k in c["r"]]
                           + [end[j][0] + lag + (0.0 if end[j][1] == "P" and "P" in c["t"] or c["soft"] == j
                                                 or calls[j]["soft"] == i else HOP) for j in pre[i]])

        for i in range(len(calls)):
            if not left[i]:
                arrive(i)
        while ready:
            best = []
            for i in ready:
                c = calls[i]
                opts = []
                for q in c["t"]:
                    t = max([free[q], ready[i]] + [bank[k][0] + HOP for k in c["bank"] if k in bank and bank[k][1] != q])
                    opts.append((t + c["t"][q] + (SPARE if q == "V" else 0.0), t, q))
                best.append(min(opts)[1:] + (i,))
            soon, q, _ = min(best)
            t, q, i = max((b for b in best if b[0] <= soon + SLACK and b[1] == q), key=lambda b: (chain[b[2]], -b[2]))
            c = calls[i]
            free[q] = t + c["t"][q]
            end[i] = (free[q] + (0.0 if back else c["late"]), q)
            for k in c["bank"]:
                bank[k] = (free[q], q)
            res.append((i, q))
            del ready[i]
            for j in post[i]:
                left[j] -= 1
                if not left[j]:
                    arrive(j)
        return res, [end[i][0] for i in range(len(calls))]

    chain = [0.0] * len(calls)
    for i in reversed(range(len(calls))):
        chain[i] = min(calls[i]["t"].values()) + calls[i]["late"] + max([HOP + chain[j] for j in post[i]] + [0.0])
    best = None
    for _ in range(PASSES):
        res, end = run(pre, post, chain, False)
        if best is None or max(end) < best[0]:
            best = (max(end), res)
        chain = run(post, pre, end, True)[1]
    return best[1]


def rank_program(g, core, T, topo):
    rank = T.rank_of(core)
    if rank is None:
        return
    n = len(T.cores)
    v, s, pe = g.vector, g.scalar, g.tensor
    calls = []

    def size(ap):
        m = 1
        for d in ap.shape[1:]:
            m *= d
        return m

    def call(f, t, r, w, kind="compute", late=0.0, group=None):
        calls.append({"f": f, "t": t, "r": list(r), "w": list(w), "kind": kind, "late": late, "sum": group,
                      "bank": [k for k in r if k in PSUM]})

    def cost(q, out, rate):
        return FIX[q] + CYC * (size(out) * rate if rate == GATHER else max(64, size(out) * rate))

    def ts(out, i, a, b, o0, o1, r, w, rate=1.0):
        args = (out, i, a, None, o0) if o1 is None else (out, i, a, b, o0, o1)
        call(lambda q: v.tensor_scalar(*args), {"V": cost("V", out, rate)}, r, w)

    def tt(out, a, b, o, r, w, rate=1.0):
        call(lambda q: v.tensor_tensor(out, a, b, o), {"V": cost("V", out, rate)}, r, w)

    def act(out, i, r, w, func, **kw):
        call(lambda q: s.activation(out, i, func, **kw), {"S": cost("S", out, 1.0)}, r, w)

    def lin(out, i, a, b, r, w, rate=1.0, qs="VS"):
        def f(q):
            if q == "V":
                return v.tensor_scalar(out, i, a, b, A.mult, A.add)
            return s.activation(out, i, AF.Identity, scale=a, bias=b)
        call(f, {q: cost(q, out, rate if q == "V" else max(rate, 1.0)) for q in qs}, r, w)

    def band(out, i, m, r, w):
        ts(out, i, m, None, A.bitwise_and, None, r, w)

    def scan(out, a, b, first, o0, o1, r, w):
        call(lambda q: v.tensor_tensor_scan(out, a, b, first, o0, o1), {"V": cost("V", out, 1.0)}, r, w)

    def fill(out, x, w, rate=1.0):
        call(lambda q: v.memset(out, x), {"V": cost("V", out, rate)}, [], w)

    sums = {}

    def mm(out, l, rh, name, r, bank, rate=PE):
        c = sums.setdefault(name, [0, 0])
        c[0] += 1

        def f(q):
            c[1] += 1
            return pe.matmul(out, l, rh, c[1] == 1, c[1] == c[0])
        call(f, {"P": FIX["P"] + CYC * rate * max(64, size(out))}, r, [bank], group=name)

    def iota(out, pat, base, cm, w, r=()):
        call(lambda q: g.iota(out, pat, base, cm, allow_small_or_imprecise_dtypes=True), {"G": cost("G", out, 2.0)}, r, w)

    peers = _peers(T, topo, rank)
    got = [0, 0]
    slot = {}

    def engines(prs, j, part):
        return prs[j][2 if j == len(prs) - 1 and part == "a" else 1]

    for q in range(n):
        if q != rank:
            prs = _peers(T, topo, q)
            for j, pr in enumerate(prs):
                if pr[0] == rank:
                    got = [got[0] + sum(len(engines(prs, j, h)) for h in [st[3:] for st in ROUND if st[0:3] == "Gw%d" % j]), got[1] + len(pr[2])]
                    slot[q] = j
    wr = {"HR": ("arH", got[1]), "OL": ("arA", got[1]), "LB": ("arB", got[1])}
    for e in range(NR):
        wr["W%d" % e] = ("ar%d" % e, got[0])
    sent = [0]

    def to_all(sem, key, r, src, dst, t=ISSUE):
        trs = []
        for q, _, el in peers:
            rid, pid = topo.addr(T.cores[q], core)
            trs.append(RemoteDMATransfer(dst_ids=[DstId(rid=rid, pnc=pid)], dma_engine_mask=_bits(el), remote_sem=T.sem[sem],
                                         src=src(q), dst=dst(q)))
            sent[0] += len(el)
        call(lambda q: g.remote_dma_fused(trs, local_sem=T.sem.loc), {"G": t}, r, [key], "remote", LISTS[key] - HOP)

    def store(out, i, r):
        call(lambda q: g.sync.dma_start(out, i).then_inc(T.sem.st, 16), {"Y": FIX["Y"]}, r, [], "store", STORE)

    g.sync.dma_start(T.CMA[:], T.came[:, 0:96]).then_inc(T.sem.ldA, 16)
    s.dma_start(T.HCI[0:8, 1:28], T.hc[:]).then_inc(T.sem.ldH, 16)
    s.dma_start(T.HCI[0:8, 0:1], T.had[:]).then_inc(T.sem.ldH, 16)
    g.sync.dma_start(T.CMB[:], T.came[:, 96:384]).then_inc(T.sem.ldB, 16)
    g.sync.dma_start(T.WIN[:, 0:P], T.ring[:]).then_inc(T.sem.ldR, 16)
    wr["CMA"], wr["CMB"], wr["HCI"] = ("ldA", 16), ("ldB", 16), ("ldH", 32)
    RING = ["RING%d" % i for i in range(4)]
    for key in RING:
        wr[key] = ("ldR", 16)

    iota(T.PCI[:, 0:1], [[0, 1]], 0, 1, ["p"])
    iota(T.MG[:], [[16, 8], [0, 16]], 0, 0, ["MG"])
    iota(T.MI[:], [[1, 144]], 0, 0, ["MI"])
    fill(T.FZ[:, :, 32:33], 0.0, ["FA", "FB"])
    fill(T.PD[:, 0:1], -BIG, ["PD"])
    fill(T.PM[:, 0:1], -BIG, ["PM"])
    fill(T.CBM[:], float(TT), ["CBM"], 0.5)
    fill(T.CBM[:, 0:297:33], 0.0, ["CBM"])
    fill(T.NE[:, 1:2], 0.0, ["NE1"])
    fill(T.DL[:, 0:1], float(P), ["DL0"])
    pf, gf, bf, g15, bB, th0, th1, p15, hb, g1 = [T.PCF[:, i:i + 1] for i in range(10)]
    band(T.PCI[:, 1:2], T.PCI[:, 0:1], 112, ["p"], ["gi"])
    band(T.PCI[:, 2:3], T.PCI[:, 0:1], 15, ["p"], ["bi"])
    lin(T.PCF[:, 0:3], T.PCI[:, 0:3], 1.0, 0.0, ["p", "gi", "bi"], ["pf"])
    ts(T.BON[:], T.MG[:], gf, None, A.is_equal, None, ["MG", "pf"], ["BON"], 0.5)
    call(lambda q: g.affine_select(T.UT[:], T.BON[:], [[-1, 128]], A.is_gt, 0.0, 0, 1), {"G": cost("G", T.UT, 2.0)}, ["BON"], ["UT"])
    call(lambda q: g.affine_select(T.UU[:], T.UT[:], [[-1, 128]], A.not_equal, -512.0, 0, 1), {"G": cost("G", T.UU, 2.0)},
         ["UT"], ["UU"])
    iota(T.CBR[:, 0:99], [[0, 3], [1, 33]], (TT * rank + 2048 - int(BIG)) // 16, 0, ["CBRA"])
    iota(T.K2[:, 0:6], [[66, 3], [0, 2]], 32, 0, ["K2A"])
    iota(T.CBR[:, 99:396], [[32, 9], [1, 33]], -64, 0, ["CBRB"], ["later"])
    iota(T.K2[:, 6:24], [[66, 3], [198, 3], [0, 2]], 32, 0, ["K2B"], ["later"])
    iota(T.KB[:], [[-TT, 3], [-3 * TT, 3], [0, 32]], TT * rank + 2048, 0, ["KB"], ["later"])
    iota(T.FC[:], [[3 * CAP, 4]], P - 1 + 2 * CAP, 0, ["FC"], ["later"])
    iota(T.PLC[:], [[16, 128]], 0, 1, ["PLC"], ["later"])
    for out, i, a, b, key in ((g15, gf, 1.0, 15.0, "g15"), (bB, bf, 1.0, BIG, "bB"), (p15, pf, 1.0, -15.0, "p15"),
                              (th0, bf, 16.0, 15.5, "th0"), (th1, bf, 16.0, 271.5, "th1"), (hb, bf, -BIG, 0.0, "hb"),
                              (g1, gf, 1.0, -1.0, "g1")):
        lin(out, i, a, b, ["pf"], [key], qs="S")
    ts(T.E8[0:8, :], T.MG[0:8, :], 1.0 / 16, T.PCF[0:8, 0:1], A.mult, A.is_equal, ["MG", "pf"], ["E8"])
    ts(T.WM[:], T.MI[:], g15, bB, A.is_equal, A.mult, ["MI", "g15", "bB"], ["WM"])
    ts(T.IDB[:], T.MI[:, 0:128], pf, None, A.is_equal, None, ["MI", "pf"], ["IDB"])
    ts(T.EH[:], T.MG[:], p15, None, A.is_equal, None, ["MG", "p15"], ["EH"], 0.5)
    ts(T.EB[:], T.MG[:], p15, -512.0, A.is_equal, A.mult, ["MG", "p15"], ["EB"], 0.5)
    lin(T.IDH[:], T.IDB[:], 1.0, 0.0, ["IDB"], ["IDH"], 0.5)

    lin(T.HCF[0:8, :], T.HCI[0:8, :], 1.0, 0.0, ["HCI"], ["HCF"])
    mm(T.PH[:, 0:28], T.E8[0:8, :], T.HCF[0:8, :], "hc", ["E8", "HCF"], "PH", 4 * PE)
    lin(T.HC[:], T.PH[:, 0:28], 1.0, 0.0, ["PH"], ["HC"])
    to_all("arH", "HR", ["HC"], lambda q: T.HC[:, 0:8], lambda q: T.HR[:, (rank - q) % n - 1, :], ISSUE + FIRST)
    for k in range(3):
        lin(T.DG[:, 128 * k:128 * k + 128], T.IDB[:], T.HC[:, 25 + k:26 + k], 0.0, ["IDB", "HC"], ["DG%d" % k], 0.5)
    for i in range(4):
        c = T.WIN[:, i * P // 4:(i + 1) * P // 4]
        lin(c, c, 1.0 / 256, 0.0, RING[i:i + 1], RING[i:i + 1], 0.5)

    def lists(b):
        s0, ns = BATCH[b]
        w = 33 * ns
        F = T.FZ[:, s0:s0 + ns, :]
        CI = T.CI[:, 33 * s0:33 * s0 + w]
        RM, RB, RH, OH, HB, VL, MX = [T[x + b] for x in ("RM", "RB", "RH", "OH", "HB", "VL", "MX")]
        a0, ne = 2 * s0, ns // 3
        cs, cu, cd = ("PCS", "PU", "PD") if b == "A" else ("PX0", "PX2", "PM")
        pd, pc = T[cd][:, 1:1 + w], T.PX1[:, 0:w]
        lin(T.FZ[:, s0:s0 + ns, 0:32], T["CM" + b][:], 1.0, 0.0, ["CM" + b], ["F" + b])
        mm(T[cs][:, 0:w], T.BON[:], F, "cs" + b, ["BON", "F" + b], cs)
        mm(T[cu][:, 0:w], T.UU[:], F, "cu" + b, ["UU", "F" + b], cu)
        scan(CI, T.CBM[:, 0:w], T[cs][:, 0:w], 0.0, A.min, A.add, ["CBM", cs], ["CI" + b])
        tt(RM[:], CI, T[cu][:, 0:w], A.subtract, ["CI" + b, cu], ["RM" + b])
        band(RB[:], RM[:], 527, ["RM" + b], ["RB" + b])
        lin(RH[:, 0, 0:w], RB[:], 1.0, 0.0, ["RB" + b], ["RH0" + b])
        lin(RH[:, 1, 0:w], RB[:], 1.0, -8.0, ["RB" + b], ["RH1" + b])
        if b == "A":
            mm(pc, T.EH[:], RH[:, 0, 0:w], "pc", ["EH", "RH0" + b], "PX1")
            mm(pc, T.EB[:], F, "pc", ["EB", "F" + b], "PX1")
            act(HB[:], pc, ["PX1", "hb"], ["HB" + b], AF.Relu, scale=BIG, bias=hb)
        else:
            lin(T.CJ[:], CI, 1.0, 0.0, ["CI" + b], ["CJ"])
            band(T.CK[:], T.CJ[:], 15, ["CJ"], ["CK"])
            act(HB[:], T.CK[:], ["CK", "hb"], ["HB" + b], AF.Relu, scale=BIG, bias=hb)
        for i in range(2 * ns):
            h = i % 2
            sl = s0 + 3 * ((i // 2) % ne) + i // (2 * ne)
            act(T.JK[:, 32 * (a0 + i):32 * (a0 + i + 1)], T.CI[:, 33 * sl:33 * sl + 32], ["CI" + b, "th%d" % h],
                ["ACC%d" % (a0 + i)], AF.Sign, scale=-1.0, bias=(th0, th1)[h], accum_out=T.ACC[:, a0 + i:a0 + i + 1])
        tt(T.AC2[:, a0:a0 + 2 * ns], T.ACC[:, a0:a0 + 2 * ns], T.K2[:, a0:a0 + 2 * ns], A.add,
           ["ACC%d" % (a0 + i) for i in range(2 * ns)] + ["K2" + b], ["AC2" + b])
        lin(T["OF" + b][:], T.AC2[:, a0:a0 + 2 * ns], 0.5, 0.0, ["AC2" + b], ["OF" + b])
        mm(pd, T.BON[:], T.CBR[:, 33 * s0:33 * s0 + w], "pd" + b, ["BON", "CBR" + b], cd)
        for j in range(8):
            ts(OH[:, j:16:8, 0:w], RH[:, :, 0:w], float(512 + j), None, A.is_equal, None, ["RH0" + b, "RH1" + b],
               ["OH%s%d" % (b, j)], 0.5)
            for m in (j, j + 8):
                k = (m - 1) % 16
                mm(pd, T.WM[:, 15 - k:143 - k], OH[:, m, 0:w], "pd" + b, ["WM", "OH%s%d" % (b, j)], cd)
        tt(VL[:], pd, HB[:], A.subtract, [cd, "HB" + b], ["VL" + b])
        for lo, hi in (THIRDS if b == "A" else ((0, ns),)):
            scan(MX[:, 33 * lo:33 * hi], T[cd][:, 33 * lo:33 * hi], VL[:, 33 * lo:33 * hi], -BIG, A.max, A.max,
                 [cd, "VL" + b], ["MX%s%d" % (b, lo)])

    def stage(f, e, src, dst, w=180):
        for lo, hi in CUTS[e]:
            a, b = 180 * e + 60 * lo, 180 * e + min(w, 60 * hi)
            f(T[dst][:, a:b], T[src][:, a:b], ["%s%d%d" % (src, e, k) for k in range(lo, hi)],
              ["%s%d%d" % (dst, e, k) for k in range(lo, hi)])

    def hash_(e):
        if e == 0:
            for j in range(3):
                for k in range(3):
                    lin(T.Z0[:, 3 * j + k, :], T.MXA[:].indirect(T.OFA[:, 2 * j:2 * j + 2]), T.HR[:, j, 1 + k:2 + k],
                        T.HR[:, j, 4 + k:5 + k], ["MXA0", "MXA1", "MXA2", "OFA", "HR"], ["Z0%d%d" % (j, k)], GATHER)
                band(T.Z2[:, 60 * j:60 * j + 60], T.Z0[:, 3 * j:3 * j + 3, 0:CW], 4095, ["Z0%d%d" % (j, k) for k in range(3)],
                     ["Z20%d" % j])
        else:
            for k in range(3):
                lin(T.Z1[:, 180 * e + 60 * k:180 * e + 60 * k + 60], T.LB[:, :, 32 * (e - 1):32 * (e - 1) + CW],
                    T.HC[:, 6 * e + 1 + k:6 * e + 2 + k], T.HC[:, 6 * e + 4 + k:6 * e + 5 + k], ["LB", "HC"], ["Z1%d%d" % (e, k)])
            stage(lambda o, i, r, w: band(o, i, 4095, r, w), e, "Z1", "Z2")
        stage(lambda o, i, r, w: act(o, i, r, w, AF.Square, scale=2.0, bias=-4095.5), e, "Z2", "Z3")
        stage(lambda o, i, r, w: band(o, i, 8190, r, w), e, "Z3", "Z4")

    def place(e):
        w = 180 if e < NR else 128
        na = T.NA[:, 180 * e:180 * e + w]
        nk = ["NA%d%d" % (e, k) for k in range(3)]
        lin(T.TH[:, 16 * (e - 1):16 * (e - 1) + 13], T.NE[:, 0:13], -1.0, T.NE[:, 1 + 3 * e:2 + 3 * e], ["NE0", "NE1", "NE2"],
            ["TH%d" % e])
        if e < NR:
            stage(lambda o, i, r, x: lin(o, i, T.NC[:, e:e + 1], T.MU[:, e:e + 1], r + ["NC", "MU"], x), e, "Z4", "Z5")
        else:
            stage(lambda o, i, r, x: lin(o, T.PLC[:], -1.0, T.MM[:, 5:6], ["PLC", "MUG"], x), e, "Z5", "Z5", w)
        stage(lambda o, i, r, x: band(o, i, P - 1, r, x), e, "Z5", "Z6", w)
        stage(lambda o, i, r, x: lin(o, i, -1.0, 0.0, r, x), e, "Z6", "NA", w)
        bank = ("PH", "PM")[e % 2]
        mm(T[bank][:, 0:w], T.IDH[:], na, "pl%d" % e, ["IDH"] + nk, bank)
        for i in range(3 * e + 1):
            t = 16 * (e - 1) + i
            c = 180 * (3 * e * (e - 1) // 2 + e - 1 + i)
            ts(T.TM[:, c:c + w], na, T.TH[:, t:t + 1], T.DL[:, i:i + 1], A.is_le, A.mult,
               nk + ["TH%d" % e, "DL0", "DL1", "DL2"], ["TM%d" % t], 0.5)
            mm(T[bank][:, 0:w], T.IDH[:], T.TM[:, c:c + w], "pl%d" % e, ["IDH", "TM%d" % t], bank)
        lin(T.OFF[:, 180 * e:180 * e + w], T[bank][:, 0:w], 1.0, T.FE[:, e - 1:e], [bank, "FE"], ["OFF%d" % e])

    def round_(e):
        last = {}
        for st in ROUND:
            j, h = int(st[2]), st[3:].strip("012")
            bank = ("PU", "PD", "PCS")[j] if h == "b" else "PX%d" % j
            c, w = CAP * j + (CAP // 2 if h == "b" else 0), CAP // (2 if h else 1)
            px, ki, o = T[bank][:, 0:w], T.KI[:, c:c + w], T.OUT[:, 3 * CAP * e + c:3 * CAP * e + c + w]
            if st[1] == "g":
                k = int(st[3])
                d = (c - CAP * j) // 16
                a = 180 * e + 60 * k + CW * j + d
                off = T.OFF[:, a:a + w // 16] if e else T.OL[:, j, CW * k + d:CW * k + d + w // 16]
                lin(T.GG[:, c + CAP * (2 * j + k):c + CAP * (2 * j + k) + w], T.WIN[:, 0:P + 3 * CAP * e].indirect(off), 1.0, 0.0,
                    RING + ["OFF%d" % e if e else "OL"] + ["W%d" % i for i in range(e)],
                    ["G%d%d%s" % (j, k, x) for x in h or "ab"], GATHER, st[0].replace("E", "VS"))
            elif st[1] == "c":
                for k in range(3):
                    d = c + CAP * (2 * j + k)
                    mm(px, T.DG[:, 128 * k:128 * k + 128], T.GG[:, d:d + w], "x%d%d%s" % (e, j, h),
                       ["DG%d" % k] + ["G%d%d%s" % (j, k, x) for x in h or "ab"], bank)
                lin(ki, px, 1.0, -127.5 / 256, [bank], ["KI%d%s" % (j, h)], qs=st[0].replace("E", "VS"))
            elif st[1] == "r":
                tt(o, px, ki, A.subtract, [bank, "KI%d%s" % (j, h)], ["O%d%d%s" % (e, j, h)])
            else:
                write(e, j, h, o, c, w, [h] if h else ["", "a", "b"])
                continue
            if st[0] in last and st[0] != "E":
                calls[-1]["follows"] = last[st[0]]
            last[st[0]] = len(calls) - 1

    def write(e, j, h, o, c, w, parts):
        r = peers[j][0]
        en = engines(peers, j, h)
        rid, pid = topo.addr(T.cores[r], core)
        d = P + CAP * (3 * e + (rank - r) % n - 1 - j) + c
        sent[0] += len(en)
        key = "O%d%d%s" % (e, j, h)
        call(lambda q: g.remote_dma(T.WIN[:, d:d + w], o, T.sem["ar%d" % e], T.sem.loc, pid, rid, _bits(en)), {"G": ISSUE},
             ["O%d%d%s" % (e, j, x) for x in parts], [key + "w"], "remote")
        call(None, {"L": FAR * w / CAP} if j < 2 else {"N": NEAR}, [key + "w"], ["W%d" % e], "link", LAND - 2 * HOP,
             "W%d" % e)

    lists("A")
    hash_(0)
    ts(T.CR[:], T.HR[:, :, 0:1], float(P), 1.0 / 8192, A.min, A.mult, ["HR"], ["CR"])
    for j in range(3):
        lin(T.OS[:, 60 * j:60 * j + 60], T.Z4[:, 60 * j:60 * j + 60], T.CR[:, j:j + 1], EPS - 0.5, ["Z40%d" % j, "CR"], ["OS%d" % j])
    to_all("arA", "OL", ["OS0", "OS1", "OS2"], lambda q: T.OS[:, 60 * ((q - rank) % n - 1):60 * ((q - rank) % n)],
           lambda q: T.OL[:, slot[q], :])
    lists("B")
    tt(T.XB[:], T.MXB[:].indirect(T.OFB[:]), T.KB[:], A.add, ["MXB0", "OFB", "KB"], ["XB"], GATHER)
    to_all("arB", "LB", ["XB"], lambda q: T.XB[:, 96 * ((q - rank) % n - 1):96 * ((q - rank) % n - 1) + 84],
           lambda q: T.LB[:, slot[q], 0:84])

    cn = T.CI[:, 32:396:33]
    scan(T.NE[:, 2:14], cn, cn, 0.0, A.min, A.subtract, ["CIA", "CIB"], ["NE2"])
    lin(T.MM[:, 0:5], T.NE[:, 1:14:3], -1.0, T.HC[:, 0:1], ["NE1", "NE2", "HC"], ["MM"])
    store(T.now[:], T.MM[0:128:16, 4:5], ["MM"])
    act(T.NC[:, 4:8], T.MM[:, 0:4], ["MM"], ["NR"], AF.Relu, scale=-1.0, bias=float(P))
    lin(T.NC[:, 0:4], T.NC[:, 4:8], 1.0 / 8192, -0.25, ["NR"], ["NC"])
    lin(T.MUI[:, 0:4], T.MM[:, 0:4], 1.0, -1.0, ["MM"], ["MU0"])
    band(T.MUI[:, 4:8], T.MUI[:, 0:4], P - 1, ["MU0"], ["MU1"])
    lin(T.MU[:], T.MUI[:, 4:8], 1.0, 0.5 - EPS, ["MU1"], ["MU"])
    lin(T.NE[:, 0:1], T.MUI[:, 4:5], 1.0, 1.0, ["MU1"], ["NE0"])
    lin(T.DL[:, 1:2], T.MUI[:, 4:5], 1.0, 1.0 - P, ["MU1"], ["DL1"])
    lin(T.DL[:, 2:13], T.CI[:, 32:363:33], 1.0, -float(CAP), ["CIA", "CIB"], ["DL2"])
    lin(T.MM[:, 5:6], T.MM[:, 4:5], 1.0, g1, ["MM", "g1"], ["MUG"])
    tt(T.FE[:], T.CI[:, 98:396:99], T.FC[:], A.add, ["CIA", "CIB", "FC"], ["FE"])

    for e in range(NR):
        if e:
            hash_(e)
            place(e)
        round_(e)

    place(NR)
    pieces = ((0, 256), (256, 896), (896, 1600), (1600, P))
    for lo, hi in pieces:
        mid = (lo + hi) // 2
        for q, c, d in (("V", lo, mid), ("S", mid, hi)):
            lin(T.YY[:, c:d], T.WIN[:].indirect(T.OFF[:, 720 + c // 16:720 + d // 16]), 256.0, 0.0,
                RING + ["OFF4"] + ["W%d" % i for i in range(NR)] + (["Y%s%d" % (q, lo)] if lo else []), ["Y%s%d" % (q, hi)], GATHER, q)
        store(T.y[:, lo:hi], T.YY[:, lo:hi], ["YV%d" % hi, "YS%d" % hi])

    Q = {"V": v, "S": s, "P": pe, "G": g, "Y": g.sync}
    cnt = {"V": 0, "S": 0, "P": 0, "G": 0}
    waited = {q: {} for q in Q}
    rd = {}

    def wait(q, sem, count):
        if waited[q].get(sem, 0) < count:
            Q[q].wait_ge(T.sem[sem], count)
            waited[q][sem] = count

    if not ORDER:
        ORDER.extend(_order(calls))
    for i, q in ORDER:
        c = calls[i]
        if c["kind"] == "link":
            continue
        toks = [wr[k] for k in c["r"] if k in wr and not (k[0] == "Y" and q != "Y")]
        toks += [t for k in c["r"] if k in PSUM for t in rd.get(k, []) if t[0] != "s" + q]
        if c["kind"] == "compute":
            toks += [t for k in c["w"] for t in ([wr[k]] if k in wr else []) + rd.get(k, []) if not (q == "P" and t[0] == "sP")]
        need = {}
        for sem, count in toks:
            need[sem] = max(need.get(sem, 0), count)
        for sem in need:
            wait(q, sem, need[sem])
        ins = c["f"](q)
        if c["kind"] == "compute":
            cnt[q] += 1
            ins.then_inc(T.sem["s" + q], 1)
            for k in c["r"]:
                rd.setdefault(k, []).append(("s" + q, cnt[q]))
            for k in c["w"]:
                wr[k] = ("s" + q, cnt[q])
                rd[k] = []

    g.sync.wait_ge(T.sem.st, 16 * (1 + len(pieces)))
    g.wait_ge(T.sem.loc, sent[0])
    for q in cnt:
        wait("G", "s" + q, cnt[q])
